import numpy as np, ml_dtypes
CORES = [66,74,82,90,194,202,210,218]
N = 8
import mx_ref
BF = ml_dtypes.bfloat16
def gentries(a):
    return np.ascontiguousarray(a.reshape(8, 16, -1).transpose(0, 2, 1)).reshape(8, -1)
def gtable(e):
    e = np.asarray(e); return np.ascontiguousarray(e.reshape(8, -1, 16).transpose(0, 2, 1)).reshape(128, -1).astype(np.int32)
def gcols(t, e):
    v = np.concatenate([t.reshape(8, 16, -1, 4), np.zeros((8, 16, 1, 4), BF)], axis=2)
    return np.ascontiguousarray(np.stack([v[g][:, e[g]] for g in range(8)])).reshape(128, -1)
def tile(rs):
    return np.stack(rs, axis=2).reshape(128, -1).astype(BF)
def pick(q, e):
    c = np.concatenate([q[0].reshape(128, -1, 4), np.zeros((128, 1, 4), np.uint8)], axis=1); s = np.concatenate([q[1], np.ones((16, 1), np.uint8)], axis=1)
    return (np.ascontiguousarray(c[:, e].reshape(128, -1)), np.ascontiguousarray(s[:, e]))
def join(*qs):
    return (np.concatenate([q[0] for q in qs], axis=1), np.concatenate([q[1] for q in qs], axis=1))
def put(q, e, v):
    c, s = q[0].reshape(128, -1, 4).copy(), q[1].copy(); c[:, e] = v[0].reshape(128, -1, 4); s[:, e] = v[1]
    return (c.reshape(128, -1), s)
def pk(c, s):
    return (np.ascontiguousarray(c), mx_ref.live(s))
def emit(q):
    return q[0], q[1]
def packed(v, rng):
    q = [mx_ref.quantize(np.ascontiguousarray(v[r])) for r in range(N)]
    return np.stack([a for a, b in q]), np.stack([mx_ref.plane(b, rng) for a, b in q])
def values_of_codes():
    e, c = np.zeros((128, 128, 4), np.float32), np.zeros((128, 2, 4), np.uint8)
    e[np.arange(128), np.arange(128), 0] = 1
    c[:127, :, 0] = np.arange(256).reshape(2, 128).T[:127]
    return mx_ref.matmul(mx_ref.quantize(e.reshape(128, 512).astype(BF)), (c.reshape(128, 8), np.full((16, 2), 127, np.uint8))).T.reshape(-1).astype(np.float64)
CODE_VALUE, SCALE_VALUE = values_of_codes(), 2.0 ** (np.arange(256) - 127.0)
def decode(q):
    return (CODE_VALUE[q[0]].reshape(16, 8, -1, 4) * SCALE_VALUE[q[1]][:, None, :, None] + 0.0).reshape(128, -1).astype(np.float32)
def f(rng, *shape):
    return mx_ref.flush((rng.standard_normal(shape, dtype=np.float32) * np.exp2(rng.integers(-2, 3, shape[:-1] + (1,)))).astype(BF))
def wide(rng, *shape, cols=0):
    v = rng.standard_normal(shape, dtype=np.float32) * np.exp2(rng.integers(-12, 13, shape)).astype(np.float32)
    if cols: v *= np.repeat(np.exp2(rng.integers(-cols, cols + 1, shape[:-2] + (1, shape[-1] // 4))) * (rng.random(shape[:-2] + (1, shape[-1] // 4)) > 0.0625), 4, axis=-1).astype(np.float32)
    return mx_ref.flush(v.astype(BF))
C, F = 320, 240
MASK = [4, 1, 2]
def numbers_of(rng):
    return {"x": np.array(f(rng, N, 128, 4 * C)), "u": np.array(f(rng, N, 128, 512)), "v": np.array(f(rng, N, 128, 512))}
def stored(k, n):
    return {"dl": np.stack([gtable(k[r]) for r in range(N)]), "nl": np.stack([gtable(n[r]) for r in range(N)])}
def lists(rng):
    e = np.tile(np.arange(C), (N, 8, 1))
    k, e = rng.permuted(e, axis=2), rng.permuted(e, axis=2)
    n = np.empty_like(e)
    np.put_along_axis(n, e, e.reshape(N, 8, -1, 2)[..., ::-1].reshape(N, 8, C), axis=2)
    return k, n
def layers(rng, still=[]):
    w = np.array(f(rng, N, 128, 2048)).reshape(N, 8, 16, 4, 8, 16, 4)
    for i in still:
        w[:, :, i] = 0
        w[:, :, :, :, :, i] = 0
    return w
def weights(rng, w):
    c, s = packed(np.ascontiguousarray(w).reshape(N, 128, 2048), rng)
    return {"wc": c, "ws": s}
def setup_inputs(rng):
    return {**numbers_of(rng), **stored(*lists(rng)), **weights(rng, layers(rng))}
def setup_inputs_ties(rng):
    d = numbers_of(rng)
    k, n = lists(rng)
    o, h = rng.permutation(N), rng.permutation(8)
    i = np.arange(N)
    e = (i ^ (i >> 1) ^ (i >> 2)) % 2
    s = rng.integers(0, 4, (N, 8, C))
    s[o[1]] += 1
    s[:, h[:3]] = 1
    for g in h[:2]:
        for r in np.flatnonzero(e):
            k[r, g] = n[r, g]
            s[r, g] = np.where(np.arange(C) < n[r, g], 2, 0)
    c = np.ones((N, 8), np.float32)
    c[o[0]] = 0
    c[o[1]] = -1
    c[:, h[:3]] = 1
    x = d["x"].reshape(N, 8, 16, C, 4)
    x[:, :, 0] = 0
    x[:, :, 0, :, 0] = s.astype(np.float32).astype(BF)
    a = np.exp2(rng.integers(-3, 4, (1, 8, 1)).astype(np.float32))
    x[:, :, 8:] = 0
    x[:, :, 8, :, 0] = (-1.125 * a).astype(BF)
    x[:, :, 10, :, 0] = (-0.0703125 * a).astype(BF)
    u = d["u"].reshape(N, 128, 128, 4)
    u[:, :, ::16] = 0
    w = layers(rng, [0])
    w[:, :, :, :, :, 8:] = 0
    for g in range(8):
        u[:, 16 * g, 16 * g, 0] = c[:, g].astype(BF)
        w[:, g, 8, 0, g, 8, 0] = -28.0
        for b in range(4): w[:, g, 10, b, g, 9, 0] = -2.0 ** (b - 5)
    return {"x": x.reshape(N, 128, 4 * C), "u": u.reshape(N, 128, 512), "v": d["v"], **stored(k, n), **weights(rng, w)}
def setup_inputs_near(rng):
    d = numbers_of(rng)
    k, n = lists(rng)
    x = d["x"].astype(np.float32).reshape(N, 8, 16, C, 4)
    x[:, :, 0] = 0
    x[:, :, 8:] = 0
    u = d["u"].reshape(N, 128, 128, 4)
    u[:, :, ::16] = 0
    w = layers(rng, [0, 8, 9, 10, 11, 12, 13, 14, 15])
    at = [0, C - 1, int(rng.integers(C)), int(rng.integers(C))]
    for i, g in enumerate(rng.permutation(8)):
        h, c = 16 * g, 1.0 if i < 2 else 2.0 ** -30
        s = rng.integers(0, 16, (N, C))
        digits = ((s[:, :, None] >> np.arange(4)) & 1) * np.exp2(np.arange(4) - 23.0)
        u[:, h, h, 0] = c
        if i < 4:
            x[:, g, 0, :, 0] = i % 2 * 3.0 - 1.5
            x[:, g, 8] = digits
            x[:, g, 11, :, 0] = 2.0 ** -10
            u[:, h + 11, h, 0] = c
        elif i < 6: x[:, g, 8] = digits * rng.choice([-1.0, 1.0], (N, C, 1))
        else:
            x[:, g, 10, :, 0] = rng.choice([-1.0, 1.0], (N, C)) * 2.0 ** -30
            x[:, g, 11, :, 0] = 2.0 ** -29
            w[:, g, 10, 0, g, 9, 0] = 2.0 ** -9
            w[:, g, 12, 0, g, 9, 0] = 1.0
            w[:, g, 10, 0, g, 13, 0] = -2.0 ** -9
            w[:, g, 12, 0, g, 13, 0] = 1.0
            w[:, g, 11, 0, g, 11, 0] = 16.0
            u[:, h + 9, h, 0] = 1.125 * c
            u[:, h + 13, h, 0] = c
        if i < 6: u[:, h + 8, h] = c
        if i % 2: x[:, g, 0, at[i // 2], 0] = 2.0 ** 29 * rng.choice([-1.0, 1.0], N)
    return {"x": x.reshape(N, 128, 4 * C).astype(BF), "u": u.reshape(N, 128, 512), "v": d["v"], **stored(k, n), **weights(rng, w)}
def setup_inputs_odd(rng):
    d = numbers_of(rng)
    x = (1.0 + (2 * rng.integers(0, 64, (N, 16, 8, C, 4)) + 1) * 2.0 ** -7) * np.exp2(-rng.integers(0, 7, (N, 16, 8, C, 4)).astype(np.float64)) * rng.choice([-1.0, 1.0], (N, 16, 8, C, 4))
    x[:, :, 0, :, 0] = 1.96875 * 2.0 ** 8 * rng.choice([-1.0, 1.0], (N, 16, C))
    x[:, ::2, 1, :, 0] = (8 + rng.integers(0, 2, (N, 8, C))) * 2.0 ** -8
    u = d["u"].reshape(N, 128, 128, 4)
    u[:, :, ::16] = 0
    for h in range(0, 128, 16): u[:, h + 1, h, 0] = 1.0
    return {"x": x.astype(np.float32).reshape(N, 128, 4 * C).astype(BF), "u": u.reshape(N, 128, 512), "v": d["v"], **stored(*lists(rng)), **weights(rng, layers(rng, [0, 8]))}
def setup_inputs_ends(rng):
    d = numbers_of(rng)
    k, n = lists(rng)
    j = np.arange(C)
    o = np.zeros(N, np.int64)
    for i, r in enumerate(rng.permutation([r for r in range(N) if not r & MASK[0]])):
        o[r], o[r ^ MASK[0]] = rng.permutation([1, 2] if i % 2 else [0, 3])
    e, h = rng.permutation(N) % 4, rng.permutation(N) % 4
    k[e == 0] = j
    k[e == 1] = j[::-1]
    k[e == 2] = (j + 1) % C
    n[h == 0] = j[::-1]
    n[h == 1] = j ^ 1
    n[h == 2] = (j + C // 2) % C
    s = rng.choice([-1.0, 1.0], (N, 8, 16, C, 4))
    s[o == 0] = -1
    s[o == 1] = rng.choice([-1.0, 1.0], (N, 1, 1, C, 1))[o == 1]
    x = s * (0.955 + 0.02 * rng.random((N, 8, 16, C, 4))) * 2.0 ** 30
    x[o == 3] = 2.0 ** -30
    g = int(rng.integers(8))
    x[:, g, :8] = 2.0 ** -30
    size = np.where(o == 3, 2.0 ** -30, 2.0 ** 30)
    a = np.stack([rng.permutation(8) % 2 * 2.0 - 1.0 for r in range(N)]) * size[:, None]
    u = d["u"].reshape(N, 128, 128, 4)
    u[:, :, ::16] = a.astype(np.float32).astype(BF)[:, None, :, None]
    v = rng.choice([-1.0, 1.0], (N, 128, 512)) * size[:, None, None]
    w = np.zeros((N, 128, 4, 128, 4), np.float32)
    i, l = np.arange(128), np.arange(16 * g, 16 * g + 8)
    for b in range(4):
        w[:, i, b, i, b] = np.where(o == 3, 32.0, -0.125)[:, None]
        w[:, l, b, l, b] = np.where(o == 3, 256.0, 0.0)[:, None]
    return {"x": x.astype(np.float32).reshape(N, 128, 4 * C).astype(BF), "u": u.reshape(N, 128, 512), "v": v.astype(np.float32).astype(BF), **stored(k, n), **weights(rng, w.astype(BF))}
def setup_inputs_spread(rng):
    d = setup_inputs(rng)
    d["x"] = wide(rng, N, 128, 4 * C, cols=6)
    return d
def check_inputs(d):
    b = []
    for k in ("x", "u", "v"):
        a = np.abs(d[k].astype(np.float32))
        if not (np.isfinite(a).all() and ((a == 0) | (a >= 2.0 ** -30) & (a <= 2.0 ** 30)).all()): b.append("a value of " + k)
    none, least, most = [emit(mx_ref.quantize(np.full((128, 16), k, np.float32).astype(BF)))[1][0, 0] for k in (0.0, 2.0 ** -8, 2.0 ** 8)]
    top = emit(mx_ref.quantize(np.ascontiguousarray(np.tile(np.repeat(1.0 + np.arange(128) * 2.0 ** -7, 4), (128, 1))).astype(np.float32).astype(BF)))[0] & 0x7F
    for r in range(N):
        k, n = gentries(d["dl"][r]), gentries(d["nl"][r])
        if not (np.sort(k, axis=1) == np.arange(C)).all(): b.append("dl: not every column once")
        if not ((n >= 0) & (n < C)).all(): b.append("an entry of nl")
        elif not ((at(n, n) == np.arange(C)) & (n != np.arange(C))).all(): b.append("nl: not in pairs")
        if ((d["wc"][r] == 0x7F) | (d["wc"][r] == 0xFF)).any(): b.append("wc: a code that is no number")
        s = mx_ref.live(d["ws"][r])
        if ((s != none) & ((s < least) | (s > most))).any(): b.append("ws: a scale out of range")
        a = np.max(d["wc"][r].reshape(16, 8, 512, 4) & 0x7F, axis=(1, 3))
        if ((s == none) & (a != 0)).any(): b.append("wc: a code other than zero under the scale of zeros")
        if ((s != none) & ((a < top.min()) | (a > top.max()))).any(): b.append("wc: a block whose largest code isn't one of quantize_mx")
    return b
def at(t, e):
    return np.take_along_axis(t, e, axis=1)
def layer(w, q):
    return tile([mx_ref.matmul(pick(w, np.arange(128 * b, 128 * b + 128)), q) * np.float32(0.03125) for b in range(4)])
def reference(x, u, v, dl, nl, wc, ws):
    qu = [mx_ref.quantize(u[r]) for r in range(N)]
    lay = [pk(wc[r], ws[r]) for r in range(N)]
    d, n = [gentries(dl[r]) for r in range(N)], [gentries(nl[r]) for r in range(N)]
    now = [x[r] for r in range(N)]
    for m in MASK:
        s = [mx_ref.matmul(qu[r], mx_ref.quantize(now[r]))[::16] + np.float32(0.0) for r in range(N)]
        new, h, made = [], [], []
        for r in range(N):
            p = r ^ m
            a, b, k = np.tile(np.arange(C), (8, 1)), n[r], np.zeros((8, C), np.int64)
            for step in range(6):
                own = at(s[r], a) > at(s[p], b)
                a, b, k = np.where(own, at(d[r], a), a), np.where(own, b, at(d[p], b)), k + own
            z = ((gcols(now[r], a).astype(np.float32) + gcols(now[r], b).astype(np.float32)) * np.float32(0.5)).astype(BF)
            h.append(layer(lay[r], mx_ref.quantize(z)))
            new.append(np.where((k + at(k, n[r])) % 2 == 1, at(d[r], n[r]), d[r]))
        for r in range(N):
            p = r ^ m
            far = decode(mx_ref.quantize(np.ascontiguousarray(h[p][:, :4 * F]))).astype(BF)
            both = np.concatenate([far, h[r][:, 4 * F:]], axis=1)
            place = at(np.argsort(d[p], axis=1), new[r])
            made.append((now[r].astype(np.float32) + gcols(both, place).astype(np.float32)).astype(BF))
        now, d = made, new
    y, dn = np.zeros((N, 128, C), np.float32), np.zeros((N, 8, C), np.float32)
    oc, osc = np.zeros((N, 128, 4 * C), np.uint8), np.zeros((N, 16, C), np.uint8)
    for r in range(N):
        q = mx_ref.quantize(now[r])
        y[r] = mx_ref.matmul(mx_ref.quantize(v[r]), q)
        dn[r] = d[r]
        oc[r], osc[r] = emit(q)
    return {"y": y, "dn": dn, "oc": oc, "osc": osc}

@@ -1,0 +1,423 @@
+import numpy as np
+from concourse.mybir import dt, AluOpType as A, ActivationFunctionType as F
+
+C, FAR, HALF = 320, 240, 160
+MASKS = [4, 1, 2]
+HUGE = 2.0 ** 80
+UNIT = 2.0 ** 18
+
+f32, b16, i32, u16, q8, u8 = "float32", "bfloat16", "int32", "uint16", "float8_e4m3fn_x4", "uint8"
+SCRATCH = {
+    "xa": ("sbuf", [128, 4 * C], b16), "xb": ("sbuf", [128, 4 * C], b16),
+    "xh": ("sbuf", [128, 4 * C], b16), "zb": ("sbuf", [128, 4 * C], b16), "z": ("sbuf", [128, 4 * C], b16),
+    "h": ("sbuf", [128, 4 * C], b16), "j": ("sbuf", [128, 4 * C], b16),
+    "ut": ("sbuf", [128, 512], b16), "vt": ("sbuf", [128, 512], b16),
+    "ones": ("sbuf", [128, 512], b16), "eb": ("sbuf", [128, 2048], b16),
+    "qu": ("sbuf", [128, 128], q8), "pu": ("sbuf", [128, 128], u8),
+    "qr": ("sbuf", [128, 128], q8), "pr": ("sbuf", [128, 128], u8),
+    "qv": ("sbuf", [128, 128], q8), "pv": ("sbuf", [128, 128], u8),
+    "qe": ("sbuf", [128, 512], q8), "pe": ("sbuf", [128, 512], u8),
+    "qw": ("sbuf", [128, 512], q8), "pw": ("sbuf", [128, 512], u8),
+    "qx": ("sbuf", [128, C], q8), "px": ("sbuf", [128, C], u8),
+    "qz": ("sbuf", [128, C], q8), "pz": ("sbuf", [128, C], u8),
+    "dli": ("sbuf", [128, 20], i32), "nli": ("sbuf", [128, 20], i32),
+    "n_o": ("sbuf", [128, 20], u16), "f_o0": ("sbuf", [128, 20], u16),
+    "d_f0": ("sbuf", [128, 20], f32), "d_f1": ("sbuf", [128, 20], f32), "ddif": ("sbuf", [128, 20], f32),
+    "a_o": ("sbuf", [128, 20], u16), "b_o": ("sbuf", [128, 20], u16), "l_o": ("sbuf", [128, 20], u16),
+    "ints": ("sbuf", [128, 120], i32),
+    "parf": ("sbuf", [128, 20], f32), "dnf": ("sbuf", [128, 20], f32),
+    "ta": ("sbuf", [128, 24], f32), "tb": ("sbuf", [128, 24], f32),
+    "pidx": ("sbuf", [128, 1], i32), "sli": ("sbuf", [128, 1], i32), "hfi": ("sbuf", [128, 1], i32),
+    "rowi": ("sbuf", [128, 8], i32), "row_o": ("sbuf", [128, 8], u16),
+    "cst": ("sbuf", [128, 24], f32), "tv": ("sbuf", [128, 6], f32),
+    "iot": ("sbuf", [128, C], f32), "i512": ("sbuf", [128, C], f32), "cs": ("sbuf", [128, 672], f32),
+    "mask": ("sbuf", [128, C], f32), "seg": ("sbuf", [128, C], f32), "hold": ("sbuf", [128, C], f32),
+    "kt": ("sbuf", [128, 672], b16), "b0": ("sbuf", [128, C], f32),
+    "ts": ("sbuf", [128, C], f32), "bf": ("sbuf", [128, C], f32), "sbp": ("sbuf", [128, C], f32),
+    "tmt": ("sbuf", [128, C], f32), "tat": ("sbuf", [128, C], f32), "tbt": ("sbuf", [128, C], f32),
+    "wa": ("sbuf", [128, C], f32), "wb": ("sbuf", [128, C], f32), "m0": ("sbuf", [128, C], f32),
+    "einv": ("sbuf", [128, C], f32), "xm": ("sbuf", [128, C], f32), "xs": ("sbuf", [128, C], f32),
+    "irow": ("sbuf", [128, 352], b16), "irow2": ("sbuf", [128, 352], b16), "prow": ("sbuf", [128, 352], f32),
+    "tin": ("sbuf", [128, 672], b16), "tin2": ("sbuf", [128, 672], b16), "tp": ("sbuf", [128, 672], f32),
+    "sc": ("sbuf", [128, 672], f32), "sc2": ("sbuf", [128, 672], b16),
+}
+for _r in range(3):
+    SCRATCH["ss%d" % _r] = ("sbuf", [128, 20], f32)
+    SCRATCH["sl%d" % _r] = ("sbuf", [128, 20], f32)
+    SCRATCH["el%d" % _r] = ("sbuf", [128, 20], u16)
+    SCRATCH["f_o%d" % (_r + 1)] = ("sbuf", [128, 20], u16)
+    SCRATCH["qh%d" % _r] = ("sbuf", [128, C], q8)
+    SCRATCH["ph%d" % _r] = ("sbuf", [128, C], u8)
+    SCRATCH["ql%d" % _r] = ("sbuf", [128, FAR], q8)
+    SCRATCH["pl%d" % _r] = ("sbuf", [128, FAR], u8)
+for _c in "mr", "ar", "br", "yp":
+    SCRATCH[_c + "a"] = ("sbuf", [128, 3 * C], f32)
+    SCRATCH[_c + "b"] = ("sbuf", [128, 3 * C], f32)
+for _i in range(8):
+    SCRATCH["ps%d" % _i] = ("psum", [128, 512], f32)
+
+SEMAPHORES = ["sv", "sa", "st", "sg", "sent", "ldx", "ldu", "ldw", "ldv", "ldd", "ldn", "out", "ta", "tb", "tm"]
+for _r in range(3):
+    SEMAPHORES += ["s%d" % _r, "e%d" % _r, "ca%d" % _r, "cb%d" % _r, "cp%d" % _r]
+
+
+def rank_program(g, core, T, topo):
+    rank = T.rank_of(core)
+    if rank is None:
+        return
+    V, S, P, Y = g.vector, g.scalar, g.tensor, g.sync
+    queue = {"v": V, "s": S, "p": P, "y": Y, "g": g}
+    cnt = {"sv": 0, "sa": 0, "st": 0, "sg": 0, "sent": 0, "ta": 0, "tb": 0, "tm": 0}
+    known = {}
+
+    def need(q, sem, n):
+        if known.get((q, sem), 0) < n:
+            queue[q].wait_ge(T.sem[sem], n)
+            known[(q, sem)] = n
+
+    def done(sem, ins, k=1):
+        ins.then_inc(T.sem[sem], k)
+        cnt[sem] += k
+        return cnt[sem]
+
+    def v(ins):
+        return done("sv", ins)
+
+    def s(ins):
+        return done("sa", ins)
+
+    def p(ins):
+        return done("st", ins)
+
+    def gc(ins):
+        return done("sg", ins)
+
+    def vv(n=None):
+        need("v", "sv", cnt["sv"] if n is None else n)
+
+    def peer(r):
+        return T.cores[rank ^ MASKS[r]]
+
+    def send(dst, out, in_, sem):
+        rid, pid = topo.addr(dst, core)
+        g.remote_dma(out, in_, T.sem[sem], T.sem.sent, pid, rid, topo.mask(core, dst))
+        cnt["sent"] += len(topo.engines(core, dst))
+
+    def landed(q, r, sem):
+        need(q, "%s%d" % (sem, r), len(topo.engines(peer(r), core)))
+
+    def slot(sem, tile, i, src):
+        done(sem, Y.dma_start(tile[i:128:16, :], src), 16)
+
+    def rows(name, k, i=None):
+        lo = C * (k // 2)
+        buf = T[name + "ab"[k % 2]]
+        return buf[:, lo:lo + C] if i is None else buf[i:128:16, lo:lo + C]
+
+    Y.dma_start(T.xa[:], T.x[:]).then_inc(T.sem.ldx, 16)
+    S.dma_start(T.dli[:], T.dl[:]).then_inc(T.sem.ldd, 16)
+    S.dma_start(T.ut[:], T.u[:]).then_inc(T.sem.ldu, 16)
+    S.dma_start(T.nli[:], T.nl[:]).then_inc(T.sem.ldn, 16)
+    Y.dma_start(T.qw[:].bitcast(dt.uint8), T.wc[:]).then_inc(T.sem.ldw, 16)
+    Y.dma_start(T.pw[:], T.ws[:]).then_inc(T.sem.ldw, 16)
+    Y.dma_start(T.vt[:], T.v[:]).then_inc(T.sem.ldv, 16)
+
+    gc(g.iota(T.pidx[:], [[0, 1]], 0, 1))
+    gc(g.iota(T.rowi[:], [[16, 8]], 0, 0))
+    g1 = gc(g.iota(T.tv[:], [[1, 6]], 1, 0, allow_small_or_imprecise_dtypes=True))
+    g2 = gc(g.iota(T.iot[:], [[1, C]], 0, 0, allow_small_or_imprecise_dtypes=True))
+
+    def col(k):
+        return T.cst[:, k:k + 1]
+    SLOT, M1, M0, LE6, S7 = range(5)
+    actp, bip = T.cst[:, 8:14], T.cst[:, 14:20]
+    v(V.memset(T.tat[:], 0.0))
+    ms = v(V.memset(T.tbt[:], 0.0))
+    need("v", "sg", g1)
+    v(V.tensor_scalar(T.sli[:], T.pidx[:], 15, None, A.bitwise_and))
+    v(V.tensor_scalar(T.hfi[:], T.pidx[:], 16, None, A.bitwise_and))
+    v(V.tensor_copy(T.row_o[:], T.rowi[:]))
+    vv()
+    v(V.tensor_copy(col(SLOT), T.sli[:]))
+    v(V.tensor_scalar(col(M1), T.hfi[:], 0.0625, None, A.mult))
+    vv()
+    sl = col(SLOT)
+    v(V.tensor_scalar(col(M0), col(M1), -1.0, 1.0, A.mult, A.add))
+    v(V.tensor_scalar(col(LE6), sl, 6.0, None, A.is_le))
+    v(V.tensor_scalar(col(S7), sl, -1.0, 7.0, A.mult, A.add))
+    vv()
+    v(V.tensor_scalar(actp, T.tv[:], col(S7), col(LE6), A.is_ge, A.mult))
+    vv()
+    v(V.tensor_scalar(bip, actp, -HUGE, HUGE, A.mult, A.add))
+    need("v", "ldd", 16)
+    vd = v(V.tensor_copy(T.f_o0[:], T.dli[:]))
+    v(V.tensor_copy(T.d_f0[:], T.dli[:]))
+    need("g", "sv", vd)
+    send(peer(0), T.el0[:], T.f_o0[:], "e0")
+    g3 = gc(g.iota(T.cs[:], [[0, 42], [1, 16]], 0, 0, allow_small_or_imprecise_dtypes=True))
+    need("v", "sg", g2)
+    vi = v(V.tensor_scalar(T.i512[:], T.iot[:], 512.0, None, A.mult))
+    v(V.memset(T.tmt[:], HUGE))
+    v(V.memset(T.b0[:], 0.0))
+    need("v", "ldu", 16)
+    v(V.quantize_mx(T.qu[:], T.pu[:], T.ut[:]))
+    vv()
+    v(V.tensor_copy(T.qr[:].bitcast(dt.uint32), T.qu[:].bitcast(dt.uint32).indirect(T.row_o[:])))
+    v(V.tensor_copy(T.pr[:], T.pu[:].indirect(T.row_o[:])))
+    need("v", "ldn", 16)
+    v(V.tensor_copy(T.n_o[:], T.nli[:]))
+    need("y", "sg", g2)
+    need("y", "sv", vi)
+    slot("ta", T.tat, 6, T.iot[6:128:16, :])
+    slot("tb", T.tbt, 0, T.i512[0:128:16, :])
+    need("v", "ldx", 16)
+
+    po_, ai_, bi_, ki_, k2_, par_ = [T.ints[:, 20 * k:20 * k + 20] for k in range(6)]
+    X = [T.xa, T.xb, T.xa, T.xb]
+    ps = [T["ps%d" % i] for i in range(8)]
+
+    def scan_pick(src, out):
+        vv()
+        v(V.tensor_tensor_scan(T.xs[:], T.seg[:], src, 0.0, A.mult, A.add))
+        vv()
+        return v(V.tensor_copy(out, T.xs[:, 15:C:16]))
+
+    def to_offsets(sc, out):
+        vv()
+        v(V.tensor_scalar(T.ta[:, 0:21], sc[:, 6:672:32], col(M0), None, A.mult))
+        v(V.tensor_scalar(T.tb[:, 0:21], sc[:, 22:672:32], col(M1), None, A.mult))
+        vv()
+        v(V.tensor_tensor(T.ints[:, out:out + 20:2], T.ta[:, 0:10], T.tb[:, 10:20], A.add))
+        return v(V.tensor_tensor(T.ints[:, out + 1:out + 20:2], T.ta[:, 11:21], T.tb[:, 0:10], A.add))
+
+    def own_places(f_o, ks):
+        for k in ks:
+            win = T.iot[:] if k == 1 else rows("ar", k - 2)
+            if k > 1:
+                need("s", "sa", na_[0])
+            na_[0] = s(S.activation(rows("ar", k - 1), win.indirect(f_o[:]), F.Identity, bias=UNIT))
+            need("y", "sa", na_[0])
+            slot("ta", T.tat, 6 - k, rows("ar", k - 1, 6 - k))
+    na_ = [0]
+
+    def far_places(e_o, ks):
+        for k in ks:
+            win = T.i512[:] if k == 1 else rows("br", k - 2)
+            if k > 1:
+                need("s", "sa", nb_[0])
+            nb_[0] = s(S.activation(rows("br", k - 1), win.indirect(e_o[:]), F.Copy))
+            need("y", "sa", nb_[0])
+            slot("tb", T.tbt, k, rows("br", k - 1, k))
+    nb_ = [0]
+
+    need("s", "sg", g2)
+    need("s", "sv", vi)
+    own_places(T.f_o0, range(1, 7))
+
+    for r in range(3):
+        x, xn = X[r], X[r + 1]
+        d_o, e_o, f_o = T["f_o%d" % r], T["el%d" % r], T["f_o%d" % (r + 1)]
+        d_f, f_f = (T.d_f0, T.d_f1) if r % 2 == 0 else (T.d_f1, T.d_f0)
+        vv()
+        need("p", "sv", v(V.quantize_mx(T.qx[:], T.px[:], x[:])))
+        t1 = p(P.matmul_mx(ps[0][:, 0:C], T.qr[:], T.pr[:], T.qx[:], T.px[:], True, True))
+        t2 = p(P.matmul_mx(ps[1][:, 0:C], T.qr[:], T.pr[:], T.qx[:], T.px[:], True, True))
+        need("v", "st", t1)
+        v(V.transpose(T.ts[:], ps[0][:, 0:C]))
+        vv()
+        need("g", "sv", v(V.tensor_copy(T["ss%d" % r][:], T.ts[:, 0:C:16])))
+        send(peer(r), T["sl%d" % r][:], T["ss%d" % r][:], "s%d" % r)
+        need("s", "st", t2)
+        v(V.tensor_copy(T.m0[:], ps[0][:, 0:C]))
+        n = s(S.activation(rows("mr", 0), ps[1][:, 0:C], F.Copy))
+        landed("s", r, "e")
+        far_places(e_o, range(1, 7) if r == 0 else range(3, 7))
+        need("y", "sa", n)
+        slot("tm", T.tmt, 6, rows("mr", 0, 6))
+        need("v", "sa", n)
+        for k in range(1, 6):
+            vv()
+            n = v(V.tensor_tensor(rows("mr", k), rows("mr", k - 1).indirect(d_o[:]), T.m0[:], A.min))
+            need("y", "sv", n)
+            slot("tm", T.tmt, 6 - k, rows("mr", k, 6 - k))
+        for k in range(4):
+            s(S.activation(T.xh[:, C * k:C * k + C], x[:, k:4 * C:4], F.Copy, scale=0.5))
+        if r == 0:
+            v(V.memset(T.ones[:], 1.0))
+            need("g", "sv", cnt["sv"])
+            for b in range(4):
+                g4 = gc(g.affine_select(T.eb[:, 512 * b:512 * b + 512], T.ones[:], [[-1, 512]], A.is_equal, 0.0, b, 4))
+            need("v", "sg", g3)
+            v(V.tensor_scalar(T.hold[:], T.cs[:, 0:C], 2.0, None, A.is_ge))
+            v(V.memset(T.irow[:], 0.0))
+            v(V.memset(T.prow[:], 0.0))
+            vv()
+        landed("v", r, "e")
+        v(V.tensor_copy(T.einv[:].indirect(e_o[:]), T.iot[:]))
+        need("v", "ta", cnt["ta"])
+        need("v", "tb", cnt["tb"])
+        v(V.tensor_tensor(T.prow[:, 16:336], T.tbt[:].indirect(T.n_o[:]), T.tat[:], A.add))
+        vv()
+        v(V.transpose(T.tp[:, 0:320], T.prow[:, 16:336]))
+        v(V.transpose(T.tp[:, 320:672], T.prow[:, 0:352]))
+        landed("v", r, "s")
+        v(V.tensor_copy(T.b0[:, 1:C:16], T["sl%d" % r][:]))
+        vv()
+        v(V.tensor_tensor_scan(T.bf[:], T.hold[:], T.b0[:], 0.0, A.mult, A.add))
+        vv()
+        n = v(V.transpose(T.sbp[:], T.bf[:]))
+        need("s", "sv", n)
+        ya = [s(S.activation(rows("yp", k), T.sbp[:], F.Identity, bias=bip[:, k:k + 1], scale=actp[:, k:k + 1])) for k in range(1, 6)]
+        vv()
+        v(V.tensor_scalar(rows("yp", 0), T.sbp[:], actp[:, 0:1], bip[:, 0:1], A.mult, A.add))
+        win = rows("yp", 0)
+        for k in range(1, 6):
+            need("v", "sa", ya[k - 1])
+            vv()
+            out = (T.wa if k % 2 else T.wb)[:]
+            v(V.tensor_tensor(out, win.indirect(e_o[:]), rows("yp", k), A.min))
+            win = out
+        need("v", "tm", cnt["tm"])
+        vv()
+        v(V.tensor_tensor(T.irow[:, 16:336], win.indirect(T.n_o[:]), T.tmt[:], A.is_lt))
+        vv()
+        v(V.transpose(T.tin[:, 0:320], T.irow[:, 16:336]))
+        nir = v(V.transpose(T.tin[:, 320:672], T.irow[:, 0:352]))
+        vv()
+        v(V.tensor_tensor_scan(T.sc[:], T.tin[:], T.tp[:], 0.0, A.mult, A.max))
+        to_offsets(T.sc, 0)
+        vv()
+        n1 = v(V.tensor_scalar(bi_, po_, 9, 511, A.logical_shift_right, A.bitwise_and))
+        n2 = v(V.tensor_scalar(ai_, po_, 511, None, A.bitwise_and))
+        vv(n1)
+        nb = v(V.tensor_copy(T.b_o[:], bi_))
+        vv(n2)
+        na = v(V.tensor_copy(T.a_o[:], ai_))
+        need("s", "sv", nb)
+        za = [[s(S.activation(T.zb[:, C * k + HALF * h:C * k + HALF * h + HALF], T.xh[:, C * k:C * k + C].indirect(T.b_o[:, 10 * h:10 * h + 10]), F.Copy)) for k in range(4)] for h in range(2)]
+        tz = []
+        if r == 0:
+            need("p", "ldw", 32)
+        for h in range(2):
+            for k in range(4):
+                need("v", "sa", za[h][k])
+                vv(na)
+                v(V.tensor_tensor(T.z[:, 4 * HALF * h + k:4 * HALF * h + 4 * HALF:4], T.xh[:, C * k:C * k + C].indirect(T.a_o[:, 10 * h:10 * h + 10]), T.zb[:, C * k + HALF * h:C * k + HALF * h + HALF], A.add))
+            vv()
+            lo, hi = HALF * h, HALF * h + HALF
+            need("p", "sv", v(V.quantize_mx(T.qz[:, lo:hi], T.pz[:, lo:hi], T.z[:, 4 * lo:4 * hi])))
+            tz.append([p(P.matmul_mx(ps[4 * h + b][:, 0:HALF], T.qw[:, 128 * b:128 * b + 128], T.pw[:, 128 * b:128 * b + 128], T.qz[:, lo:hi], T.pz[:, lo:hi], True, True)) for b in range(4)])
+        qh, ph = T["qh%d" % r], T["ph%d" % r]
+        for b in range(4):
+            need("s", "st", tz[0][b])
+            ha = s(S.activation(T.h[:, b:4 * HALF:4], ps[b][:, 0:HALF], F.Copy, scale=0.03125))
+        for b in range(2):
+            need("s", "st", tz[1][b])
+            hb = s(S.activation(T.h[:, 4 * HALF + b:4 * C:4], ps[4 + b][:, 0:HALF], F.Copy, scale=0.03125))
+        need("v", "sa", ha)
+        n1 = v(V.quantize_mx(qh[:, 0:HALF], ph[:, 0:HALF], T.h[:, 0:4 * HALF]))
+        for b in range(2, 4):
+            need("v", "st", tz[1][b])
+            vb = v(V.tensor_scalar(T.h[:, 4 * HALF + b:4 * C:4], ps[4 + b][:, 0:HALF], 0.03125, None, A.mult))
+        need("v", "sa", hb)
+        vv()
+        n2 = v(V.quantize_mx(qh[:, HALF:C], ph[:, HALF:C], T.h[:, 4 * HALF:4 * C]))
+        need("g", "sv", n1)
+        send(peer(r), T["ql%d" % r][:, 0:HALF].bitcast(dt.uint8), qh[:, 0:HALF].bitcast(dt.uint8), "ca%d" % r)
+        need("g", "sv", n2)
+        send(peer(r), T["ql%d" % r][:, HALF:FAR].bitcast(dt.uint8), qh[:, HALF:FAR].bitcast(dt.uint8), "cb%d" % r)
+        send(peer(r), T["pl%d" % r][:, 0:FAR], ph[:, 0:FAR], "cp%d" % r)
+        if r == 0:
+            v(V.memset(T.irow2[:], 0.0))
+            vv()
+            need("s", "sv", cnt["sv"])
+        ni = s(S.activation(T.irow2[:, 16:336], T.irow[:, 16:336].indirect(T.n_o[:]), F.Copy))
+        for b in range(4):
+            if b == 2:
+                need("s", "sv", vb)
+            s(S.activation(T.j[:, C * b + FAR:C * b + C], ps[4 + b][:, FAR - HALF:HALF], F.Copy, scale=0.03125))
+        v(V.tensor_scalar(ki_, po_, 18, None, A.logical_shift_right))
+        if r == 0:
+            v(V.tensor_scalar(T.mask[:], T.cs[:, 0:C], sl, None, A.is_equal))
+            v(V.tensor_scalar(T.seg[:], T.cs[:, 0:C], 1.0, None, A.is_ge))
+            v(V.tensor_scalar(T.kt[:], T.cs[:], -1.0, 6.0, A.mult, A.add))
+            vv()
+            v(V.tensor_tensor(T.xm[:], rows("ar", 0).indirect(T.n_o[:]), T.mask[:], A.mult))
+            scan_pick(T.xm[:], T.parf[:])
+            vv()
+            v(V.tensor_scalar(T.dnf[:], T.parf[:], UNIT, None, A.subtract))
+            vv()
+            v(V.tensor_tensor(T.ddif[:], T.dnf[:], d_f[:], A.subtract))
+        need("v", "sa", ni)
+        v(V.transpose(T.tin2[:, 0:320], T.irow2[:, 16:336]))
+        v(V.transpose(T.tin2[:, 320:672], T.irow2[:, 0:352]))
+        vv()
+        v(V.tensor_tensor_scan(T.sc2[:], T.tin2[:], T.kt[:], 0.0, A.mult, A.max))
+        to_offsets(T.sc2, 80)
+        vv()
+        v(V.tensor_tensor(par_, ki_, k2_, A.add))
+        vv()
+        v(V.tensor_scalar(par_, par_, 1, None, A.bitwise_and))
+        vv()
+        v(V.tensor_copy(T.parf[:], par_))
+        vv()
+        v(V.tensor_tensor(T.parf[:], T.parf[:], T.ddif[:], A.mult))
+        vv()
+        v(V.tensor_tensor(f_f[:], d_f[:], T.parf[:], A.add))
+        vv()
+        nf = v(V.tensor_copy(f_o[:], f_f[:]))
+        if r < 2:
+            need("g", "sv", nf)
+            send(peer(r + 1), T["el%d" % (r + 1)][:], f_o[:], "e%d" % (r + 1))
+        vv()
+        v(V.tensor_tensor(T.xm[:], T.einv[:].indirect(f_o[:]), T.mask[:], A.mult))
+        nl = scan_pick(T.xm[:], T.l_o[:])
+        need("s", "sv", nf)
+        if r < 2:
+            own_places(f_o, range(1, 5))
+            v(V.tensor_scalar(T.dnf[:], T.parf[:], -2.0, None, A.mult))
+            vv()
+            v(V.tensor_tensor(T.ddif[:], T.ddif[:], T.dnf[:], A.add))
+        else:
+            n = s(S.activation(rows("ar", 0), T.iot[:].indirect(f_o[:]), F.Copy))
+            need("y", "sa", n)
+            Y.dma_start(T.dn[:], rows("ar", 0, 0)).then_inc(T.sem.out, 16)
+        if r == 0:
+            need("v", "sg", g4)
+            v(V.quantize_mx(T.qe[:], T.pe[:], T.eb[:]))
+            need("p", "sv", cnt["sv"])
+        if r == 1:
+            need("v", "ldv", 16)
+            v(V.quantize_mx(T.qv[:], T.pv[:], T.vt[:]))
+        need("p", "sa", ha)
+        need("p", "sv", vb)
+        for k in ("ca", "cb", "cp"):
+            landed("p", r, k)
+        for b in range(4):
+            td = p(P.matmul_mx(ps[b][:, 0:FAR], T.qe[:, 128 * b:128 * b + 128], T.pe[:, 128 * b:128 * b + 128], T["ql%d" % r][:], T["pl%d" % r][:], True, True))
+            need("s", "st", td)
+            ja = s(S.activation(T.j[:, C * b:C * b + FAR], ps[b][:, 0:FAR], F.Copy))
+            need("v", "sa", ja)
+            vv(nl)
+            v(V.tensor_tensor(xn[:, b:4 * C:4], T.j[:, C * b:C * b + C].indirect(T.l_o[:]), x[:, b:4 * C:4], A.add))
+        if r < 2:
+            own_places(f_o, range(5, 7))
+            landed("s", r + 1, "e")
+            far_places(T["el%d" % (r + 1)], range(1, 3))
+
+    vv()
+    n = v(V.quantize_mx(T.qx[:], T.px[:], X[3][:]))
+    need("p", "sv", n)
+    t = p(P.matmul_mx(ps[0][:, 0:C], T.qv[:], T.pv[:], T.qx[:], T.px[:], True, True))
+    need("y", "sv", n)
+    need("s", "sv", n)
+    Y.dma_start(T.oc[:], T.qx[:].bitcast(dt.uint8)).then_inc(T.sem.out, 16)
+    for k in range(4):
+        (S if k % 2 else Y).dma_start(T.osc[4 * k:4 * k + 4, :], T.px[32 * k:32 * k + 4, :]).then_inc(T.sem.out, 16)
+    need("v", "st", t)
+    n = v(V.tensor_copy(T.ts[:], ps[0][:, 0:C]))
+    need("y", "sv", n)
+    Y.dma_start(T.y[:], T.ts[:]).then_inc(T.sem.out, 16)
+    g.wait_ge(T.sem.out, 16 * 7)
+    for k in ("sv", "sa", "st", "sg", "sent", "ta", "tb", "tm"):
+        need("g", k, cnt[k])

@@ -1,16 +1,24 @@
 import numpy as np
 from concourse.mybir import dt, AluOpType as A, ActivationFunctionType as F
 
-C, FAR, HALF = 320, 240, 160
+C, FAR = 320, 240
 MASKS = [4, 1, 2]
 HUGE = 2.0 ** 80
 UNIT = 2.0 ** 18
+PARTS = [(0, 128), (128, 256), (256, 320)]
+SENT = [(0, 128), (128, FAR)]
+FLAG_SLOT = [0, 0, 1, 9, 5, 2, 10, 6]
+DEPTH = [(0, 4, 2.0), (2, 4, -1.0), (1, 16, 2.0), (7, 8, 2.0), (9, 16, 1.0), (11, 16, 1.0)]
+
+CHAIN = [("ar", 1), ("ar", 2), ("ar", 3), ("br", 1), ("ar", 4), ("br", 2), ("ar", 5), ("br", 3), ("ar", 6), ("br", 4), ("u", 0), ("br", 5), ("br", 6)]
+FIRST = [("ar", k) for k in range(1, 7)] + [("br", 1), ("br", 2), ("br", 3), ("u", 0), ("br", 4), ("br", 5), ("br", 6)]
+M0, EDIT0, M = 5, 3, [1, 0, 2, 2, 5]
 
 f32, b16, i32, u16, q8, u8 = "float32", "bfloat16", "int32", "uint16", "float8_e4m3fn_x4", "uint8"
 SCRATCH = {
     "xa": ("sbuf", [128, 4 * C], b16), "xb": ("sbuf", [128, 4 * C], b16),
     "xh": ("sbuf", [128, 4 * C], b16), "zb": ("sbuf", [128, 4 * C], b16), "z": ("sbuf", [128, 4 * C], b16),
-    "h": ("sbuf", [128, 4 * C], b16), "j": ("sbuf", [128, 4 * C], b16),
+    "h": ("sbuf", [128, 4 * FAR], b16), "j": ("sbuf", [128, 4 * C], b16),
     "ut": ("sbuf", [128, 512], b16), "vt": ("sbuf", [128, 512], b16),
     "ones": ("sbuf", [128, 512], b16), "eb": ("sbuf", [128, 2048], b16),
     "qu": ("sbuf", [128, 128], q8), "pu": ("sbuf", [128, 128], u8),
@@ -19,46 +27,50 @@ SCRATCH = {
     "qe": ("sbuf", [128, 512], q8), "pe": ("sbuf", [128, 512], u8),
     "qw": ("sbuf", [128, 512], q8), "pw": ("sbuf", [128, 512], u8),
     "qx": ("sbuf", [128, C], q8), "px": ("sbuf", [128, C], u8),
-    "qz": ("sbuf", [128, C], q8), "pz": ("sbuf", [128, C], u8),
     "dli": ("sbuf", [128, 20], i32), "nli": ("sbuf", [128, 20], i32),
     "n_o": ("sbuf", [128, 20], u16), "f_o0": ("sbuf", [128, 20], u16),
-    "d_f0": ("sbuf", [128, 20], f32), "d_f1": ("sbuf", [128, 20], f32), "ddif": ("sbuf", [128, 20], f32),
     "a_o": ("sbuf", [128, 20], u16), "b_o": ("sbuf", [128, 20], u16), "l_o": ("sbuf", [128, 20], u16),
-    "ints": ("sbuf", [128, 120], i32),
-    "parf": ("sbuf", [128, 20], f32), "dnf": ("sbuf", [128, 20], f32),
-    "ta": ("sbuf", [128, 24], f32), "tb": ("sbuf", [128, 24], f32),
-    "pidx": ("sbuf", [128, 1], i32), "sli": ("sbuf", [128, 1], i32), "hfi": ("sbuf", [128, 1], i32),
+    "d3_o": ("sbuf", [128, 20], u16), "e3_o": ("sbuf", [128, 20], u16),
+    "flag_o": ("sbuf", [128, 10], u16), "place_o": ("sbuf", [128, 10], u16), "extra_o": ("sbuf", [128, 10], u16),
+    "ints": ("sbuf", [128, 60], i32), "odd": ("sbuf", [128, 20], f32),
+    "dif": ("sbuf", [128, 40], f32), "trade": ("sbuf", [128, 40], f32), "new": ("sbuf", [128, 40], f32),
+    "pidx": ("sbuf", [128, 1], i32), "bits": ("sbuf", [128, 4], i32),
     "rowi": ("sbuf", [128, 8], i32), "row_o": ("sbuf", [128, 8], u16),
-    "cst": ("sbuf", [128, 24], f32), "tv": ("sbuf", [128, 6], f32),
-    "iot": ("sbuf", [128, C], f32), "i512": ("sbuf", [128, C], f32), "cs": ("sbuf", [128, 672], f32),
-    "mask": ("sbuf", [128, C], f32), "seg": ("sbuf", [128, C], f32), "hold": ("sbuf", [128, C], f32),
-    "kt": ("sbuf", [128, 672], b16), "b0": ("sbuf", [128, C], f32),
-    "ts": ("sbuf", [128, C], f32), "bf": ("sbuf", [128, C], f32), "sbp": ("sbuf", [128, C], f32),
-    "tmt": ("sbuf", [128, C], f32), "tat": ("sbuf", [128, C], f32), "tbt": ("sbuf", [128, C], f32),
-    "wa": ("sbuf", [128, C], f32), "wb": ("sbuf", [128, C], f32), "m0": ("sbuf", [128, C], f32),
-    "einv": ("sbuf", [128, C], f32), "xm": ("sbuf", [128, C], f32), "xs": ("sbuf", [128, C], f32),
+    "cst": ("sbuf", [128, 24], f32), "tv": ("sbuf", [128, 3], f32), "c32": ("sbuf", [128, 10], f32),
+    "krow": ("sbuf", [128, 64], f32), "kcol": ("sbuf", [128, 64], f32),
+    "iot": ("sbuf", [128, C], f32), "i512": ("sbuf", [128, C], f32),
+    "wt": ("sbuf", [128, 160], f32), "alt": ("sbuf", [128, 160], b16),
+    "w0": ("sbuf", [128, C], f32), "w1": ("sbuf", [128, C], f32), "w2": ("sbuf", [128, C], f32),
+    "y1": ("sbuf", [128, C], f32), "y2": ("sbuf", [128, C], f32), "yo": ("sbuf", [128, C], f32), "oa": ("sbuf", [128, C], f32),
+    "ts": ("sbuf", [128, 352], f32), "pt": ("sbuf", [128, 352], f32),
+    "wp": ("sbuf", [128, C], f32), "yp": ("sbuf", [128, C], f32), "mb": ("sbuf", [128, C], f32),
+    "tat": ("sbuf", [128, C], f32), "tbt": ("sbuf", [128, C], f32),
+    "einv": ("sbuf", [128, C], f32), "urow": ("sbuf", [128, C], f32),
     "irow": ("sbuf", [128, 352], b16), "irow2": ("sbuf", [128, 352], b16), "prow": ("sbuf", [128, 352], f32),
     "tin": ("sbuf", [128, 672], b16), "tin2": ("sbuf", [128, 672], b16), "tp": ("sbuf", [128, 672], f32),
-    "sc": ("sbuf", [128, 672], f32), "sc2": ("sbuf", [128, 672], b16),
+    "pc": ("sbuf", [128, 160], f32), "xc": ("sbuf", [128, 160], f32), "fc": ("sbuf", [128, 160], b16),
+    "sc": ("sbuf", [128, 160], f32), "yc": ("sbuf", [128, 160], b16), "sy": ("sbuf", [128, 160], b16),
 }
 for _r in range(3):
-    SCRATCH["ss%d" % _r] = ("sbuf", [128, 20], f32)
-    SCRATCH["sl%d" % _r] = ("sbuf", [128, 20], f32)
+    SCRATCH["ss%d" % _r] = ("sbuf", [128, 80], f32)
+    SCRATCH["sl%d" % _r] = ("sbuf", [128, 80], f32)
     SCRATCH["el%d" % _r] = ("sbuf", [128, 20], u16)
     SCRATCH["f_o%d" % (_r + 1)] = ("sbuf", [128, 20], u16)
-    SCRATCH["qh%d" % _r] = ("sbuf", [128, C], q8)
-    SCRATCH["ph%d" % _r] = ("sbuf", [128, C], u8)
+    SCRATCH["qz%d" % _r] = ("sbuf", [128, 128], q8)
+    SCRATCH["pz%d" % _r] = ("sbuf", [128, 128], u8)
+    SCRATCH["qh%d" % _r] = ("sbuf", [128, 256], q8)
+    SCRATCH["ph%d" % _r] = ("sbuf", [128, 256], u8)
     SCRATCH["ql%d" % _r] = ("sbuf", [128, FAR], q8)
     SCRATCH["pl%d" % _r] = ("sbuf", [128, FAR], u8)
-for _c in "mr", "ar", "br", "yp":
+for _c in "ar", "br":
     SCRATCH[_c + "a"] = ("sbuf", [128, 3 * C], f32)
     SCRATCH[_c + "b"] = ("sbuf", [128, 3 * C], f32)
 for _i in range(8):
     SCRATCH["ps%d" % _i] = ("psum", [128, 512], f32)
 
-SEMAPHORES = ["sv", "sa", "st", "sg", "sent", "ldx", "ldu", "ldw", "ldv", "ldd", "ldn", "out", "ta", "tb", "tm"]
+SEMAPHORES = ["sv", "sa", "st", "sg", "sent", "ldx", "ldu", "ldw", "ldv", "ldd", "ldn", "out", "slots"]
 for _r in range(3):
-    SEMAPHORES += ["s%d" % _r, "e%d" % _r, "ca%d" % _r, "cb%d" % _r, "cp%d" % _r]
+    SEMAPHORES += ["s%d" % _r, "e%d" % _r, "c0%d" % _r, "c1%d" % _r, "p0%d" % _r, "p1%d" % _r]
 
 
 def rank_program(g, core, T, topo):
@@ -67,7 +79,7 @@ def rank_program(g, core, T, topo):
         return
     V, S, P, Y = g.vector, g.scalar, g.tensor, g.sync
     queue = {"v": V, "s": S, "p": P, "y": Y, "g": g}
-    cnt = {"sv": 0, "sa": 0, "st": 0, "sg": 0, "sent": 0, "ta": 0, "tb": 0, "tm": 0}
+    cnt = {"sv": 0, "sa": 0, "st": 0, "sg": 0, "sent": 0, "slots": 0}
     known = {}
 
     def need(q, sem, n):
@@ -106,186 +118,221 @@ def rank_program(g, core, T, topo):
     def landed(q, r, sem):
         need(q, "%s%d" % (sem, r), len(topo.engines(peer(r), core)))
 
-    def slot(sem, tile, i, src):
-        done(sem, Y.dma_start(tile[i:128:16, :], src), 16)
+    def slot(tile, i, row):
+        done("slots", Y.dma_start(tile[i:128:16, :], row[i:128:16, :]), 16)
 
-    def rows(name, k, i=None):
+    def rows(name, k):
         lo = C * (k // 2)
-        buf = T[name + "ab"[k % 2]]
-        return buf[:, lo:lo + C] if i is None else buf[i:128:16, lo:lo + C]
+        return T[name + "ab"[k % 2]][:, lo:lo + C]
 
-    Y.dma_start(T.xa[:], T.x[:]).then_inc(T.sem.ldx, 16)
-    S.dma_start(T.dli[:], T.dl[:]).then_inc(T.sem.ldd, 16)
-    S.dma_start(T.ut[:], T.u[:]).then_inc(T.sem.ldu, 16)
+    def turn(out, row):
+        v(V.transpose(out[:, 0:320], row[:, 16:336]))
+        return v(V.transpose(out[:, 320:672], row[:, 0:352]))
+
+    Y.dma_start(T.dli[:], T.dl[:]).then_inc(T.sem.ldd, 16)
+    S.dma_start(T.xa[:], T.x[:]).then_inc(T.sem.ldx, 16)
+    Y.dma_start(T.ut[:], T.u[:]).then_inc(T.sem.ldu, 16)
     S.dma_start(T.nli[:], T.nl[:]).then_inc(T.sem.ldn, 16)
-    Y.dma_start(T.qw[:].bitcast(dt.uint8), T.wc[:]).then_inc(T.sem.ldw, 16)
-    Y.dma_start(T.pw[:], T.ws[:]).then_inc(T.sem.ldw, 16)
-    Y.dma_start(T.vt[:], T.v[:]).then_inc(T.sem.ldv, 16)
 
+    g2 = gc(g.iota(T.iot[:], [[1, C]], 0, 0, allow_small_or_imprecise_dtypes=True))
     gc(g.iota(T.pidx[:], [[0, 1]], 0, 1))
     gc(g.iota(T.rowi[:], [[16, 8]], 0, 0))
-    g1 = gc(g.iota(T.tv[:], [[1, 6]], 1, 0, allow_small_or_imprecise_dtypes=True))
-    g2 = gc(g.iota(T.iot[:], [[1, C]], 0, 0, allow_small_or_imprecise_dtypes=True))
+    gc(g.iota(T.c32[:], [[32, 10]], 0, 0, allow_small_or_imprecise_dtypes=True))
+    g1 = gc(g.iota(T.tv[:], [[1, 3]], 0, 0, allow_small_or_imprecise_dtypes=True))
 
     def col(k):
         return T.cst[:, k:k + 1]
-    SLOT, M1, M0, LE6, S7 = range(5)
-    actp, bip = T.cst[:, 8:14], T.cst[:, 14:20]
+    T7, LOW, HALF8, HALF16, ODD, BASE, FB, PB, XB, W0 = range(10)
+    act, bias = T.cst[:, 12:15], T.cst[:, 16:19]
     v(V.memset(T.tat[:], 0.0))
-    ms = v(V.memset(T.tbt[:], 0.0))
-    need("v", "sg", g1)
-    v(V.tensor_scalar(T.sli[:], T.pidx[:], 15, None, A.bitwise_and))
-    v(V.tensor_scalar(T.hfi[:], T.pidx[:], 16, None, A.bitwise_and))
-    v(V.tensor_copy(T.row_o[:], T.rowi[:]))
+    v(V.memset(T.tbt[:], 0.0))
+    v(V.memset(T.krow[:], 0.0))
     vv()
-    v(V.tensor_copy(col(SLOT), T.sli[:]))
-    v(V.tensor_scalar(col(M1), T.hfi[:], 0.0625, None, A.mult))
-    vv()
-    sl = col(SLOT)
-    v(V.tensor_scalar(col(M0), col(M1), -1.0, 1.0, A.mult, A.add))
-    v(V.tensor_scalar(col(LE6), sl, 6.0, None, A.is_le))
-    v(V.tensor_scalar(col(S7), sl, -1.0, 7.0, A.mult, A.add))
-    vv()
-    v(V.tensor_scalar(actp, T.tv[:], col(S7), col(LE6), A.is_ge, A.mult))
-    vv()
-    v(V.tensor_scalar(bip, actp, -HUGE, HUGE, A.mult, A.add))
+    for first, step, depth in DEPTH:
+        v(V.memset(T.krow[:, first:32:step], depth))
+    for t in range(2, 8):
+        v(V.memset(T.krow[:, 32 + t:64:8], float(FLAG_SLOT[t])))
     need("v", "ldd", 16)
     vd = v(V.tensor_copy(T.f_o0[:], T.dli[:]))
-    v(V.tensor_copy(T.d_f0[:], T.dli[:]))
     need("g", "sv", vd)
     send(peer(0), T.el0[:], T.f_o0[:], "e0")
-    g3 = gc(g.iota(T.cs[:], [[0, 42], [1, 16]], 0, 0, allow_small_or_imprecise_dtypes=True))
+    g3 = gc(g.iota(T.wt[:], [[0, 20], [-1, 8]], 7, 0, allow_small_or_imprecise_dtypes=True))
     need("v", "sg", g2)
     vi = v(V.tensor_scalar(T.i512[:], T.iot[:], 512.0, None, A.mult))
-    v(V.memset(T.tmt[:], HUGE))
-    v(V.memset(T.b0[:], 0.0))
+    vv()
+    v(V.transpose(T.kcol[:], T.krow[:]))
+    need("v", "sg", g1)
+    v(V.tensor_copy(T.row_o[:], T.rowi[:]))
+    vv()
+    v(V.tensor_scalar(act, T.tv[:], T.kcol[:, 0:1], None, A.is_le))
     need("v", "ldu", 16)
     v(V.quantize_mx(T.qu[:], T.pu[:], T.ut[:]))
     vv()
+    v(V.tensor_scalar(bias, act, -HUGE, HUGE, A.mult, A.add))
+    v(V.tensor_scalar(col(W0), act[:, 2:3], -2 * HUGE, HUGE, A.mult, A.add))
     v(V.tensor_copy(T.qr[:].bitcast(dt.uint32), T.qu[:].bitcast(dt.uint32).indirect(T.row_o[:])))
     v(V.tensor_copy(T.pr[:], T.pu[:].indirect(T.row_o[:])))
-    need("v", "ldn", 16)
-    v(V.tensor_copy(T.n_o[:], T.nli[:]))
     need("y", "sg", g2)
     need("y", "sv", vi)
-    slot("ta", T.tat, 6, T.iot[6:128:16, :])
-    slot("tb", T.tbt, 0, T.i512[0:128:16, :])
+    slot(T.tat, 7, T.iot)
+    slot(T.tbt, 1, T.i512)
     need("v", "ldx", 16)
 
-    po_, ai_, bi_, ki_, k2_, par_ = [T.ints[:, 20 * k:20 * k + 20] for k in range(6)]
+    def late_constants():
+        v(V.memset(T.ts[:, 0:32], 0.0))
+        v(V.memset(T.pt[:], HUGE))
+        v(V.memset(T.prow[:], 0.0))
+        v(V.memset(T.irow[:], 0.0))
+        v(V.memset(T.irow2[:], 0.0))
+        v(V.memset(T.alt[:], -1.0))
+        v(V.memset(T.ones[:], 1.0))
+        v(V.tensor_scalar(T.bits[:, 0:1], T.pidx[:], 7, None, A.bitwise_and))
+        v(V.tensor_scalar(T.bits[:, 1:2], T.pidx[:], 3, 1, A.logical_shift_right, A.bitwise_and))
+        v(V.tensor_scalar(T.bits[:, 2:3], T.pidx[:], 4, 1, A.logical_shift_right, A.bitwise_and))
+        need("v", "ldn", 16)
+        v(V.tensor_copy(T.n_o[:], T.nli[:]))
+        need("v", "sg", g3)
+        v(V.tensor_scalar(T.wt[:], T.wt[:], UNIT, None, A.mult))
+        vv()
+        v(V.memset(T.alt[:, 0:160:8], 0.0))
+        v(V.tensor_tensor(col(ODD), T.bits[:, 1:2], T.bits[:, 2:3], A.not_equal))
+        v(V.tensor_scalar(col(HALF8), T.bits[:, 1:2], 16.0, None, A.mult))
+        v(V.tensor_copy(col(T7), T.bits[:, 0:1]))
+        vv()
+        v(V.tensor_scalar(col(BASE), col(ODD), 336.0, col(HALF8), A.mult, A.add))
+        vv()
+        v(V.tensor_scalar(T.flag_o[:], T.c32[:], col(BASE), T.kcol[:, 32:33], A.add, A.add))
+        v(V.tensor_scalar(T.place_o[:], T.c32[:], col(BASE), col(T7), A.add, A.add))
+        vv()
+        n = v(V.tensor_scalar(T.extra_o[:], T.place_o[:], 8.0, None, A.add))
+        need("g", "sv", n)
+        return [gc(g.affine_select(T.eb[:, 512 * b:512 * b + 512], T.ones[:], [[-1, 512]], A.is_equal, 0.0, b, 4)) for b in range(4)][-1]
+
+    po_, ai_, bi_ = [T.ints[:, 20 * k:20 * k + 20] for k in range(3)]
     X = [T.xa, T.xb, T.xa, T.xb]
     ps = [T["ps%d" % i] for i in range(8)]
+    last = {"ar": 0, "br": 0}
 
-    def scan_pick(src, out):
-        vv()
-        v(V.tensor_tensor_scan(T.xs[:], T.seg[:], src, 0.0, A.mult, A.add))
-        vv()
-        return v(V.tensor_copy(out, T.xs[:, 15:C:16]))
-
-    def to_offsets(sc, out):
-        vv()
-        v(V.tensor_scalar(T.ta[:, 0:21], sc[:, 6:672:32], col(M0), None, A.mult))
-        v(V.tensor_scalar(T.tb[:, 0:21], sc[:, 22:672:32], col(M1), None, A.mult))
-        vv()
-        v(V.tensor_tensor(T.ints[:, out:out + 20:2], T.ta[:, 0:10], T.tb[:, 10:20], A.add))
-        return v(V.tensor_tensor(T.ints[:, out + 1:out + 20:2], T.ta[:, 11:21], T.tb[:, 0:10], A.add))
-
-    def own_places(f_o, ks):
+    def places(name, lst, ks):
         for k in ks:
-            win = T.iot[:] if k == 1 else rows("ar", k - 2)
+            win = (T.iot[:] if name == "ar" else T.i512[:]) if k == 1 else rows(name, k - 2)
             if k > 1:
-                need("s", "sa", na_[0])
-            na_[0] = s(S.activation(rows("ar", k - 1), win.indirect(f_o[:]), F.Identity, bias=UNIT))
-            need("y", "sa", na_[0])
-            slot("ta", T.tat, 6 - k, rows("ar", k - 1, 6 - k))
-    na_ = [0]
+                need("s", "sa", last[name])
+            row = rows(name, k - 1)
+            last[name] = s(S.activation(row, win.indirect(lst[:]), F.Copy))
+            need("y", "sa", last[name])
+            if name == "ar":
+                slot(T.tat, 7 - k, row)
+                if k == 1:
+                    slot(T.tat, 8, row)
+                    slot(T.tbt, 9, row)
+                if k == 3:
+                    slot(T.tat, 10, row)
+            else:
+                slot(T.tbt, 1 + k, row)
+                if k == 3:
+                    slot(T.tat, 11, row)
 
-    def far_places(e_o, ks):
-        for k in ks:
-            win = T.i512[:] if k == 1 else rows("br", k - 2)
-            if k > 1:
-                need("s", "sa", nb_[0])
-            nb_[0] = s(S.activation(rows("br", k - 1), win.indirect(e_o[:]), F.Copy))
-            need("y", "sa", nb_[0])
-            slot("tb", T.tbt, k, rows("br", k - 1, k))
-    nb_ = [0]
+    def inverse(r):
+        landed("v", r, "e")
+        return v(V.tensor_copy(T.einv[:].indirect(T["el%d" % r][:]), T.iot[:]))
+
+    def inverse_at(r, n):
+        need("s", "sv", n)
+        n = s(S.activation(T.urow[:], T.einv[:].indirect(T["f_o%d" % r][:]), F.Copy))
+        need("y", "sa", n)
+        slot(T.tat, 12, T.urow)
+        slot(T.tbt, 13, T.urow)
 
     need("s", "sg", g2)
     need("s", "sv", vi)
-    own_places(T.f_o0, range(1, 7))
+    todo, inv = [(0, name, k) for name, k in FIRST], [0]
+
+    def more(n):
+        for r, name, k in todo[:n]:
+            if name == "ar":
+                places(name, T["f_o%d" % r], [k])
+            elif name == "br":
+                landed("s", r, "e")
+                places(name, T["el%d" % r], [k])
+            elif name == "u":
+                inverse_at(r, inv[0])
+            else:
+                n1 = s(S.activation(rows("ar", 0), T.iot[:].indirect(T.f_o3[:]), F.Copy))
+                need("y", "sa", n1)
+                Y.dma_start(T.dn[:], rows("ar", 0)[0:128:16, :]).then_inc(T.sem.out, 16)
+        del todo[:n]
+
+    more(M0)
 
     for r in range(3):
         x, xn = X[r], X[r + 1]
         d_o, e_o, f_o = T["f_o%d" % r], T["el%d" % r], T["f_o%d" % (r + 1)]
-        d_f, f_f = (T.d_f0, T.d_f1) if r % 2 == 0 else (T.d_f1, T.d_f0)
         vv()
         need("p", "sv", v(V.quantize_mx(T.qx[:], T.px[:], x[:])))
         t1 = p(P.matmul_mx(ps[0][:, 0:C], T.qr[:], T.pr[:], T.qx[:], T.px[:], True, True))
         t2 = p(P.matmul_mx(ps[1][:, 0:C], T.qr[:], T.pr[:], T.qx[:], T.px[:], True, True))
-        need("v", "st", t1)
-        v(V.transpose(T.ts[:], ps[0][:, 0:C]))
-        vv()
-        need("g", "sv", v(V.tensor_copy(T["ss%d" % r][:], T.ts[:, 0:C:16])))
-        send(peer(r), T["sl%d" % r][:], T["ss%d" % r][:], "s%d" % r)
         need("s", "st", t2)
-        v(V.tensor_copy(T.m0[:], ps[0][:, 0:C]))
-        n = s(S.activation(rows("mr", 0), ps[1][:, 0:C], F.Copy))
-        landed("s", r, "e")
-        far_places(e_o, range(1, 7) if r == 0 else range(3, 7))
-        need("y", "sa", n)
-        slot("tm", T.tmt, 6, rows("mr", 0, 6))
-        need("v", "sa", n)
-        for k in range(1, 6):
-            vv()
-            n = v(V.tensor_tensor(rows("mr", k), rows("mr", k - 1).indirect(d_o[:]), T.m0[:], A.min))
-            need("y", "sv", n)
-            slot("tm", T.tmt, 6 - k, rows("mr", k, 6 - k))
-        for k in range(4):
-            s(S.activation(T.xh[:, C * k:C * k + C], x[:, k:4 * C:4], F.Copy, scale=0.5))
+        y1 = s(S.activation(T.y1[:], ps[1][:, 0:C], F.Identity, bias=bias[:, 1:2], scale=act[:, 1:2]))
+        y2 = s(S.activation(T.y2[:], ps[1][:, 0:C], F.Identity, bias=bias[:, 0:1], scale=act[:, 0:1]))
+        need("v", "st", t1)
+        v(V.tensor_scalar(T.w0[:], ps[0][:, 0:C], col(W0), None, A.max))
+        vv()
+        need("v", "sa", y1)
+        v(V.tensor_tensor(T.w1[:], T.w0[:].indirect(d_o[:]), T.y1[:], A.min))
+        vv()
+        need("v", "sa", y2)
+        v(V.tensor_tensor(T.w2[:], T.w1[:].indirect(d_o[:]), T.y2[:], A.min))
+        vv()
+        v(V.transpose(T.ts[:, 32:352], T.w2[:]))
+        vv()
+        need("g", "sv", v(V.tensor_copy(T["ss%d" % r][:], T.ts[:, 35:352:4])))
+        send(peer(r), T["sl%d" % r][:], T["ss%d" % r][:], "s%d" % r)
         if r == 0:
-            v(V.memset(T.ones[:], 1.0))
-            need("g", "sv", cnt["sv"])
-            for b in range(4):
-                g4 = gc(g.affine_select(T.eb[:, 512 * b:512 * b + 512], T.ones[:], [[-1, 512]], A.is_equal, 0.0, b, 4))
-            need("v", "sg", g3)
-            v(V.tensor_scalar(T.hold[:], T.cs[:, 0:C], 2.0, None, A.is_ge))
-            v(V.memset(T.irow[:], 0.0))
-            v(V.memset(T.prow[:], 0.0))
-            vv()
-        landed("v", r, "e")
-        v(V.tensor_copy(T.einv[:].indirect(e_o[:]), T.iot[:]))
-        need("v", "ta", cnt["ta"])
-        need("v", "tb", cnt["tb"])
+            Y.dma_start(T.qw[:].bitcast(dt.uint8), T.wc[:]).then_inc(T.sem.ldw, 16)
+            Y.dma_start(T.pw[:], T.ws[:]).then_inc(T.sem.ldw, 16)
+            Y.dma_start(T.vt[:], T.v[:]).then_inc(T.sem.ldv, 16)
+            inv[0] = inverse(0)
+            g4 = late_constants()
+        more(len(todo))
+        for k in range(4):
+            xh = s(S.activation(T.xh[:, C * k:C * k + C], x[:, k:4 * C:4], F.Copy, scale=0.5))
+        v(V.transpose(T.yo[:], T.ts[:, 31:351]))
+        need("v", "slots", cnt["slots"])
         v(V.tensor_tensor(T.prow[:, 16:336], T.tbt[:].indirect(T.n_o[:]), T.tat[:], A.add))
         vv()
-        v(V.transpose(T.tp[:, 0:320], T.prow[:, 16:336]))
-        v(V.transpose(T.tp[:, 320:672], T.prow[:, 0:352]))
+        turn(T.tp, T.prow)
+        vv()
+        n1 = v(V.tensor_copy(T.xc[:], T.tp[:].indirect(T.extra_o[:])))
+        v(V.tensor_tensor(T.pc[:], T.tp[:].indirect(T.place_o[:]), T.wt[:], A.add))
+        vv(n1)
+        n1 = v(V.tensor_copy(T.d3_o[:], T.xc[:, 2:160:8]))
+        v(V.tensor_scalar(T.e3_o[:], T.xc[:, 3:160:8], 1.0 / 512, None, A.mult))
+        v(V.tensor_tensor(T.dif[:], T.xc[:, 1:160:4], T.xc[:, 0:160:4], A.subtract))
+        vv(n1)
+        v(V.tensor_tensor(T.oa[:], T.w2[:].indirect(T.d3_o[:]), T.yo[:], A.min))
+        sl = T["sl%d" % r]
         landed("v", r, "s")
-        v(V.tensor_copy(T.b0[:, 1:C:16], T["sl%d" % r][:]))
+        v(V.tensor_copy(T.pt[:, 2:320:4], sl[:]))
+        v(V.tensor_copy(T.pt[:, 3:320:8], sl[:, 1:80:2]))
+        v(V.tensor_copy(T.pt[:, 7:320:16], sl[:, 1:80:4]))
         vv()
-        v(V.tensor_tensor_scan(T.bf[:], T.hold[:], T.b0[:], 0.0, A.mult, A.add))
+        v(V.transpose(T.wp[:], T.pt[:, 0:320]))
+        v(V.transpose(T.yp[:], T.pt[:, 1:321]))
         vv()
-        n = v(V.transpose(T.sbp[:], T.bf[:]))
+        v(V.tensor_tensor(T.mb[:], T.wp[:].indirect(T.e3_o[:]), T.yp[:], A.min))
+        vv()
+        n = v(V.tensor_tensor(T.irow[:, 16:336], T.mb[:].indirect(T.n_o[:]), T.oa[:], A.is_lt))
         need("s", "sv", n)
-        ya = [s(S.activation(rows("yp", k), T.sbp[:], F.Identity, bias=bip[:, k:k + 1], scale=actp[:, k:k + 1])) for k in range(1, 6)]
+        ni = s(S.activation(T.irow2[:, 16:336], T.irow[:, 16:336].indirect(T.n_o[:]), F.Copy))
         vv()
-        v(V.tensor_scalar(rows("yp", 0), T.sbp[:], actp[:, 0:1], bip[:, 0:1], A.mult, A.add))
-        win = rows("yp", 0)
-        for k in range(1, 6):
-            need("v", "sa", ya[k - 1])
-            vv()
-            out = (T.wa if k % 2 else T.wb)[:]
-            v(V.tensor_tensor(out, win.indirect(e_o[:]), rows("yp", k), A.min))
-            win = out
-        need("v", "tm", cnt["tm"])
+        turn(T.tin, T.irow)
         vv()
-        v(V.tensor_tensor(T.irow[:, 16:336], win.indirect(T.n_o[:]), T.tmt[:], A.is_lt))
+        v(V.tensor_copy(T.fc[:], T.tin[:].indirect(T.flag_o[:])))
         vv()
-        v(V.transpose(T.tin[:, 0:320], T.irow[:, 16:336]))
-        nir = v(V.transpose(T.tin[:, 320:672], T.irow[:, 0:352]))
+        v(V.tensor_tensor_scan(T.sc[:], T.fc[:], T.pc[:], 0.0, A.mult, A.max))
         vv()
-        v(V.tensor_tensor_scan(T.sc[:], T.tin[:], T.tp[:], 0.0, A.mult, A.max))
-        to_offsets(T.sc, 0)
+        v(V.tensor_copy(po_, T.sc[:, 7:160:8]))
         vv()
         n1 = v(V.tensor_scalar(bi_, po_, 9, 511, A.logical_shift_right, A.bitwise_and))
         n2 = v(V.tensor_scalar(ai_, po_, 511, None, A.bitwise_and))
@@ -293,95 +340,95 @@ def rank_program(g, core, T, topo):
         nb = v(V.tensor_copy(T.b_o[:], bi_))
         vv(n2)
         na = v(V.tensor_copy(T.a_o[:], ai_))
+
+        def far_side(h):
+            lo, hi = PARTS[h]
+            return [s(S.activation(T.zb[:, C * k + lo:C * k + hi], T.xh[:, C * k:C * k + C].indirect(T.b_o[:, lo // 16:hi // 16]), F.Copy)) for k in range(4)]
+
+        def means(h, zb, banks, between):
+            lo, hi = PARTS[h]
+            for k in range(4):
+                need("v", "sa", zb[k])
+                vv(na)
+                v(V.tensor_tensor(T.z[:, 4 * lo + k:4 * hi:4], T.xh[:, C * k:C * k + C].indirect(T.a_o[:, lo // 16:hi // 16]), T.zb[:, C * k + lo:C * k + hi], A.add))
+                between()
+            vv()
+            qz, pz = T["qz%d" % h], T["pz%d" % h]
+            need("p", "sv", v(V.quantize_mx(qz[:], pz[:], T.z[:, 4 * hi - 512:4 * hi])))
+            return [p(P.matmul_mx(banks[b][:, 0:128], T.qw[:, 128 * b:128 * b + 128], T.pw[:, 128 * b:128 * b + 128], qz[:], pz[:], True, True)) for b in range(4)]
+
+        def layer(h, tz, banks, q, bs):
+            lo, hi = SENT[h]
+            for b in bs:
+                need(q, "st", tz[b])
+                out, in_ = T.h[:, 4 * lo + b:4 * hi:4], banks[b][:, 0:hi - lo]
+                n = s(S.activation(out, in_, F.Copy, scale=0.03125)) if q == "s" else v(V.tensor_scalar(out, in_, 0.03125, None, A.mult))
+            return n
+
+        def codes(h):
+            lo, hi = SENT[h]
+            qh, ph, end = T["qh%d" % r], T["ph%d" % r], 128 * h + 128
+            need("g", "sv", v(V.quantize_mx(qh[:, end - 128:end], ph[:, end - 128:end], T.h[:, 4 * hi - 512:4 * hi])))
+            send(peer(r), T["ql%d" % r][:, lo:hi].bitcast(dt.uint8), qh[:, end - (hi - lo):end].bitcast(dt.uint8), "c%d%d" % (h, r))
+            send(peer(r), T["pl%d" % r][:, lo:hi], ph[:, end - (hi - lo):end], "p%d%d" % (h, r))
+
+        edit = [
+            lambda: [turn(T.tin2, T.irow2)],
+            lambda: [v(V.tensor_tensor(T.yc[:], T.tin2[:].indirect(T.flag_o[:]), T.fc[:], A.subtract))],
+            lambda: [v(V.tensor_tensor_scan(T.sy[:], T.alt[:], T.yc[:], 0.0, A.mult, A.add))],
+            lambda: [v(V.tensor_tensor(T.odd[:], T.sy[:, 7:160:8], T.sy[:, 7:160:8], A.mult))],
+            lambda: [v(V.tensor_tensor(T.trade[:, k:40:2], T.odd[:], T.dif[:, k:40:2], A.mult)) for k in range(2)],
+            lambda: [v(V.tensor_tensor(T.new[:], T.trade[:], T.xc[:, 0:160:4], A.add))],
+            lambda: [v(V.tensor_copy(out[:], T.new[:, k:40:2])) for k, out in enumerate([f_o, T.l_o])],
+        ]
+        state = [0]
+
+        def edit_step():
+            if edit:
+                vv(state[0])
+                state[0] = edit.pop(0)()[-1]
+
+        need("s", "sa", xh)
         need("s", "sv", nb)
-        za = [[s(S.activation(T.zb[:, C * k + HALF * h:C * k + HALF * h + HALF], T.xh[:, C * k:C * k + C].indirect(T.b_o[:, 10 * h:10 * h + 10]), F.Copy)) for k in range(4)] for h in range(2)]
-        tz = []
+        zb0, zb1 = far_side(0), far_side(1)
+        need("v", "sa", ni)
+        for _ in range(EDIT0):
+            edit_step()
         if r == 0:
             need("p", "ldw", 32)
-        for h in range(2):
-            for k in range(4):
-                need("v", "sa", za[h][k])
-                vv(na)
-                v(V.tensor_tensor(T.z[:, 4 * HALF * h + k:4 * HALF * h + 4 * HALF:4], T.xh[:, C * k:C * k + C].indirect(T.a_o[:, 10 * h:10 * h + 10]), T.zb[:, C * k + HALF * h:C * k + HALF * h + HALF], A.add))
-            vv()
-            lo, hi = HALF * h, HALF * h + HALF
-            need("p", "sv", v(V.quantize_mx(T.qz[:, lo:hi], T.pz[:, lo:hi], T.z[:, 4 * lo:4 * hi])))
-            tz.append([p(P.matmul_mx(ps[4 * h + b][:, 0:HALF], T.qw[:, 128 * b:128 * b + 128], T.pw[:, 128 * b:128 * b + 128], T.qz[:, lo:hi], T.pz[:, lo:hi], True, True)) for b in range(4)])
-        qh, ph = T["qh%d" % r], T["ph%d" % r]
-        for b in range(4):
-            need("s", "st", tz[0][b])
-            ha = s(S.activation(T.h[:, b:4 * HALF:4], ps[b][:, 0:HALF], F.Copy, scale=0.03125))
-        for b in range(2):
-            need("s", "st", tz[1][b])
-            hb = s(S.activation(T.h[:, 4 * HALF + b:4 * C:4], ps[4 + b][:, 0:HALF], F.Copy, scale=0.03125))
-        need("v", "sa", ha)
-        n1 = v(V.quantize_mx(qh[:, 0:HALF], ph[:, 0:HALF], T.h[:, 0:4 * HALF]))
-        for b in range(2, 4):
-            need("v", "st", tz[1][b])
-            vb = v(V.tensor_scalar(T.h[:, 4 * HALF + b:4 * C:4], ps[4 + b][:, 0:HALF], 0.03125, None, A.mult))
-        need("v", "sa", hb)
-        vv()
-        n2 = v(V.quantize_mx(qh[:, HALF:C], ph[:, HALF:C], T.h[:, 4 * HALF:4 * C]))
-        need("g", "sv", n1)
-        send(peer(r), T["ql%d" % r][:, 0:HALF].bitcast(dt.uint8), qh[:, 0:HALF].bitcast(dt.uint8), "ca%d" % r)
-        need("g", "sv", n2)
-        send(peer(r), T["ql%d" % r][:, HALF:FAR].bitcast(dt.uint8), qh[:, HALF:FAR].bitcast(dt.uint8), "cb%d" % r)
-        send(peer(r), T["pl%d" % r][:, 0:FAR], ph[:, 0:FAR], "cp%d" % r)
-        if r == 0:
-            v(V.memset(T.irow2[:], 0.0))
-            vv()
-            need("s", "sv", cnt["sv"])
-        ni = s(S.activation(T.irow2[:, 16:336], T.irow[:, 16:336].indirect(T.n_o[:]), F.Copy))
-        for b in range(4):
-            if b == 2:
-                need("s", "sv", vb)
-            s(S.activation(T.j[:, C * b + FAR:C * b + C], ps[4 + b][:, FAR - HALF:HALF], F.Copy, scale=0.03125))
-        v(V.tensor_scalar(ki_, po_, 18, None, A.logical_shift_right))
-        if r == 0:
-            v(V.tensor_scalar(T.mask[:], T.cs[:, 0:C], sl, None, A.is_equal))
-            v(V.tensor_scalar(T.seg[:], T.cs[:, 0:C], 1.0, None, A.is_ge))
-            v(V.tensor_scalar(T.kt[:], T.cs[:], -1.0, 6.0, A.mult, A.add))
-            vv()
-            v(V.tensor_tensor(T.xm[:], rows("ar", 0).indirect(T.n_o[:]), T.mask[:], A.mult))
-            scan_pick(T.xm[:], T.parf[:])
-            vv()
-            v(V.tensor_scalar(T.dnf[:], T.parf[:], UNIT, None, A.subtract))
-            vv()
-            v(V.tensor_tensor(T.ddif[:], T.dnf[:], d_f[:], A.subtract))
-        need("v", "sa", ni)
-        v(V.transpose(T.tin2[:, 0:320], T.irow2[:, 16:336]))
-        v(V.transpose(T.tin2[:, 320:672], T.irow2[:, 0:352]))
-        vv()
-        v(V.tensor_tensor_scan(T.sc2[:], T.tin2[:], T.kt[:], 0.0, A.mult, A.max))
-        to_offsets(T.sc2, 80)
-        vv()
-        v(V.tensor_tensor(par_, ki_, k2_, A.add))
-        vv()
-        v(V.tensor_scalar(par_, par_, 1, None, A.bitwise_and))
-        vv()
-        v(V.tensor_copy(T.parf[:], par_))
-        vv()
-        v(V.tensor_tensor(T.parf[:], T.parf[:], T.ddif[:], A.mult))
-        vv()
-        v(V.tensor_tensor(f_f[:], d_f[:], T.parf[:], A.add))
-        vv()
-        nf = v(V.tensor_copy(f_o[:], f_f[:]))
+        tz0 = means(0, zb0, ps[0:4], edit_step)
+        while edit:
+            edit_step()
+        nl = state[0]
+        nf = nl - 1
         if r < 2:
             need("g", "sv", nf)
             send(peer(r + 1), T["el%d" % (r + 1)][:], f_o[:], "e%d" % (r + 1))
-        vv()
-        v(V.tensor_tensor(T.xm[:], T.einv[:].indirect(f_o[:]), T.mask[:], A.mult))
-        nl = scan_pick(T.xm[:], T.l_o[:])
-        need("s", "sv", nf)
-        if r < 2:
-            own_places(f_o, range(1, 5))
-            v(V.tensor_scalar(T.dnf[:], T.parf[:], -2.0, None, A.mult))
-            vv()
-            v(V.tensor_tensor(T.ddif[:], T.ddif[:], T.dnf[:], A.add))
+            todo[:] = [(r + 1, name, k) for name, k in CHAIN]
         else:
-            n = s(S.activation(rows("ar", 0), T.iot[:].indirect(f_o[:]), F.Copy))
-            need("y", "sa", n)
-            Y.dma_start(T.dn[:], rows("ar", 0, 0)).then_inc(T.sem.out, 16)
+            todo[:] = [(3, "dn", 0)]
+        zb2 = far_side(2)
+        need("s", "sv", nf)
+        more(M[0])
+        ha = layer(0, tz0, ps[0:4], "s", range(4))
+        more(M[1])
+        tz1 = means(1, zb1, ps[4:8], edit_step)
+        need("v", "sa", ha)
+        codes(0)
+        hb = layer(1, tz1, ps[4:8], "s", [0, 1])
+        vb = layer(1, tz1, ps[4:8], "v", [2, 3])
+        need("v", "sa", hb)
+        vv()
+        codes(1)
+        more(M[2])
+        need("p", "sa", ha)
+        tz2 = means(2, zb2, ps[0:4], edit_step)
+        if r < 2:
+            inv[0] = inverse(r + 1)
+        for b in range(4):
+            need("s", "st", tz2[b])
+            s(S.activation(T.j[:, C * b + FAR:C * b + C], ps[b][:, 128 - (C - FAR):128], F.Copy, scale=0.03125))
+        more(M[3])
         if r == 0:
             need("v", "sg", g4)
             v(V.quantize_mx(T.qe[:], T.pe[:], T.eb[:]))
@@ -389,21 +436,19 @@ def rank_program(g, core, T, topo):
         if r == 1:
             need("v", "ldv", 16)
             v(V.quantize_mx(T.qv[:], T.pv[:], T.vt[:]))
-        need("p", "sa", ha)
+        need("p", "sa", hb)
         need("p", "sv", vb)
-        for k in ("ca", "cb", "cp"):
+        for k in ("c0", "p0", "c1", "p1"):
             landed("p", r, k)
         for b in range(4):
-            td = p(P.matmul_mx(ps[b][:, 0:FAR], T.qe[:, 128 * b:128 * b + 128], T.pe[:, 128 * b:128 * b + 128], T["ql%d" % r][:], T["pl%d" % r][:], True, True))
+            td = p(P.matmul_mx(ps[4 + b][:, 0:FAR], T.qe[:, 128 * b:128 * b + 128], T.pe[:, 128 * b:128 * b + 128], T["ql%d" % r][:], T["pl%d" % r][:], True, True))
             need("s", "st", td)
-            ja = s(S.activation(T.j[:, C * b:C * b + FAR], ps[b][:, 0:FAR], F.Copy))
+            ja = s(S.activation(T.j[:, C * b:C * b + FAR], ps[4 + b][:, 0:FAR], F.Copy))
             need("v", "sa", ja)
             vv(nl)
             v(V.tensor_tensor(xn[:, b:4 * C:4], T.j[:, C * b:C * b + C].indirect(T.l_o[:]), x[:, b:4 * C:4], A.add))
-        if r < 2:
-            own_places(f_o, range(5, 7))
-            landed("s", r + 1, "e")
-            far_places(T["el%d" % (r + 1)], range(1, 3))
+        need("p", "sa", ja)
+        more(M[4])
 
     vv()
     n = v(V.quantize_mx(T.qx[:], T.px[:], X[3][:]))
@@ -415,9 +460,9 @@ def rank_program(g, core, T, topo):
     for k in range(4):
         (S if k % 2 else Y).dma_start(T.osc[4 * k:4 * k + 4, :], T.px[32 * k:32 * k + 4, :]).then_inc(T.sem.out, 16)
     need("v", "st", t)
-    n = v(V.tensor_copy(T.ts[:], ps[0][:, 0:C]))
+    n = v(V.tensor_copy(T.w0[:], ps[0][:, 0:C]))
     need("y", "sv", n)
-    Y.dma_start(T.y[:], T.ts[:]).then_inc(T.sem.out, 16)
+    Y.dma_start(T.y[:], T.w0[:]).then_inc(T.sem.out, 16)
     g.wait_ge(T.sem.out, 16 * 7)
-    for k in ("sv", "sa", "st", "sg", "sent", "ta", "tb", "tm"):
+    for k in ("sv", "sa", "st", "sg", "sent", "slots"):
         need("g", k, cnt[k])

@@ -1,18 +1,19 @@
 import numpy as np
 from concourse.mybir import dt, AluOpType as A, ActivationFunctionType as F
 
-C, FAR = 320, 240
+C, FAR, MID = 320, 240, 160
 MASKS = [4, 1, 2]
 HUGE = 2.0 ** 80
-UNIT = 2.0 ** 18
 PARTS = [(0, 128), (128, 256), (256, 320)]
 SENT = [(0, 128), (128, FAR)]
-FLAG_SLOT = [0, 0, 1, 9, 5, 2, 10, 6]
-DEPTH = [(0, 4, 2.0), (2, 4, -1.0), (1, 16, 2.0), (7, 8, 2.0), (9, 16, 1.0), (11, 16, 1.0)]
-
-CHAIN = [("ar", 1), ("ar", 2), ("ar", 3), ("br", 1), ("ar", 4), ("br", 2), ("ar", 5), ("br", 3), ("ar", 6), ("br", 4), ("u", 0), ("br", 5), ("br", 6)]
-FIRST = [("ar", k) for k in range(1, 7)] + [("br", 1), ("br", 2), ("br", 3), ("u", 0), ("br", 4), ("br", 5), ("br", 6)]
-M0, EDIT0, M = 5, 3, [1, 0, 2, 2, 5]
+HALVES = [(0, 192), (192, C)]
+OWN_SLOT, FAR_SLOT = [4, 8, 12, 1, 5, 9, 13], [2, 6, 10, 14, 3, 7, 11]
+FIRST = ["a1", "a2", "a3", "e1", "e2", "e3", "a4", "dn", "e4", "u"]
+CHAIN = ["a1", "a2", "a3", "e1", "e2", "e3", "a4", "e4", "u"]
+M0, M1, M = 3, 3, [0, 1, 3, 1, 1, 3, 0]
+SPLIT = [(0, MID), (MID, C)]
+ORDER0 = "mommcpcpcppppp"
+W1 = [3, 5, 5]
 
 f32, b16, i32, u16, q8, u8 = "float32", "bfloat16", "int32", "uint16", "float8_e4m3fn_x4", "uint8"
 SCRATCH = {
@@ -27,50 +28,48 @@ SCRATCH = {
     "qe": ("sbuf", [128, 512], q8), "pe": ("sbuf", [128, 512], u8),
     "qw": ("sbuf", [128, 512], q8), "pw": ("sbuf", [128, 512], u8),
     "qx": ("sbuf", [128, C], q8), "px": ("sbuf", [128, C], u8),
+    "qz": ("sbuf", [128, 384], q8), "pz": ("sbuf", [128, 384], u8),
     "dli": ("sbuf", [128, 20], i32), "nli": ("sbuf", [128, 20], i32),
     "n_o": ("sbuf", [128, 20], u16), "f_o0": ("sbuf", [128, 20], u16),
     "a_o": ("sbuf", [128, 20], u16), "b_o": ("sbuf", [128, 20], u16), "l_o": ("sbuf", [128, 20], u16),
-    "d3_o": ("sbuf", [128, 20], u16), "e3_o": ("sbuf", [128, 20], u16),
-    "flag_o": ("sbuf", [128, 10], u16), "place_o": ("sbuf", [128, 10], u16), "extra_o": ("sbuf", [128, 10], u16),
-    "ints": ("sbuf", [128, 60], i32), "odd": ("sbuf", [128, 20], f32),
-    "dif": ("sbuf", [128, 40], f32), "trade": ("sbuf", [128, 40], f32), "new": ("sbuf", [128, 40], f32),
-    "pidx": ("sbuf", [128, 1], i32), "bits": ("sbuf", [128, 4], i32),
+    "flag_o": ("sbuf", [128, 10], u16), "own_o": ("sbuf", [128, 14], u16), "far_o": ("sbuf", [128, 10], u16), "one_o": ("sbuf", [128, 2], u16),
+    "odd": ("sbuf", [128, 20], f32), "sign": ("sbuf", [128, 20], f32),
+    "old": ("sbuf", [128, 40], f32), "dif": ("sbuf", [128, 40], f32), "trade": ("sbuf", [128, 40], f32), "new": ("sbuf", [128, 40], f32),
     "rowi": ("sbuf", [128, 8], i32), "row_o": ("sbuf", [128, 8], u16),
-    "cst": ("sbuf", [128, 24], f32), "tv": ("sbuf", [128, 3], f32), "c32": ("sbuf", [128, 10], f32),
-    "krow": ("sbuf", [128, 64], f32), "kcol": ("sbuf", [128, 64], f32),
-    "iot": ("sbuf", [128, C], f32), "i512": ("sbuf", [128, C], f32),
-    "wt": ("sbuf", [128, 160], f32), "alt": ("sbuf", [128, 160], b16),
+    "cst": ("sbuf", [128, 12], f32), "tv": ("sbuf", [128, 44], f32),
+    "krow": ("sbuf", [128, 320], f32), "kcol": ("sbuf", [128, 320], f32),
+    "iot": ("sbuf", [128, C], b16), "wt": ("sbuf", [128, 208], f32), "alt": ("sbuf", [128, 160], b16),
     "w0": ("sbuf", [128, C], f32), "w1": ("sbuf", [128, C], f32), "w2": ("sbuf", [128, C], f32),
     "y1": ("sbuf", [128, C], f32), "y2": ("sbuf", [128, C], f32), "yo": ("sbuf", [128, C], f32), "oa": ("sbuf", [128, C], f32),
-    "ts": ("sbuf", [128, 352], f32), "pt": ("sbuf", [128, 352], f32),
+    "ts": ("sbuf", [128, C], f32), "pt": ("sbuf", [128, 352], f32),
     "wp": ("sbuf", [128, C], f32), "yp": ("sbuf", [128, C], f32), "mb": ("sbuf", [128, C], f32),
-    "tat": ("sbuf", [128, C], f32), "tbt": ("sbuf", [128, C], f32),
-    "einv": ("sbuf", [128, C], f32), "urow": ("sbuf", [128, C], f32),
-    "irow": ("sbuf", [128, 352], b16), "irow2": ("sbuf", [128, 352], b16), "prow": ("sbuf", [128, 352], f32),
-    "tin": ("sbuf", [128, 672], b16), "tin2": ("sbuf", [128, 672], b16), "tp": ("sbuf", [128, 672], f32),
-    "pc": ("sbuf", [128, 160], f32), "xc": ("sbuf", [128, 160], f32), "fc": ("sbuf", [128, 160], b16),
-    "sc": ("sbuf", [128, 160], f32), "yc": ("sbuf", [128, 160], b16), "sy": ("sbuf", [128, 160], b16),
+    "tat": ("sbuf", [128, C], b16), "tbt": ("sbuf", [128, C], b16), "a456": ("sbuf", [128, C], b16), "e456": ("sbuf", [128, C], b16),
+    "r1": ("sbuf", [128, 2 * C], b16), "r2": ("sbuf", [128, 2 * C], b16), "e3": ("sbuf", [128, C], b16), "a3": ("sbuf", [128, 352], b16),
+    "einv": ("sbuf", [128, C], b16), "urow": ("sbuf", [128, C], b16),
+    "irow": ("sbuf", [128, 352], b16), "irow2": ("sbuf", [128, 352], b16), "prow": ("sbuf", [128, 352], b16),
+    "tin": ("sbuf", [128, 704], b16), "tin2": ("sbuf", [128, 704], b16), "tp": ("sbuf", [128, 672], b16), "t3": ("sbuf", [128, 672], b16),
+    "qa": ("sbuf", [128, 216], f32), "qb": ("sbuf", [128, 168], f32), "da": ("sbuf", [128, 160], f32), "db": ("sbuf", [128, 160], f32),
+    "fc": ("sbuf", [128, 160], b16), "sa": ("sbuf", [128, 160], f32), "sb": ("sbuf", [128, 160], f32),
+    "yc": ("sbuf", [128, 160], b16), "sy": ("sbuf", [128, 160], b16),
 }
 for _r in range(3):
     SCRATCH["ss%d" % _r] = ("sbuf", [128, 80], f32)
     SCRATCH["sl%d" % _r] = ("sbuf", [128, 80], f32)
     SCRATCH["el%d" % _r] = ("sbuf", [128, 20], u16)
+    SCRATCH["e3l%d" % _r] = ("sbuf", [128, 20], u16)
+    SCRATCH["d3_o%d" % _r] = ("sbuf", [128, 32], u16)
     SCRATCH["f_o%d" % (_r + 1)] = ("sbuf", [128, 20], u16)
-    SCRATCH["qz%d" % _r] = ("sbuf", [128, 128], q8)
-    SCRATCH["pz%d" % _r] = ("sbuf", [128, 128], u8)
     SCRATCH["qh%d" % _r] = ("sbuf", [128, 256], q8)
     SCRATCH["ph%d" % _r] = ("sbuf", [128, 256], u8)
     SCRATCH["ql%d" % _r] = ("sbuf", [128, FAR], q8)
     SCRATCH["pl%d" % _r] = ("sbuf", [128, FAR], u8)
-for _c in "ar", "br":
-    SCRATCH[_c + "a"] = ("sbuf", [128, 3 * C], f32)
-    SCRATCH[_c + "b"] = ("sbuf", [128, 3 * C], f32)
 for _i in range(8):
     SCRATCH["ps%d" % _i] = ("psum", [128, 512], f32)
 
-SEMAPHORES = ["sv", "sa", "st", "sg", "sent", "ldx", "ldu", "ldw", "ldv", "ldd", "ldn", "out", "slots"]
+COUNTED = ["sv", "sa", "st", "sg", "sent", "ta", "tb", "shift", "out"]
+SEMAPHORES = COUNTED + ["ldx", "ldu", "ldw", "ldv", "ldd", "ldn"]
 for _r in range(3):
-    SEMAPHORES += ["s%d" % _r, "e%d" % _r, "c0%d" % _r, "c1%d" % _r, "p0%d" % _r, "p1%d" % _r]
+    SEMAPHORES += ["s%d" % _r, "e%d" % _r, "t%d" % _r, "c0%d" % _r, "c1%d" % _r, "p0%d" % _r, "p1%d" % _r]
 
 
 def rank_program(g, core, T, topo):
@@ -79,18 +78,24 @@ def rank_program(g, core, T, topo):
         return
     V, S, P, Y = g.vector, g.scalar, g.tensor, g.sync
     queue = {"v": V, "s": S, "p": P, "y": Y, "g": g}
-    cnt = {"sv": 0, "sa": 0, "st": 0, "sg": 0, "sent": 0, "slots": 0}
+    cnt = {k: 0 for k in COUNTED}
     known = {}
 
-    def need(q, sem, n):
+    def need(q, sem, n=None):
+        n = cnt[sem] if n is None else n
         if known.get((q, sem), 0) < n:
             queue[q].wait_ge(T.sem[sem], n)
             known[(q, sem)] = n
 
+    def after(q, *calls):
+        for call in calls:
+            if call:
+                need(q, *call)
+
     def done(sem, ins, k=1):
         ins.then_inc(T.sem[sem], k)
         cnt[sem] += k
-        return cnt[sem]
+        return sem, cnt[sem]
 
     def v(ins):
         return done("sv", ins)
@@ -104,8 +109,21 @@ def rank_program(g, core, T, topo):
     def gc(ins):
         return done("sg", ins)
 
-    def vv(n=None):
-        need("v", "sv", cnt["sv"] if n is None else n)
+    aside = []
+
+    def step(n=1):
+        for _ in range(min(n, len(aside))):
+            aside.pop(0)()
+
+    def chain(*calls):
+        last = [None]
+
+        def link(call):
+            def run():
+                after("v", last[0])
+                last[0] = call() or last[0]
+            return run
+        return [link(call) for call in calls]
 
     def peer(r):
         return T.cores[rank ^ MASKS[r]]
@@ -118,249 +136,362 @@ def rank_program(g, core, T, topo):
     def landed(q, r, sem):
         need(q, "%s%d" % (sem, r), len(topo.engines(peer(r), core)))
 
-    def slot(tile, i, row):
-        done("slots", Y.dma_start(tile[i:128:16, :], row[i:128:16, :]), 16)
-
-    def rows(name, k):
-        lo = C * (k // 2)
-        return T[name + "ab"[k % 2]][:, lo:lo + C]
+    def slot(sem, tile, i, row, k=None, step=16):
+        done(sem, Y.dma_start(tile[i:128:step, :], row[(i if k is None else k):128:step, :]), 16)
 
     def turn(out, row):
         v(V.transpose(out[:, 0:320], row[:, 16:336]))
         return v(V.transpose(out[:, 320:672], row[:, 0:352]))
 
+    def turn_part(out, row, h):
+        lo, hi, at = ((0, 128, 0), (128, C, 288))[h]
+        v(V.transpose(out[:, at:at + hi - lo], row[:, 16 + lo:16 + hi]))
+        return v(V.transpose(out[:, at + hi - lo:at + 2 * (hi - lo) + 32], row[:, lo:hi + 32]))
+
     Y.dma_start(T.dli[:], T.dl[:]).then_inc(T.sem.ldd, 16)
-    S.dma_start(T.xa[:], T.x[:]).then_inc(T.sem.ldx, 16)
     Y.dma_start(T.ut[:], T.u[:]).then_inc(T.sem.ldu, 16)
+    S.dma_start(T.xa[:], T.x[:]).then_inc(T.sem.ldx, 16)
     S.dma_start(T.nli[:], T.nl[:]).then_inc(T.sem.ldn, 16)
+    S.dma_start(T.qw[:].bitcast(dt.uint8), T.wc[:]).then_inc(T.sem.ldw, 16)
+    S.dma_start(T.pw[:], T.ws[:]).then_inc(T.sem.ldw, 16)
 
-    g2 = gc(g.iota(T.iot[:], [[1, C]], 0, 0, allow_small_or_imprecise_dtypes=True))
-    gc(g.iota(T.pidx[:], [[0, 1]], 0, 1))
+    def count(out, pattern, base):
+        return gc(g.iota(out, pattern, base, 0, allow_small_or_imprecise_dtypes=True))
+
+    def table(k, first=0, step=1, last=32):
+        return T.krow[:, 32 * k + first:32 * k + last:step]
+
+    def turned(k):
+        return T.kcol[:, 32 * k:32 * k + 1]
+
+    def halves(k, inner, even, odd, base=0):
+        count(table(k, 0, 1, 16), [inner[0], [even + odd, 2]] + inner[1:], base)
+        return count(table(k, 16), [inner[0], [even - odd, 2]] + inner[1:], base + odd)
+    DEPTH, AT1, AT2, AT8, ATA, ATB, FLAG, OWN, OTHER, SLOT = range(10)
+    g2 = count(T.iot[:], [[1, C]], -MID)
     gc(g.iota(T.rowi[:], [[16, 8]], 0, 0))
-    gc(g.iota(T.c32[:], [[32, 10]], 0, 0, allow_small_or_imprecise_dtypes=True))
-    g1 = gc(g.iota(T.tv[:], [[1, 3]], 0, 0, allow_small_or_imprecise_dtypes=True))
+    count(table(DEPTH, 1, 4), [[0, 2], [-1, 2], [-2, 2]], 2)
+    count(table(DEPTH, 3, 4), [[0, 2], [1, 2], [2, 2]], 0)
+    halves(AT1, [[32, 8]], 16, 336)
+    count(T.tv[:, 0:3], [[1, 3]], 0)
+    g1 = count(T.tv[:, 4:6], [[256, 2]], 0)
 
-    def col(k):
-        return T.cst[:, k:k + 1]
-    T7, LOW, HALF8, HALF16, ODD, BASE, FB, PB, XB, W0 = range(10)
-    act, bias = T.cst[:, 12:15], T.cst[:, 16:19]
+    act, bias, floor = T.cst[:, 0:3], T.cst[:, 4:7], T.cst[:, 8:9]
+    v(V.memset(table(DEPTH, 0, 4), 2.0))
+    v(V.memset(table(DEPTH, 2, 4), -1.0))
     v(V.memset(T.tat[:], 0.0))
-    v(V.memset(T.tbt[:], 0.0))
-    v(V.memset(T.krow[:], 0.0))
-    vv()
-    for first, step, depth in DEPTH:
-        v(V.memset(T.krow[:, first:32:step], depth))
-    for t in range(2, 8):
-        v(V.memset(T.krow[:, 32 + t:64:8], float(FLAG_SLOT[t])))
+    n0 = v(V.memset(T.tbt[:], 0.0))
+    for pad in T.a3, T.irow2, T.prow, T.irow:
+        v(V.memset(pad[:], 0.0))
+    v(V.memset(T.pt[:], HUGE))
+    ones = v(V.memset(T.ones[:], 1.0))
+    after("s", g2)
+    for out, lo, hi, fill in (T.wt, 0, 160, 0.0), (T.wt, 160, 208, MID), (T.qa, 0, 8, 0.0), (T.qb, 0, 8, 0.0), (T.alt, 0, 160, -1.0):
+        n = s(S.activation(out[:, lo:hi], T.iot[:, lo:hi], F.Identity, scale=0.0, bias=float(fill)))
+    yo = s(S.activation(T.yo[:], T.iot[:], F.Copy))
+    after("s", n)
+    s(S.activation(T.alt[:, 0:160:8], T.iot[:, 0:20], F.Copy, scale=0.0))
     need("v", "ldd", 16)
     vd = v(V.tensor_copy(T.f_o0[:], T.dli[:]))
-    need("g", "sv", vd)
+    after("g", vd)
     send(peer(0), T.el0[:], T.f_o0[:], "e0")
-    g3 = gc(g.iota(T.wt[:], [[0, 20], [-1, 8]], 7, 0, allow_small_or_imprecise_dtypes=True))
-    need("v", "sg", g2)
-    vi = v(V.tensor_scalar(T.i512[:], T.iot[:], 512.0, None, A.mult))
-    vv()
-    v(V.transpose(T.kcol[:], T.krow[:]))
-    need("v", "sg", g1)
+    after("v", g1, n0)
     v(V.tensor_copy(T.row_o[:], T.rowi[:]))
-    vv()
-    v(V.tensor_scalar(act, T.tv[:], T.kcol[:, 0:1], None, A.is_le))
+    n1 = v(V.transpose(T.kcol[:, 0:64], T.krow[:, 0:64]))
     need("v", "ldu", 16)
-    v(V.quantize_mx(T.qu[:], T.pu[:], T.ut[:]))
-    vv()
-    v(V.tensor_scalar(bias, act, -HUGE, HUGE, A.mult, A.add))
-    v(V.tensor_scalar(col(W0), act[:, 2:3], -2 * HUGE, HUGE, A.mult, A.add))
+    n2 = v(V.quantize_mx(T.qu[:], T.pu[:], T.ut[:]))
+    after("v", n1)
+    n1 = v(V.tensor_scalar(act, T.tv[:, 0:3], turned(DEPTH), None, A.is_le))
+    v(V.tensor_scalar(T.one_o[:], T.tv[:, 4:6], turned(AT1), 671.0, A.add, A.min))
+    after("v", n2)
     v(V.tensor_copy(T.qr[:].bitcast(dt.uint32), T.qu[:].bitcast(dt.uint32).indirect(T.row_o[:])))
     v(V.tensor_copy(T.pr[:], T.pu[:].indirect(T.row_o[:])))
-    need("y", "sg", g2)
-    need("y", "sv", vi)
-    slot(T.tat, 7, T.iot)
-    slot(T.tbt, 1, T.i512)
+    after("v", n1)
+    v(V.tensor_scalar(bias, act, -HUGE, HUGE, A.mult, A.add))
+    masks = v(V.tensor_scalar(floor, act[:, 2:3], -2 * HUGE, HUGE, A.mult, A.add))
+    after("y", n0, yo)
+    slot("ta", T.tat, OWN_SLOT[0], T.iot)
+    slot("tb", T.tbt, FAR_SLOT[0], T.iot)
     need("v", "ldx", 16)
+    for first, stride, base in (0, 2, 0), (1, 9, 1), (2, -3, 9), (3, 9, 5):
+        count(table(FLAG, first, 4), [[0, 4], [stride, 2]], base)
+    halves(ATA, [[0, 1], [0, 8]], 16, 144)
+    halves(ATB, [[0, 1], [0, 8]], 16, 208, 160)
 
-    def late_constants():
-        v(V.memset(T.ts[:, 0:32], 0.0))
-        v(V.memset(T.pt[:], HUGE))
-        v(V.memset(T.prow[:], 0.0))
-        v(V.memset(T.irow[:], 0.0))
-        v(V.memset(T.irow2[:], 0.0))
-        v(V.memset(T.alt[:], -1.0))
-        v(V.memset(T.ones[:], 1.0))
-        v(V.tensor_scalar(T.bits[:, 0:1], T.pidx[:], 7, None, A.bitwise_and))
-        v(V.tensor_scalar(T.bits[:, 1:2], T.pidx[:], 3, 1, A.logical_shift_right, A.bitwise_and))
-        v(V.tensor_scalar(T.bits[:, 2:3], T.pidx[:], 4, 1, A.logical_shift_right, A.bitwise_and))
-        need("v", "ldn", 16)
-        v(V.tensor_copy(T.n_o[:], T.nli[:]))
-        need("v", "sg", g3)
-        v(V.tensor_scalar(T.wt[:], T.wt[:], UNIT, None, A.mult))
-        vv()
-        v(V.memset(T.alt[:, 0:160:8], 0.0))
-        v(V.tensor_tensor(col(ODD), T.bits[:, 1:2], T.bits[:, 2:3], A.not_equal))
-        v(V.tensor_scalar(col(HALF8), T.bits[:, 1:2], 16.0, None, A.mult))
-        v(V.tensor_copy(col(T7), T.bits[:, 0:1]))
-        vv()
-        v(V.tensor_scalar(col(BASE), col(ODD), 336.0, col(HALF8), A.mult, A.add))
-        vv()
-        v(V.tensor_scalar(T.flag_o[:], T.c32[:], col(BASE), T.kcol[:, 32:33], A.add, A.add))
-        v(V.tensor_scalar(T.place_o[:], T.c32[:], col(BASE), col(T7), A.add, A.add))
-        vv()
-        n = v(V.tensor_scalar(T.extra_o[:], T.place_o[:], 8.0, None, A.add))
-        need("g", "sv", n)
-        return [gc(g.affine_select(T.eb[:, 512 * b:512 * b + 512], T.ones[:], [[-1, 512]], A.is_equal, 0.0, b, 4)) for b in range(4)][-1]
+    def more_tables():
+        halves(AT8, [[0, 1], [0, 8]], 16, 336)
+        halves(AT2, [[32, 4], [15, 2]], 16, 336)
 
-    po_, ai_, bi_ = [T.ints[:, 20 * k:20 * k + 20] for k in range(3)]
+    def late_tables():
+        count(table(OWN), [[0, 4], [-1, 2], [-4, 4]], 13)
+        count(table(OTHER), [[0, 4], [1, 2], [4, 4]], 2)
+        count(T.tv[:, 8:18], [[32, 10]], 0)
+        count(T.tv[:, 20:24], [[128, 4]], 0)
+        count(table(SLOT), [[0, 2], [-1, 16]], 0)
+        return count(T.tv[:, 24:44], [[-16, 20]], 0)
+
+    def late_constants(g3):
+        def last():
+            after("v", g3)
+            v(V.memset(table(OWN, 7, 8), float(OWN_SLOT[0])))
+            return v(V.memset(table(OTHER, 7, 8), float(OWN_SLOT[0])))
+
+        def lists():
+            v(V.tensor_scalar(T.wt[:, 7:160:8], T.tv[:, 24:44], turned(SLOT), None, A.add))
+            for base, k, out, lo, hi in (ATA, FLAG, T.flag_o, 0, 4), (ATB, FLAG, T.flag_o, 4, 10), (AT8, OWN, T.own_o, 0, 10), (AT8, OTHER, T.far_o, 0, 10):
+                v(V.tensor_scalar(out[:, lo:hi], T.tv[:, 8 + lo:8 + hi], turned(base), turned(k), A.add, A.add))
+            at["lists"] = v(V.tensor_scalar(T.own_o[:, 10:14], T.tv[:, 20:24], turned(AT2), 671.0, A.add, A.min))
+        return chain(last, lambda: v(V.transpose(T.kcol[:, 64:320], T.krow[:, 64:320])), lists)
+
     X = [T.xa, T.xb, T.xa, T.xb]
     ps = [T["ps%d" % i] for i in range(8)]
-    last = {"ar": 0, "br": 0}
+    at = {}
+    todo = [(0, name) for name in FIRST]
+    own_rows = [T.iot[:], T.r1[:, 0:C], T.r2[:, 0:C], T.a3[:, 16:336]]
+    far_rows = [T.iot[:], T.r1[:, C:2 * C], T.r2[:, C:2 * C], T.e3[:]]
 
-    def places(name, lst, ks):
-        for k in ks:
-            win = (T.iot[:] if name == "ar" else T.i512[:]) if k == 1 else rows(name, k - 2)
-            if k > 1:
-                need("s", "sa", last[name])
-            row = rows(name, k - 1)
-            last[name] = s(S.activation(row, win.indirect(lst[:]), F.Copy))
-            need("y", "sa", last[name])
-            if name == "ar":
-                slot(T.tat, 7 - k, row)
-                if k == 1:
-                    slot(T.tat, 8, row)
-                    slot(T.tbt, 9, row)
-                if k == 3:
-                    slot(T.tat, 10, row)
+    def more(n):
+        for r, name in todo[:n]:
+            d_o, e_o = T["f_o%d" % r], T["el%d" % min(r, 2)]
+            k = int(name[1]) if name[1:].isdigit() else 0
+            if name[0] == "e":
+                landed("s", r, "e" if k < 4 else "t")
+            if 1 < k < 4:
+                after("s", at[name[0] + str(k - 1)])
+            if name in ("a1", "a2", "a3"):
+                at[name] = s(S.activation(own_rows[k], own_rows[k - 1].indirect(d_o[:]), F.Copy))
+                need("y", "sa")
+                slot("ta", T.tat, OWN_SLOT[k], own_rows[k])
+            elif name in ("e1", "e2", "e3"):
+                at[name] = s(S.activation(far_rows[k], far_rows[k - 1].indirect(e_o[:]), F.Copy))
+                need("y", "sa")
+                slot("tb", T.tbt, FAR_SLOT[k], far_rows[k])
+            elif name == "a4":
+                need("s", "ta")
+                after("s", at["d3"])
+                s(S.activation(T.a456[:], T.tat[:].indirect(T["d3_o%d" % r][:, 0:20]), F.Copy))
+                need("y", "sa")
+                for k in 1, 2, 3:
+                    slot("ta", T.tat, OWN_SLOT[k + 3], T.a456, OWN_SLOT[k])
+            elif name == "e4":
+                need("s", "tb")
+                s(S.activation(T.e456[:], T.tbt[:].indirect(T["e3l%d" % r][:]), F.Copy))
+                need("y", "sa")
+                for k in 1, 2, 3:
+                    slot("tb", T.tbt, FAR_SLOT[k + 3], T.e456, FAR_SLOT[k])
+            elif name == "u":
+                after("s", at["inv"])
+                s(S.activation(T.urow[:], T.einv[:].indirect(d_o[:]), F.Copy))
+                need("y", "sa")
+                slot("tb", T.tbt, 15, T.urow)
+                slot("ta", T.tat, 0, T.urow)
+            elif name == "dn":
+                after("s", at["n"])
+                at["dn"] = s(S.activation(T.irow2[:, 16:336], own_rows[1].indirect(T.n_o[:]), F.Copy))
             else:
-                slot(T.tbt, 1 + k, row)
-                if k == 3:
-                    slot(T.tat, 11, row)
+                s(S.activation(T.y1[:], T.iot[:].indirect(d_o[:]), F.Identity, bias=float(MID)))
+                need("y", "sa")
+                done("out", Y.dma_start(T.dn[:], T.y1[0:128:16, :]), 16)
+        del todo[:n]
+
+    def halve(x):
+        for k in range(4):
+            at["xh"] = s(S.activation(T.xh[:, C * k:C * k + C], x[:, k:4 * C:4], F.Copy, scale=0.5))
+
+    def third_power(r):
+        def first():
+            after("v", at["a3"])
+            return turn(T.t3, T.a3)
+
+        def second():
+            at["d3"] = v(V.tensor_scalar(T["d3_o%d" % r][:], T.t3[:].indirect(T.one_o[:]), float(MID), None, A.add))
+            after("g", at["d3"])
+            send(peer(r), T["e3l%d" % r][:], T["d3_o%d" % r][:, 0:20], "t%d" % r)
+        return chain(first, second)
 
     def inverse(r):
         landed("v", r, "e")
-        return v(V.tensor_copy(T.einv[:].indirect(T["el%d" % r][:]), T.iot[:]))
+        at["inv"] = v(V.tensor_copy(T.einv[:].indirect(T["el%d" % r][:]), T.iot[:]))
 
-    def inverse_at(r, n):
-        need("s", "sv", n)
-        n = s(S.activation(T.urow[:], T.einv[:].indirect(T["f_o%d" % r][:]), F.Copy))
-        need("y", "sa", n)
-        slot(T.tat, 12, T.urow)
-        slot(T.tbt, 13, T.urow)
+    def turn_places():
+        def join():
+            need("v", "ta")
+            need("v", "tb")
+            return v(V.tensor_tensor(T.prow[:, 16:336], T.tbt[:].indirect(T.n_o[:]), T.tat[:], A.add))
 
-    need("s", "sg", g2)
-    need("s", "sv", vi)
-    todo, inv = [(0, name, k) for name, k in FIRST], [0]
+        def far():
+            after("v", at["lists"])
+            at["qb"] = v(V.tensor_tensor(T.qb[:, 8:168], T.tp[:].indirect(T.far_o[:]), T.wt[:, 0:160], A.add))
 
-    def more(n):
-        for r, name, k in todo[:n]:
-            if name == "ar":
-                places(name, T["f_o%d" % r], [k])
-            elif name == "br":
-                landed("s", r, "e")
-                places(name, T["el%d" % r], [k])
-            elif name == "u":
-                inverse_at(r, inv[0])
-            else:
-                n1 = s(S.activation(rows("ar", 0), T.iot[:].indirect(T.f_o3[:]), F.Copy))
-                need("y", "sa", n1)
-                Y.dma_start(T.dn[:], rows("ar", 0)[0:128:16, :]).then_inc(T.sem.out, 16)
-        del todo[:n]
+        def own():
+            at["qa"] = v(V.tensor_tensor(T.qa[:, 8:216], T.tp[:].indirect(T.own_o[:, 0:13]), T.wt[:], A.add))
 
+        def far_steps():
+            after("v", at["qb"])
+            at["db"] = v(V.tensor_tensor(T.db[:], T.qb[:, 7:167], T.qb[:, 8:168], A.subtract))
+
+        def own_steps():
+            after("v", at["qa"])
+            at["da"] = v(V.tensor_tensor(T.da[:], T.qa[:, 7:167], T.qa[:, 8:168], A.subtract))
+
+        def mates():
+            v(V.tensor_tensor(T.dif[:, 1:40:2], T.qa[:, 169:208:2], T.qa[:, 168:208:2], A.subtract))
+            v(V.tensor_copy(T.old[:, 1:40:2], T.qa[:, 168:208:2]))
+        return chain(join, lambda: turn(T.tp, T.prow), far, own, far_steps, own_steps, mates)
+
+    def quantise(x, lo, hi, r):
+        n = v(V.quantize_mx(T.qx[:, lo:hi], T.px[:, lo:hi], x[:, 4 * lo:4 * hi]))
+        after("p", n)
+        last = hi == C
+        if r < 3:
+            bank = ps[1 if last else 4][:, 0:hi - lo]
+            t = p(P.matmul_mx(bank, T.qr[:], T.pr[:], T.qx[:, lo:hi], T.px[:, lo:hi], True, True))
+            if last:
+                at["t1"] = p(P.matmul_mx(ps[0][:, 0:hi - lo], T.qr[:], T.pr[:], T.qx[:, lo:hi], T.px[:, lo:hi], True, True))
+            after("s", t, masks)
+            if not last:
+                s(S.activation(T.w0[:, lo:hi], bank, F.Identity, bias=bias[:, 2:3], scale=act[:, 2:3]))
+            at["y1"] = s(S.activation(T.y1[:, lo:hi], bank, F.Identity, bias=bias[:, 1:2], scale=act[:, 1:2]))
+            at["y2"] = s(S.activation(T.y2[:, lo:hi], bank, F.Identity, bias=bias[:, 0:1], scale=act[:, 0:1]))
+            return
+        bank = ps[0 if last else 4][:, 0:hi - lo]
+        t = p(P.matmul_mx(bank, T.qv[:], T.pv[:], T.qx[:, lo:hi], T.px[:, lo:hi], True, True))
+        after("y", n)
+        done("out", Y.dma_start(T.oc[:, 4 * lo:4 * hi], T.qx[:, lo:hi].bitcast(dt.uint8)), 16)
+        if last:
+            after("s", n)
+            for k in range(4):
+                done("out", (S if k % 2 else Y).dma_start(T.osc[4 * k:4 * k + 4, :], T.px[32 * k:32 * k + 4, :]), 16)
+            after("v", t)
+            after("y", v(V.tensor_copy(T.w0[:, lo:hi], bank)))
+            done("out", Y.dma_start(T.y[:, lo:hi], T.w0[:, lo:hi]), 16)
+        else:
+            after("s", t)
+            after("s", s(S.activation(T.w0[:, lo:hi], bank, F.Copy)))
+            done("out", S.dma_start(T.y[:, lo:hi], T.w0[:, lo:hi]), 16)
+
+    after("s", vd)
     more(M0)
 
     for r in range(3):
         x, xn = X[r], X[r + 1]
-        d_o, e_o, f_o = T["f_o%d" % r], T["el%d" % r], T["f_o%d" % (r + 1)]
-        vv()
-        need("p", "sv", v(V.quantize_mx(T.qx[:], T.px[:], x[:])))
-        t1 = p(P.matmul_mx(ps[0][:, 0:C], T.qr[:], T.pr[:], T.qx[:], T.px[:], True, True))
-        t2 = p(P.matmul_mx(ps[1][:, 0:C], T.qr[:], T.pr[:], T.qx[:], T.px[:], True, True))
-        need("s", "st", t2)
-        y1 = s(S.activation(T.y1[:], ps[1][:, 0:C], F.Identity, bias=bias[:, 1:2], scale=act[:, 1:2]))
-        y2 = s(S.activation(T.y2[:], ps[1][:, 0:C], F.Identity, bias=bias[:, 0:1], scale=act[:, 0:1]))
-        need("v", "st", t1)
-        v(V.tensor_scalar(T.w0[:], ps[0][:, 0:C], col(W0), None, A.max))
-        vv()
-        need("v", "sa", y1)
-        v(V.tensor_tensor(T.w1[:], T.w0[:].indirect(d_o[:]), T.y1[:], A.min))
-        vv()
-        need("v", "sa", y2)
-        v(V.tensor_tensor(T.w2[:], T.w1[:].indirect(d_o[:]), T.y2[:], A.min))
-        vv()
-        v(V.transpose(T.ts[:, 32:352], T.w2[:]))
-        vv()
-        need("g", "sv", v(V.tensor_copy(T["ss%d" % r][:], T.ts[:, 35:352:4])))
-        send(peer(r), T["sl%d" % r][:], T["ss%d" % r][:], "s%d" % r)
+        d_o, f_o = T["f_o%d" % r], T["f_o%d" % (r + 1)]
         if r == 0:
-            Y.dma_start(T.qw[:].bitcast(dt.uint8), T.wc[:]).then_inc(T.sem.ldw, 16)
-            Y.dma_start(T.pw[:], T.ws[:]).then_inc(T.sem.ldw, 16)
+            for lo, hi in HALVES:
+                quantise(x, lo, hi, 0)
+            need("v", "ldn", 16)
+            at["n"] = v(V.tensor_copy(T.n_o[:], T.nli[:]))
+            v(V.tensor_copy(T.old[:, 0:40:2], T.dli[:]))
+            aside.extend(third_power(0))
+        else:
+            more(len(todo))
+            halve(x)
+            aside.extend(turn_places())
+        lo, hi = HALVES[-1]
+        after("v", at["t1"], masks)
+        n = v(V.tensor_scalar(T.w0[:, lo:hi], ps[0][:, 0:hi - lo], floor, None, A.max))
+        step(r == 0)
+        after("v", n, at["y1"])
+        n = v(V.tensor_tensor(T.w1[:], T.w0[:].indirect(d_o[:]), T.y1[:], A.min))
+        if r == 0:
+            step()
+            more_tables()
+            more(M1)
+        after("v", n, at["y2"])
+        n = [v(V.tensor_tensor(T.w2[:, lo:hi], T.w1[:].indirect(d_o[:, lo // 16:hi // 16]), T.y2[:, lo:hi], A.min)) for lo, hi in SPLIT]
+        after("y", n[-1])
+        for k in range(2):
+            slot("shift", T.yo, k + 1, T.w2, k, 4)
+        for h, (lo, hi) in enumerate(SPLIT):
+            after("v", n[h])
+            n[h] = v(V.transpose(T.ts[:, lo:hi], T.w2[:, lo:hi]))
+        for h, (lo, hi) in enumerate(SPLIT):
+            after("v", n[h])
+            n[h] = v(V.tensor_copy(T["ss%d" % r][:, lo // 4:hi // 4], T.ts[:, lo + 3:hi:4]))
+        after("g", n[-1])
+        send(peer(r), T["sl%d" % r][:], T["ss%d" % r][:], "s%d" % r)
+
+        def own_minima():
+            need("v", "shift")
+            at["oa"] = v(V.tensor_tensor(T.oa[:], T.w2[:].indirect(T["d3_o%d" % r][:, 0:20]), T.yo[:], A.min))
+
+        if r == 1:
             Y.dma_start(T.vt[:], T.v[:]).then_inc(T.sem.ldv, 16)
-            inv[0] = inverse(0)
-            g4 = late_constants()
-        more(len(todo))
-        for k in range(4):
-            xh = s(S.activation(T.xh[:, C * k:C * k + C], x[:, k:4 * C:4], F.Copy, scale=0.5))
-        v(V.transpose(T.yo[:], T.ts[:, 31:351]))
-        need("v", "slots", cnt["slots"])
-        v(V.tensor_tensor(T.prow[:, 16:336], T.tbt[:].indirect(T.n_o[:]), T.tat[:], A.add))
-        vv()
-        turn(T.tp, T.prow)
-        vv()
-        n1 = v(V.tensor_copy(T.xc[:], T.tp[:].indirect(T.extra_o[:])))
-        v(V.tensor_tensor(T.pc[:], T.tp[:].indirect(T.place_o[:]), T.wt[:], A.add))
-        vv(n1)
-        n1 = v(V.tensor_copy(T.d3_o[:], T.xc[:, 2:160:8]))
-        v(V.tensor_scalar(T.e3_o[:], T.xc[:, 3:160:8], 1.0 / 512, None, A.mult))
-        v(V.tensor_tensor(T.dif[:], T.xc[:, 1:160:4], T.xc[:, 0:160:4], A.subtract))
-        vv(n1)
-        v(V.tensor_tensor(T.oa[:], T.w2[:].indirect(T.d3_o[:]), T.yo[:], A.min))
+        if r == 0:
+            g3 = late_tables()
+            after("g", ones)
+            g4 = [gc(g.affine_select(T.eb[:, 512 * b:512 * b + 512], T.ones[:], [[-1, 512]], A.is_equal, 0.0, b, 4)) for b in range(4)][-1]
+            inverse(0)
+            more(len(todo))
+            after("v", at["dn"])
+            mate = chain(lambda: turn(T.t3, T.irow2),
+                         lambda: v(V.tensor_scalar(T.new[:, 0:32], T.t3[:].indirect(T.one_o[:]), float(MID), None, A.add)),
+                         lambda: v(V.tensor_tensor(T.dif[:, 0:40:2], T.new[:, 0:20], T.old[:, 0:40:2], A.subtract)))
+            calls = {"m": mate, "o": [own_minima], "c": late_constants(g3), "p": turn_places()}
+            aside.extend([calls[k].pop(0) for k in ORDER0])
+        else:
+            aside.insert(2, own_minima)
+        step(W1[r])
         sl = T["sl%d" % r]
+        landed("s", r, "s")
         landed("v", r, "s")
-        v(V.tensor_copy(T.pt[:, 2:320:4], sl[:]))
-        v(V.tensor_copy(T.pt[:, 3:320:8], sl[:, 1:80:2]))
-        v(V.tensor_copy(T.pt[:, 7:320:16], sl[:, 1:80:4]))
-        vv()
+        after("s", at.get("pt"))
+        n1 = v(V.tensor_copy(T.pt[:, 2:320:4], sl[:]))
+        s(S.activation(T.pt[:, 3:320:8], sl[:, 1:80:2], F.Copy))
+        n2 = s(S.activation(T.pt[:, 7:320:16], sl[:, 1:80:4], F.Copy))
+        step()
+        after("v", n1, n2)
         v(V.transpose(T.wp[:], T.pt[:, 0:320]))
-        v(V.transpose(T.yp[:], T.pt[:, 1:321]))
-        vv()
-        v(V.tensor_tensor(T.mb[:], T.wp[:].indirect(T.e3_o[:]), T.yp[:], A.min))
-        vv()
-        n = v(V.tensor_tensor(T.irow[:, 16:336], T.mb[:].indirect(T.n_o[:]), T.oa[:], A.is_lt))
-        need("s", "sv", n)
+        at["pt"] = v(V.transpose(T.yp[:], T.pt[:, 1:321]))
+        if r == 0:
+            halve(x)
+        step()
+        after("v", at["pt"])
+        landed("v", r, "t")
+        n = v(V.tensor_tensor(T.mb[:], T.wp[:].indirect(T["e3l%d" % r][:]), T.yp[:], A.min))
+        step()
+        after("v", n, at["oa"])
+        flags = [v(V.tensor_tensor(T.irow[:, 16 + lo:16 + hi], T.mb[:].indirect(T.n_o[:, lo // 16:hi // 16]), T.oa[:, lo:hi], A.is_lt)) for lo, hi in ((0, MID), (MID, C))]
+        after("s", flags[1])
         ni = s(S.activation(T.irow2[:, 16:336], T.irow[:, 16:336].indirect(T.n_o[:]), F.Copy))
-        vv()
-        turn(T.tin, T.irow)
-        vv()
-        v(V.tensor_copy(T.fc[:], T.tin[:].indirect(T.flag_o[:])))
-        vv()
-        v(V.tensor_tensor_scan(T.sc[:], T.fc[:], T.pc[:], 0.0, A.mult, A.max))
-        vv()
-        v(V.tensor_copy(po_, T.sc[:, 7:160:8]))
-        vv()
-        n1 = v(V.tensor_scalar(bi_, po_, 9, 511, A.logical_shift_right, A.bitwise_and))
-        n2 = v(V.tensor_scalar(ai_, po_, 511, None, A.bitwise_and))
-        vv(n1)
-        nb = v(V.tensor_copy(T.b_o[:], bi_))
-        vv(n2)
-        na = v(V.tensor_copy(T.a_o[:], ai_))
+        turns, picks, scans, ends = [], [], [], []
+        for h in range(2):
+            after("v", flags[h])
+            turns.append(turn_part(T.tin, T.irow, h))
+        step(len(aside))
+        for h, (lo, hi) in enumerate(((0, 64), (64, 160))):
+            after("v", turns[h], at["lists"])
+            picks.append(v(V.tensor_copy(T.fc[:, lo:hi], T.tin[:, 0:(288, 704)[h]].indirect(T.flag_o[:, lo // 16:hi // 16]))))
+        for h, (lo, hi) in enumerate(((0, 64), (64, 160))):
+            after("v", picks[h], at["da"], at["db"])
+            scans.append([v(V.tensor_tensor_scan(out[:, lo:hi], d[:, lo:hi], T.fc[:, lo:hi], 0.0, A.add, A.mult)) for out, d in ((T.sb, T.db), (T.sa, T.da))])
+        for h, (lo, hi) in enumerate(((0, 64), (64, 160))):
+            ends.append([])
+            for k, (out, sc) in enumerate(((T.b_o, T.sb), (T.a_o, T.sa))):
+                after("v", scans[h][k])
+                ends[h].append(v(V.tensor_copy(out[:, lo // 8:hi // 8], sc[:, lo + 7:hi:8])))
 
         def far_side(h):
             lo, hi = PARTS[h]
+            after("s", ends[min(h, 1)][0])
             return [s(S.activation(T.zb[:, C * k + lo:C * k + hi], T.xh[:, C * k:C * k + C].indirect(T.b_o[:, lo // 16:hi // 16]), F.Copy)) for k in range(4)]
 
-        def means(h, zb, banks, between):
+        def mean(h, k):
             lo, hi = PARTS[h]
-            for k in range(4):
-                need("v", "sa", zb[k])
-                vv(na)
-                v(V.tensor_tensor(T.z[:, 4 * lo + k:4 * hi:4], T.xh[:, C * k:C * k + C].indirect(T.a_o[:, lo // 16:hi // 16]), T.zb[:, C * k + lo:C * k + hi], A.add))
-                between()
-            vv()
-            qz, pz = T["qz%d" % h], T["pz%d" % h]
-            need("p", "sv", v(V.quantize_mx(qz[:], pz[:], T.z[:, 4 * hi - 512:4 * hi])))
-            return [p(P.matmul_mx(banks[b][:, 0:128], T.qw[:, 128 * b:128 * b + 128], T.pw[:, 128 * b:128 * b + 128], qz[:], pz[:], True, True)) for b in range(4)]
+            after("v", zb[h][k], ends[min(h, 1)][1])
+            at["z%d" % h] = v(V.tensor_tensor(T.z[:, 4 * lo + k:4 * hi:4], T.xh[:, C * k:C * k + C].indirect(T.a_o[:, lo // 16:hi // 16]), T.zb[:, C * k + lo:C * k + hi], A.add))
+
+        def products(h, banks):
+            lo, hi = PARTS[h]
+            qz, pz = T.qz[:, 128 * h:128 * h + 128], T.pz[:, 128 * h:128 * h + 128]
+            after("v", at["z%d" % h])
+            after("p", v(V.quantize_mx(qz, pz, T.z[:, 4 * hi - 512:4 * hi])))
+            return [p(P.matmul_mx(banks[b][:, 0:128], T.qw[:, 128 * b:128 * b + 128], T.pw[:, 128 * b:128 * b + 128], qz, pz, True, True)) for b in range(4)]
 
         def layer(h, tz, banks, q, bs):
             lo, hi = SENT[h]
             for b in bs:
-                need(q, "st", tz[b])
+                after(q, tz[b])
                 out, in_ = T.h[:, 4 * lo + b:4 * hi:4], banks[b][:, 0:hi - lo]
                 n = s(S.activation(out, in_, F.Copy, scale=0.03125)) if q == "s" else v(V.tensor_scalar(out, in_, 0.03125, None, A.mult))
             return n
@@ -368,101 +499,109 @@ def rank_program(g, core, T, topo):
         def codes(h):
             lo, hi = SENT[h]
             qh, ph, end = T["qh%d" % r], T["ph%d" % r], 128 * h + 128
-            need("g", "sv", v(V.quantize_mx(qh[:, end - 128:end], ph[:, end - 128:end], T.h[:, 4 * hi - 512:4 * hi])))
+            after("g", v(V.quantize_mx(qh[:, end - 128:end], ph[:, end - 128:end], T.h[:, 4 * hi - 512:4 * hi])))
             send(peer(r), T["ql%d" % r][:, lo:hi].bitcast(dt.uint8), qh[:, end - (hi - lo):end].bitcast(dt.uint8), "c%d%d" % (h, r))
             send(peer(r), T["pl%d" % r][:, lo:hi], ph[:, end - (hi - lo):end], "p%d%d" % (h, r))
 
-        edit = [
-            lambda: [turn(T.tin2, T.irow2)],
-            lambda: [v(V.tensor_tensor(T.yc[:], T.tin2[:].indirect(T.flag_o[:]), T.fc[:], A.subtract))],
-            lambda: [v(V.tensor_tensor_scan(T.sy[:], T.alt[:], T.yc[:], 0.0, A.mult, A.add))],
-            lambda: [v(V.tensor_tensor(T.odd[:], T.sy[:, 7:160:8], T.sy[:, 7:160:8], A.mult))],
-            lambda: [v(V.tensor_tensor(T.trade[:, k:40:2], T.odd[:], T.dif[:, k:40:2], A.mult)) for k in range(2)],
-            lambda: [v(V.tensor_tensor(T.new[:], T.trade[:], T.xc[:, 0:160:4], A.add))],
-            lambda: [v(V.tensor_copy(out[:], T.new[:, k:40:2])) for k, out in enumerate([f_o, T.l_o])],
-        ]
-        state = [0]
+        def new_list():
+            at["f"] = v(V.tensor_copy(f_o[:], T.new[:, 0:40:2]))
+            at["l"] = v(V.tensor_copy(T.l_o[:], T.new[:, 1:40:2]))
+            if r < 2:
+                after("g", at["f"])
+                send(peer(r + 1), T["el%d" % (r + 1)][:], f_o[:], "e%d" % (r + 1))
 
-        def edit_step():
-            if edit:
-                vv(state[0])
-                state[0] = edit.pop(0)()[-1]
-
-        need("s", "sa", xh)
-        need("s", "sv", nb)
-        zb0, zb1 = far_side(0), far_side(1)
-        need("v", "sa", ni)
-        for _ in range(EDIT0):
-            edit_step()
+        aside.extend(chain(
+            lambda: [turn_part(T.tin2, T.irow2, h) for h in range(2)][1],
+            lambda: v(V.tensor_tensor(T.yc[:], T.tin2[:].indirect(T.flag_o[:]), T.fc[:], A.subtract)),
+            lambda: v(V.tensor_tensor_scan(T.sy[:], T.alt[:], T.yc[:], 0.0, A.mult, A.add)),
+            lambda: v(V.tensor_tensor(T.odd[:], T.sy[:, 7:160:8], T.sy[:, 7:160:8], A.mult)),
+            lambda: [v(V.tensor_tensor(T.trade[:, k:40:2], T.odd[:], T.dif[:, k:40:2], A.mult)) for k in range(2)][1],
+            lambda: v(V.tensor_tensor(T.new[:], T.trade[:], T.old[:], A.add)),
+            new_list))
+        after("s", at["xh"])
+        zb = [far_side(h) for h in range(3)]
+        after("v", ni)
         if r == 0:
             need("p", "ldw", 32)
-        tz0 = means(0, zb0, ps[0:4], edit_step)
-        while edit:
-            edit_step()
-        nl = state[0]
-        nf = nl - 1
-        if r < 2:
-            need("g", "sv", nf)
-            send(peer(r + 1), T["el%d" % (r + 1)][:], f_o[:], "e%d" % (r + 1))
-            todo[:] = [(r + 1, name, k) for name, k in CHAIN]
-        else:
-            todo[:] = [(3, "dn", 0)]
-        zb2 = far_side(2)
-        need("s", "sv", nf)
+        for k in range(4):
+            step()
+            mean(0, k)
+        step()
+        mean(1, 0)
+        tz0 = products(0, ps[0:4])
+        for k in range(1, 4):
+            step()
+            mean(1, k)
+        todo[:] = [(r + 1, name) for name in CHAIN] if r < 2 else [(3, "out")]
+        after("s", at["f"])
         more(M[0])
         ha = layer(0, tz0, ps[0:4], "s", range(4))
         more(M[1])
-        tz1 = means(1, zb1, ps[4:8], edit_step)
-        need("v", "sa", ha)
+        mean(2, 0)
+        tz1 = products(1, ps[4:8])
+        mean(2, 1)
+        after("v", ha)
         codes(0)
+        mean(2, 2)
         hb = layer(1, tz1, ps[4:8], "s", [0, 1])
         vb = layer(1, tz1, ps[4:8], "v", [2, 3])
-        need("v", "sa", hb)
-        vv()
+        mean(2, 3)
+        after("v", hb, vb)
         codes(1)
         more(M[2])
-        need("p", "sa", ha)
-        tz2 = means(2, zb2, ps[0:4], edit_step)
+        after("p", ha)
+        tz2 = products(2, ps[0:4])
         if r < 2:
-            inv[0] = inverse(r + 1)
-        for b in range(4):
-            need("s", "st", tz2[b])
-            s(S.activation(T.j[:, C * b + FAR:C * b + C], ps[b][:, 128 - (C - FAR):128], F.Copy, scale=0.03125))
-        more(M[3])
+            v(V.tensor_copy(T.old[:, 0:40:2], T.new[:, 0:40:2]))
+            n = v(V.tensor_scalar(T.sign[:], T.odd[:], -2.0, 1.0, A.mult, A.add))
+            aside.extend(third_power(r + 1))
+            step()
+            after("v", n)
+            v(V.tensor_tensor(T.dif[:, 0:40:2], T.dif[:, 0:40:2], T.sign[:], A.mult))
+            step()
+            inverse(r + 1)
         if r == 0:
-            need("v", "sg", g4)
-            v(V.quantize_mx(T.qe[:], T.pe[:], T.eb[:]))
-            need("p", "sv", cnt["sv"])
-        if r == 1:
+            after("v", g4)
+            after("p", v(V.quantize_mx(T.qe[:], T.pe[:], T.eb[:])))
+        if r == 2:
             need("v", "ldv", 16)
             v(V.quantize_mx(T.qv[:], T.pv[:], T.vt[:]))
-        need("p", "sa", hb)
-        need("p", "sv", vb)
-        for k in ("c0", "p0", "c1", "p1"):
-            landed("p", r, k)
+        step()
         for b in range(4):
-            td = p(P.matmul_mx(ps[4 + b][:, 0:FAR], T.qe[:, 128 * b:128 * b + 128], T.pe[:, 128 * b:128 * b + 128], T["ql%d" % r][:], T["pl%d" % r][:], True, True))
-            need("s", "st", td)
-            ja = s(S.activation(T.j[:, C * b:C * b + FAR], ps[4 + b][:, 0:FAR], F.Copy))
-            need("v", "sa", ja)
-            vv(nl)
-            v(V.tensor_tensor(xn[:, b:4 * C:4], T.j[:, C * b:C * b + C].indirect(T.l_o[:]), x[:, b:4 * C:4], A.add))
-        need("p", "sa", ja)
-        more(M[4])
+            after("s", tz2[b])
+            near = s(S.activation(T.j[:, C * b + FAR:C * b + C], ps[b][:, 128 - (C - FAR):128], F.Copy, scale=0.03125))
+        more(M[3])
+        after("p", hb, vb)
+        for h, banks in (0, ps[4:8]), (1, ps[0:4]):
+            lo, hi = SENT[h]
+            landed("p", r, "c%d" % h)
+            landed("p", r, "p%d" % h)
+            td = [p(P.matmul_mx(banks[b][:, 0:128], T.qe[:, 128 * b:128 * b + 128], T.pe[:, 128 * b:128 * b + 128], T["ql%d" % r][:, hi - 128:hi], T["pl%d" % r][:, hi - 128:hi], True, True)) for b in range(4)]
+            ja = []
+            for b in range(4):
+                q = "v" if h == 1 and b < 2 else "s"
+                out, in_ = T.j[:, C * b + lo:C * b + hi], banks[b][:, 128 - (hi - lo):128]
+                after(q, td[b])
+                ja.append(v(V.tensor_copy(out, in_)) if q == "v" else s(S.activation(out, in_, F.Copy)))
+            if h == 0:
+                first = ja[3]
+                after("p", near)
+                more(M[4])
+        after("v", at["l"], first)
+        after("p", ja[1], ja[3])
+        more(M[5])
 
-    vv()
-    n = v(V.quantize_mx(T.qx[:], T.px[:], X[3][:]))
-    need("p", "sv", n)
-    t = p(P.matmul_mx(ps[0][:, 0:C], T.qv[:], T.pv[:], T.qx[:], T.px[:], True, True))
-    need("y", "sv", n)
-    need("s", "sv", n)
-    Y.dma_start(T.oc[:], T.qx[:].bitcast(dt.uint8)).then_inc(T.sem.out, 16)
-    for k in range(4):
-        (S if k % 2 else Y).dma_start(T.osc[4 * k:4 * k + 4, :], T.px[32 * k:32 * k + 4, :]).then_inc(T.sem.out, 16)
-    need("v", "st", t)
-    n = v(V.tensor_copy(T.w0[:], ps[0][:, 0:C]))
-    need("y", "sv", n)
-    Y.dma_start(T.y[:], T.w0[:]).then_inc(T.sem.out, 16)
-    g.wait_ge(T.sem.out, 16 * 7)
-    for k in ("sv", "sa", "st", "sg", "sent", "slots"):
-        need("g", k, cnt[k])
+        def add(h, b):
+            lo, hi = HALVES[h]
+            after("v", ja[b])
+            return v(V.tensor_tensor(xn[:, 4 * lo + b:4 * hi:4], T.j[:, C * b:C * b + C].indirect(T.l_o[:, lo // 16:hi // 16]), x[:, 4 * lo + b:4 * hi:4], A.add))
+        n = [add(0, b) for b in range(4)][3]
+        add(1, 0)
+        after("v", n)
+        quantise(xn, *HALVES[0], r + 1)
+        more(M[6])
+        after("v", [add(1, b) for b in range(1, 4)][2])
+        quantise(xn, *HALVES[1], r + 1)
+
+    for k in COUNTED:
+        need("g", k)

@@ -7,13 +7,14 @@ HUGE = 2.0 ** 80
 PARTS = [(0, 128), (128, 256), (256, 320)]
 SENT = [(0, 128), (128, FAR)]
 HALVES = [(0, 192), (192, C)]
-OWN_SLOT, FAR_SLOT = [4, 8, 12, 1, 5, 9, 13], [2, 6, 10, 14, 3, 7, 11]
-FIRST = ["a1", "a2", "a3", "e1", "e2", "e3", "a4", "dn", "e4", "u"]
-CHAIN = ["a1", "a2", "a3", "e1", "e2", "e3", "a4", "e4", "u"]
-M0, M1, M = 3, 3, [0, 1, 3, 1, 1, 3, 0]
 SPLIT = [(0, MID), (MID, C)]
-ORDER0 = "mommcpcpcppppp"
+OWN_SLOT, FAR_SLOT = [4, 8, 12, 1, 5, 9, 13], [2, 6, 10, 14, 3, 7, 11]
+CHAIN = ["a1", "a2", "a3", "e1", "e2", "e3", "a4", "e4"]
+ORDER0 = "cocc-" + "p" * 7
 W1 = [3, 5, 5]
+ORDER1 = ["aabb-ababaabbmm"] + ["aa-bababaambmbb"] * 2
+ORDER = ["zaeaeaeaebAebebeb.cBc0csvc1....C"] * 2 + ["aaaabAzbbbeBe0esevee1ecccc..C"]
+HELP = [1, 2, 3]
 
 f32, b16, i32, u16, q8, u8 = "float32", "bfloat16", "int32", "uint16", "float8_e4m3fn_x4", "uint8"
 SCRATCH = {
@@ -31,24 +32,23 @@ SCRATCH = {
     "qz": ("sbuf", [128, 384], q8), "pz": ("sbuf", [128, 384], u8),
     "dli": ("sbuf", [128, 20], i32), "nli": ("sbuf", [128, 20], i32),
     "n_o": ("sbuf", [128, 20], u16), "f_o0": ("sbuf", [128, 20], u16),
-    "a_o": ("sbuf", [128, 20], u16), "b_o": ("sbuf", [128, 20], u16), "l_o": ("sbuf", [128, 20], u16),
-    "flag_o": ("sbuf", [128, 10], u16), "own_o": ("sbuf", [128, 14], u16), "far_o": ("sbuf", [128, 10], u16), "one_o": ("sbuf", [128, 2], u16),
-    "odd": ("sbuf", [128, 20], f32), "sign": ("sbuf", [128, 20], f32),
-    "old": ("sbuf", [128, 40], f32), "dif": ("sbuf", [128, 40], f32), "trade": ("sbuf", [128, 40], f32), "new": ("sbuf", [128, 40], f32),
+    "a_o": ("sbuf", [128, 20], u16), "b_o": ("sbuf", [128, 20], u16), "l_o": ("sbuf", [128, 32], u16),
+    "flag_o": ("sbuf", [128, 10], u16), "own_o": ("sbuf", [128, 16], u16), "far_o": ("sbuf", [128, 10], u16), "one_o": ("sbuf", [128, 2], u16),
+    "odd": ("sbuf", [128, 20], f32), "dif": ("sbuf", [128, 20], f32), "trade": ("sbuf", [128, 20], f32), "new": ("sbuf", [128, 20], f32),
     "rowi": ("sbuf", [128, 8], i32), "row_o": ("sbuf", [128, 8], u16),
-    "cst": ("sbuf", [128, 12], f32), "tv": ("sbuf", [128, 44], f32),
-    "krow": ("sbuf", [128, 320], f32), "kcol": ("sbuf", [128, 320], f32),
-    "iot": ("sbuf", [128, C], b16), "wt": ("sbuf", [128, 208], f32), "alt": ("sbuf", [128, 160], b16),
+    "cst": ("sbuf", [128, 12], f32), "tv": ("sbuf", [128, 48], f32),
+    "krow": ("sbuf", [128, 352], f32), "kcol": ("sbuf", [128, 352], f32),
+    "iot": ("sbuf", [128, C], b16), "wt": ("sbuf", [128, 240], f32), "wtb": ("sbuf", [128, 160], f32), "alt": ("sbuf", [128, 160], b16),
     "w0": ("sbuf", [128, C], f32), "w1": ("sbuf", [128, C], f32), "w2": ("sbuf", [128, C], f32),
     "y1": ("sbuf", [128, C], f32), "y2": ("sbuf", [128, C], f32), "yo": ("sbuf", [128, C], f32), "oa": ("sbuf", [128, C], f32),
     "ts": ("sbuf", [128, C], f32), "pt": ("sbuf", [128, 352], f32),
     "wp": ("sbuf", [128, C], f32), "yp": ("sbuf", [128, C], f32), "mb": ("sbuf", [128, C], f32),
     "tat": ("sbuf", [128, C], b16), "tbt": ("sbuf", [128, C], b16), "a456": ("sbuf", [128, C], b16), "e456": ("sbuf", [128, C], b16),
     "r1": ("sbuf", [128, 2 * C], b16), "r2": ("sbuf", [128, 2 * C], b16), "e3": ("sbuf", [128, C], b16), "a3": ("sbuf", [128, 352], b16),
-    "einv": ("sbuf", [128, C], b16), "urow": ("sbuf", [128, C], b16),
+    "einv": ("sbuf", [128, C], b16), "jp": ("sbuf", [128, 512], b16),
     "irow": ("sbuf", [128, 352], b16), "irow2": ("sbuf", [128, 352], b16), "prow": ("sbuf", [128, 352], b16),
     "tin": ("sbuf", [128, 704], b16), "tin2": ("sbuf", [128, 704], b16), "tp": ("sbuf", [128, 672], b16), "t3": ("sbuf", [128, 672], b16),
-    "qa": ("sbuf", [128, 216], f32), "qb": ("sbuf", [128, 168], f32), "da": ("sbuf", [128, 160], f32), "db": ("sbuf", [128, 160], f32),
+    "qa": ("sbuf", [128, 248], f32), "qb": ("sbuf", [128, 168], f32), "da": ("sbuf", [128, 160], f32), "db": ("sbuf", [128, 160], f32),
     "fc": ("sbuf", [128, 160], b16), "sa": ("sbuf", [128, 160], f32), "sb": ("sbuf", [128, 160], f32),
     "yc": ("sbuf", [128, 160], b16), "sy": ("sbuf", [128, 160], b16),
 }
@@ -143,17 +143,18 @@ def rank_program(g, core, T, topo):
         v(V.transpose(out[:, 0:320], row[:, 16:336]))
         return v(V.transpose(out[:, 320:672], row[:, 0:352]))
 
-    def turn_part(out, row, h):
+    def turn_part(out, row, h, k):
         lo, hi, at = ((0, 128, 0), (128, C, 288))[h]
-        v(V.transpose(out[:, at:at + hi - lo], row[:, 16 + lo:16 + hi]))
+        if k == 0:
+            return v(V.transpose(out[:, at:at + hi - lo], row[:, 16 + lo:16 + hi]))
         return v(V.transpose(out[:, at + hi - lo:at + 2 * (hi - lo) + 32], row[:, lo:hi + 32]))
 
     Y.dma_start(T.dli[:], T.dl[:]).then_inc(T.sem.ldd, 16)
     Y.dma_start(T.ut[:], T.u[:]).then_inc(T.sem.ldu, 16)
-    S.dma_start(T.xa[:], T.x[:]).then_inc(T.sem.ldx, 16)
-    S.dma_start(T.nli[:], T.nl[:]).then_inc(T.sem.ldn, 16)
-    S.dma_start(T.qw[:].bitcast(dt.uint8), T.wc[:]).then_inc(T.sem.ldw, 16)
-    S.dma_start(T.pw[:], T.ws[:]).then_inc(T.sem.ldw, 16)
+    Y.dma_start(T.xa[:], T.x[:]).then_inc(T.sem.ldx, 16)
+    Y.dma_start(T.nli[:], T.nl[:]).then_inc(T.sem.ldn, 16)
+    Y.dma_start(T.qw[:].bitcast(dt.uint8), T.wc[:]).then_inc(T.sem.ldw, 16)
+    Y.dma_start(T.pw[:], T.ws[:]).then_inc(T.sem.ldw, 16)
 
     def count(out, pattern, base):
         return gc(g.iota(out, pattern, base, 0, allow_small_or_imprecise_dtypes=True))
@@ -168,7 +169,6 @@ def rank_program(g, core, T, topo):
         count(table(k, 0, 1, 16), [inner[0], [even + odd, 2]] + inner[1:], base)
         return count(table(k, 16), [inner[0], [even - odd, 2]] + inner[1:], base + odd)
     DEPTH, AT1, AT2, AT8, ATA, ATB, FLAG, OWN, OTHER, SLOT = range(10)
-    g2 = count(T.iot[:], [[1, C]], -MID)
     gc(g.iota(T.rowi[:], [[16, 8]], 0, 0))
     count(table(DEPTH, 1, 4), [[0, 2], [-1, 2], [-2, 2]], 2)
     count(table(DEPTH, 3, 4), [[0, 2], [1, 2], [2, 2]], 0)
@@ -177,76 +177,84 @@ def rank_program(g, core, T, topo):
     g1 = count(T.tv[:, 4:6], [[256, 2]], 0)
 
     act, bias, floor = T.cst[:, 0:3], T.cst[:, 4:7], T.cst[:, 8:9]
+    ones = v(V.memset(T.ones[:], 1.0))
     v(V.memset(table(DEPTH, 0, 4), 2.0))
     v(V.memset(table(DEPTH, 2, 4), -1.0))
     v(V.memset(T.tat[:], 0.0))
+    after("v", ones)
+    g2 = v(V.tensor_tensor_scan(T.iot[:], T.ones[:, 0:C], T.ones[:, 0:C], -1.0 - MID, A.mult, A.add))
     n0 = v(V.memset(T.tbt[:], 0.0))
-    for pad in T.a3, T.irow2, T.prow, T.irow:
-        v(V.memset(pad[:], 0.0))
-    v(V.memset(T.pt[:], HUGE))
-    ones = v(V.memset(T.ones[:], 1.0))
+    v(V.memset(T.a3[:], 0.0))
     after("s", g2)
-    for out, lo, hi, fill in (T.wt, 0, 160, 0.0), (T.wt, 160, 208, MID), (T.qa, 0, 8, 0.0), (T.qb, 0, 8, 0.0), (T.alt, 0, 160, -1.0):
-        n = s(S.activation(out[:, lo:hi], T.iot[:, lo:hi], F.Identity, scale=0.0, bias=float(fill)))
+    for pad in T.prow, T.irow, T.irow2:
+        for lo in 0, 336:
+            s(S.activation(pad[:, lo:lo + 16], T.iot[:, 0:16], F.Copy, scale=0.0))
     yo = s(S.activation(T.yo[:], T.iot[:], F.Copy))
-    after("s", n)
-    s(S.activation(T.alt[:, 0:160:8], T.iot[:, 0:20], F.Copy, scale=0.0))
+
+    def fills():
+        for out, lo, hi, fill in (T.alt, 0, 160, -1.0), (T.wt, 0, 160, 0.0), (T.wt, 160, 240, MID), (T.wtb, 0, 160, 0.0), (T.qa, 0, 8, 0.0), (T.qb, 0, 8, 0.0):
+            n = s(S.activation(out[:, lo:hi], T.iot[:, lo:hi], F.Identity, scale=0.0, bias=float(fill)))
+        after("s", n)
+        return s(S.activation(T.alt[:, 0:160:8], T.iot[:, 0:20], F.Copy, scale=0.0))
     need("v", "ldd", 16)
     vd = v(V.tensor_copy(T.f_o0[:], T.dli[:]))
     after("g", vd)
     send(peer(0), T.el0[:], T.f_o0[:], "e0")
     after("v", g1, n0)
     v(V.tensor_copy(T.row_o[:], T.rowi[:]))
-    n1 = v(V.transpose(T.kcol[:, 0:64], T.krow[:, 0:64]))
+    after("v", v(V.transpose(T.kcol[:, 0:64], T.krow[:, 0:64])))
+    n1 = v(V.tensor_scalar(act, T.tv[:, 0:3], turned(DEPTH), None, A.is_le))
+    v(V.tensor_scalar(T.one_o[:], T.tv[:, 4:6], turned(AT1), 671.0, A.add, A.min))
     need("v", "ldu", 16)
     n2 = v(V.quantize_mx(T.qu[:], T.pu[:], T.ut[:]))
     after("v", n1)
-    n1 = v(V.tensor_scalar(act, T.tv[:, 0:3], turned(DEPTH), None, A.is_le))
-    v(V.tensor_scalar(T.one_o[:], T.tv[:, 4:6], turned(AT1), 671.0, A.add, A.min))
-    after("v", n2)
-    v(V.tensor_copy(T.qr[:].bitcast(dt.uint32), T.qu[:].bitcast(dt.uint32).indirect(T.row_o[:])))
-    v(V.tensor_copy(T.pr[:], T.pu[:].indirect(T.row_o[:])))
-    after("v", n1)
     v(V.tensor_scalar(bias, act, -HUGE, HUGE, A.mult, A.add))
     masks = v(V.tensor_scalar(floor, act[:, 2:3], -2 * HUGE, HUGE, A.mult, A.add))
+    after("v", n2)
+    v(V.tensor_copy(T.qr[:].bitcast(dt.uint32), T.qu[:].bitcast(dt.uint32).indirect(T.row_o[:])))
     after("y", n0, yo)
     slot("ta", T.tat, OWN_SLOT[0], T.iot)
-    slot("tb", T.tbt, FAR_SLOT[0], T.iot)
     need("v", "ldx", 16)
-    for first, stride, base in (0, 2, 0), (1, 9, 1), (2, -3, 9), (3, 9, 5):
-        count(table(FLAG, first, 4), [[0, 4], [stride, 2]], base)
+    count(table(OWN), [[0, 4], [-1, 2], [-4, 4]], 13)
+    places = count(table(OTHER), [[0, 4], [1, 2], [4, 4]], 2)
     halves(ATA, [[0, 1], [0, 8]], 16, 144)
     halves(ATB, [[0, 1], [0, 8]], 16, 208, 160)
-
-    def more_tables():
-        halves(AT8, [[0, 1], [0, 8]], 16, 336)
-        halves(AT2, [[32, 4], [15, 2]], 16, 336)
+    halves(AT8, [[0, 1], [0, 8]], 16, 336)
+    halves(AT2, [[32, 4], [FAR_SLOT[0] - OWN_SLOT[1], 2]], 16, 336, OWN_SLOT[1])
 
     def late_tables():
-        count(table(OWN), [[0, 4], [-1, 2], [-4, 4]], 13)
-        count(table(OTHER), [[0, 4], [1, 2], [4, 4]], 2)
-        count(T.tv[:, 8:18], [[32, 10]], 0)
+        for first, stride, base in (0, 2, 0), (1, 9, 1), (2, -3, 9), (3, 9, 5):
+            count(table(FLAG, first, 4), [[0, 4], [stride, 2]], base)
+
+    def last_tables():
         count(T.tv[:, 20:24], [[128, 4]], 0)
         count(table(SLOT), [[0, 2], [-1, 16]], 0)
+        count(T.tv[:, 8:18], [[32, 10]], 0)
         return count(T.tv[:, 24:44], [[-16, 20]], 0)
 
     def late_constants(g3):
-        def last():
+        def itself():
+            after("v", places)
+            return [v(V.memset(table(k, t, 8), float(OWN_SLOT[0]))) for k, t in ((OWN, 7), (OTHER, 0), (OTHER, 7))][2]
+
+        def first():
             after("v", g3)
-            v(V.memset(table(OWN, 7, 8), float(OWN_SLOT[0])))
-            return v(V.memset(table(OTHER, 7, 8), float(OWN_SLOT[0])))
+            return v(V.transpose(T.kcol[:, 64:320], T.krow[:, 64:320]))
 
         def lists():
-            v(V.tensor_scalar(T.wt[:, 7:160:8], T.tv[:, 24:44], turned(SLOT), None, A.add))
+            after("v", at["fills"])
+            n = [v(V.tensor_scalar(wt[:, 7:160:8], T.tv[:, 24:44], turned(SLOT), None, A.add)) for wt in (T.wt, T.wtb)][0]
             for base, k, out, lo, hi in (ATA, FLAG, T.flag_o, 0, 4), (ATB, FLAG, T.flag_o, 4, 10), (AT8, OWN, T.own_o, 0, 10), (AT8, OTHER, T.far_o, 0, 10):
                 v(V.tensor_scalar(out[:, lo:hi], T.tv[:, 8 + lo:8 + hi], turned(base), turned(k), A.add, A.add))
-            at["lists"] = v(V.tensor_scalar(T.own_o[:, 10:14], T.tv[:, 20:24], turned(AT2), 671.0, A.add, A.min))
-        return chain(last, lambda: v(V.transpose(T.kcol[:, 64:320], T.krow[:, 64:320])), lists)
+            v(V.tensor_scalar(T.own_o[:, 10:14], T.tv[:, 20:24], turned(AT2), 671.0, A.add, A.min))
+            after("v", n)
+            at["lists"] = v(V.tensor_tensor(T.wtb[:, 0:160:8], T.nli[:], T.wt[:, 7:160:8], A.add))
+        return chain(itself, first, lists)
 
     X = [T.xa, T.xb, T.xa, T.xb]
     ps = [T["ps%d" % i] for i in range(8)]
     at = {}
-    todo = [(0, name) for name in FIRST]
+    todo = [(0, name) for name in CHAIN]
     own_rows = [T.iot[:], T.r1[:, 0:C], T.r2[:, 0:C], T.a3[:, 16:336]]
     far_rows = [T.iot[:], T.r1[:, C:2 * C], T.r2[:, C:2 * C], T.e3[:]]
 
@@ -256,12 +264,16 @@ def rank_program(g, core, T, topo):
             k = int(name[1]) if name[1:].isdigit() else 0
             if name[0] == "e":
                 landed("s", r, "e" if k < 4 else "t")
+            if name in ("a1", "l", "out"):
+                after("s", at.get("f"))
             if 1 < k < 4:
                 after("s", at[name[0] + str(k - 1)])
             if name in ("a1", "a2", "a3"):
                 at[name] = s(S.activation(own_rows[k], own_rows[k - 1].indirect(d_o[:]), F.Copy))
                 need("y", "sa")
                 slot("ta", T.tat, OWN_SLOT[k], own_rows[k])
+                if k == 1:
+                    slot("tb", T.tbt, FAR_SLOT[0], own_rows[k])
             elif name in ("e1", "e2", "e3"):
                 at[name] = s(S.activation(far_rows[k], far_rows[k - 1].indirect(e_o[:]), F.Copy))
                 need("y", "sa")
@@ -279,15 +291,9 @@ def rank_program(g, core, T, topo):
                 need("y", "sa")
                 for k in 1, 2, 3:
                     slot("tb", T.tbt, FAR_SLOT[k + 3], T.e456, FAR_SLOT[k])
-            elif name == "u":
+            elif name == "l":
                 after("s", at["inv"])
-                s(S.activation(T.urow[:], T.einv[:].indirect(d_o[:]), F.Copy))
-                need("y", "sa")
-                slot("tb", T.tbt, 15, T.urow)
-                slot("ta", T.tat, 0, T.urow)
-            elif name == "dn":
-                after("s", at["n"])
-                at["dn"] = s(S.activation(T.irow2[:, 16:336], own_rows[1].indirect(T.n_o[:]), F.Copy))
+                at["lrow"] = s(S.activation(T.irow2[:, 16:336], T.einv[:].indirect(d_o[:]), F.Copy))
             else:
                 s(S.activation(T.y1[:], T.iot[:].indirect(d_o[:]), F.Identity, bias=float(MID)))
                 need("y", "sa")
@@ -321,10 +327,10 @@ def rank_program(g, core, T, topo):
 
         def far():
             after("v", at["lists"])
-            at["qb"] = v(V.tensor_tensor(T.qb[:, 8:168], T.tp[:].indirect(T.far_o[:]), T.wt[:, 0:160], A.add))
+            at["qb"] = v(V.tensor_tensor(T.qb[:, 8:168], T.tp[:].indirect(T.far_o[:]), T.wtb[:], A.add))
 
         def own():
-            at["qa"] = v(V.tensor_tensor(T.qa[:, 8:216], T.tp[:].indirect(T.own_o[:, 0:13]), T.wt[:], A.add))
+            at["qa"] = v(V.tensor_tensor(T.qa[:, 8:216], T.tp[:].indirect(T.own_o[:, 0:13]), T.wt[:, 0:208], A.add))
 
         def far_steps():
             after("v", at["qb"])
@@ -335,8 +341,7 @@ def rank_program(g, core, T, topo):
             at["da"] = v(V.tensor_tensor(T.da[:], T.qa[:, 7:167], T.qa[:, 8:168], A.subtract))
 
         def mates():
-            v(V.tensor_tensor(T.dif[:, 1:40:2], T.qa[:, 169:208:2], T.qa[:, 168:208:2], A.subtract))
-            v(V.tensor_copy(T.old[:, 1:40:2], T.qa[:, 168:208:2]))
+            v(V.tensor_tensor(T.dif[:], T.qa[:, 169:208:2], T.qa[:, 168:208:2], A.subtract))
         return chain(join, lambda: turn(T.tp, T.prow), far, own, far_steps, own_steps, mates)
 
     def quantise(x, lo, hi, r):
@@ -371,7 +376,10 @@ def rank_program(g, core, T, topo):
             done("out", S.dma_start(T.y[:, lo:hi], T.w0[:, lo:hi]), 16)
 
     after("s", vd)
-    more(M0)
+    more(1)
+    after("s", n2)
+    after("p", s(S.activation(T.pr[:], T.pu[:].indirect(T.row_o[:]), F.Copy)))
+    more(2)
 
     for r in range(3):
         x, xn = X[r], X[r + 1]
@@ -380,8 +388,8 @@ def rank_program(g, core, T, topo):
             for lo, hi in HALVES:
                 quantise(x, lo, hi, 0)
             need("v", "ldn", 16)
-            at["n"] = v(V.tensor_copy(T.n_o[:], T.nli[:]))
-            v(V.tensor_copy(T.old[:, 0:40:2], T.dli[:]))
+            v(V.tensor_copy(T.n_o[:], T.nli[:]))
+            at["pt"] = v(V.memset(T.pt[:], HUGE))
             aside.extend(third_power(0))
         else:
             more(len(todo))
@@ -390,13 +398,12 @@ def rank_program(g, core, T, topo):
         lo, hi = HALVES[-1]
         after("v", at["t1"], masks)
         n = v(V.tensor_scalar(T.w0[:, lo:hi], ps[0][:, 0:hi - lo], floor, None, A.max))
-        step(r == 0)
+        step(1 if r == 0 else 0)
         after("v", n, at["y1"])
         n = v(V.tensor_tensor(T.w1[:], T.w0[:].indirect(d_o[:]), T.y1[:], A.min))
         if r == 0:
             step()
-            more_tables()
-            more(M1)
+            late_tables()
         after("v", n, at["y2"])
         n = [v(V.tensor_tensor(T.w2[:, lo:hi], T.w1[:].indirect(d_o[:, lo // 16:hi // 16]), T.y2[:, lo:hi], A.min)) for lo, hi in SPLIT]
         after("y", n[-1])
@@ -415,27 +422,25 @@ def rank_program(g, core, T, topo):
             need("v", "shift")
             at["oa"] = v(V.tensor_tensor(T.oa[:], T.w2[:].indirect(T["d3_o%d" % r][:, 0:20]), T.yo[:], A.min))
 
-        if r == 1:
-            Y.dma_start(T.vt[:], T.v[:]).then_inc(T.sem.ldv, 16)
         if r == 0:
-            g3 = late_tables()
+            g3 = last_tables()
             after("g", ones)
             g4 = [gc(g.affine_select(T.eb[:, 512 * b:512 * b + 512], T.ones[:], [[-1, 512]], A.is_equal, 0.0, b, 4)) for b in range(4)][-1]
             inverse(0)
+            more(4)
+            at["fills"] = fills()
             more(len(todo))
-            after("v", at["dn"])
-            mate = chain(lambda: turn(T.t3, T.irow2),
-                         lambda: v(V.tensor_scalar(T.new[:, 0:32], T.t3[:].indirect(T.one_o[:]), float(MID), None, A.add)),
-                         lambda: v(V.tensor_tensor(T.dif[:, 0:40:2], T.new[:, 0:20], T.old[:, 0:40:2], A.subtract)))
-            calls = {"m": mate, "o": [own_minima], "c": late_constants(g3), "p": turn_places()}
+            calls = {"-": [lambda: None], "o": [own_minima], "c": late_constants(g3), "p": turn_places()}
             aside.extend([calls[k].pop(0) for k in ORDER0])
         else:
             aside.insert(2, own_minima)
+        if r == 1:
+            Y.dma_start(T.vt[:], T.v[:]).then_inc(T.sem.ldv, 16)
         step(W1[r])
         sl = T["sl%d" % r]
         landed("s", r, "s")
         landed("v", r, "s")
-        after("s", at.get("pt"))
+        after("s", at["pt"])
         n1 = v(V.tensor_copy(T.pt[:, 2:320:4], sl[:]))
         s(S.activation(T.pt[:, 3:320:8], sl[:, 1:80:2], F.Copy))
         n2 = s(S.activation(T.pt[:, 7:320:16], sl[:, 1:80:4], F.Copy))
@@ -451,25 +456,38 @@ def rank_program(g, core, T, topo):
         n = v(V.tensor_tensor(T.mb[:], T.wp[:].indirect(T["e3l%d" % r][:]), T.yp[:], A.min))
         step()
         after("v", n, at["oa"])
-        flags = [v(V.tensor_tensor(T.irow[:, 16 + lo:16 + hi], T.mb[:].indirect(T.n_o[:, lo // 16:hi // 16]), T.oa[:, lo:hi], A.is_lt)) for lo, hi in ((0, MID), (MID, C))]
+        flags = [v(V.tensor_tensor(T.irow[:, 16 + lo:16 + hi], T.mb[:].indirect(T.n_o[:, lo // 16:hi // 16]), T.oa[:, lo:hi], A.is_lt)) for lo, hi in SPLIT]
         after("s", flags[1])
         ni = s(S.activation(T.irow2[:, 16:336], T.irow[:, 16:336].indirect(T.n_o[:]), F.Copy))
-        turns, picks, scans, ends = [], [], [], []
-        for h in range(2):
-            after("v", flags[h])
-            turns.append(turn_part(T.tin, T.irow, h))
-        step(len(aside))
-        for h, (lo, hi) in enumerate(((0, 64), (64, 160))):
-            after("v", turns[h], at["lists"])
-            picks.append(v(V.tensor_copy(T.fc[:, lo:hi], T.tin[:, 0:(288, 704)[h]].indirect(T.flag_o[:, lo // 16:hi // 16]))))
-        for h, (lo, hi) in enumerate(((0, 64), (64, 160))):
-            after("v", picks[h], at["da"], at["db"])
-            scans.append([v(V.tensor_tensor_scan(out[:, lo:hi], d[:, lo:hi], T.fc[:, lo:hi], 0.0, A.add, A.mult)) for out, d in ((T.sb, T.db), (T.sa, T.da))])
-        for h, (lo, hi) in enumerate(((0, 64), (64, 160))):
-            ends.append([])
-            for k, (out, sc) in enumerate(((T.b_o, T.sb), (T.a_o, T.sa))):
-                after("v", scans[h][k])
-                ends[h].append(v(V.tensor_copy(out[:, lo // 8:hi // 8], sc[:, lo + 7:hi:8])))
+        ends = [[None, None], [None, None]]
+
+        def cursors(h):
+            lo, hi = ((0, 64), (64, 160))[h]
+            scans = []
+
+            def turn_half(k):
+                after("v", flags[h])
+                return turn_part(T.tin, T.irow, h, k)
+
+            def pick():
+                after("v", at["lists"])
+                return v(V.tensor_copy(T.fc[:, lo:hi], T.tin[:, 0:(288, 704)[h]].indirect(T.flag_o[:, lo // 16:hi // 16])))
+
+            def scan():
+                after("v", at["da"], at["db"])
+                scans.extend([v(V.tensor_tensor_scan(out[:, lo:hi], d[:, lo:hi], T.fc[:, lo:hi], 0.0, A.add, A.mult)) for out, d in ((T.sb, T.db), (T.sa, T.da))])
+
+            def end(k):
+                after("v", scans[k])
+                ends[h][k] = v(V.tensor_copy((T.b_o, T.a_o)[k][:, lo // 8:hi // 8], (T.sb, T.sa)[k][:, lo + 7:hi:8]))
+            return [lambda: turn_half(0)] + chain(lambda: turn_half(1), pick, scan, lambda: end(0), lambda: end(1))
+
+        def mate_flags(h):
+            after("v", ni)
+            at["mates"] = [turn_part(T.tin2, T.irow2, h, k) for k in range(2)][1]
+        calls = {"a": cursors(0), "b": cursors(1), "-": [lambda: step(len(aside))], "m": [lambda: mate_flags(0), lambda: mate_flags(1)]}
+        for call in ORDER1[r]:
+            calls[call].pop(0)()
 
         def far_side(h):
             lo, hi = PARTS[h]
@@ -504,73 +522,70 @@ def rank_program(g, core, T, topo):
             send(peer(r), T["pl%d" % r][:, lo:hi], ph[:, end - (hi - lo):end], "p%d%d" % (h, r))
 
         def new_list():
-            at["f"] = v(V.tensor_copy(f_o[:], T.new[:, 0:40:2]))
-            at["l"] = v(V.tensor_copy(T.l_o[:], T.new[:, 1:40:2]))
+            at["f"] = v(V.tensor_copy(f_o[:], T.new[:]))
             if r < 2:
                 after("g", at["f"])
                 send(peer(r + 1), T["el%d" % (r + 1)][:], f_o[:], "e%d" % (r + 1))
 
         aside.extend(chain(
-            lambda: [turn_part(T.tin2, T.irow2, h) for h in range(2)][1],
-            lambda: v(V.tensor_tensor(T.yc[:], T.tin2[:].indirect(T.flag_o[:]), T.fc[:], A.subtract)),
+            lambda: (after("v", at["mates"]), v(V.tensor_tensor(T.yc[:], T.tin2[:].indirect(T.flag_o[:]), T.fc[:], A.subtract)))[1],
             lambda: v(V.tensor_tensor_scan(T.sy[:], T.alt[:], T.yc[:], 0.0, A.mult, A.add)),
             lambda: v(V.tensor_tensor(T.odd[:], T.sy[:, 7:160:8], T.sy[:, 7:160:8], A.mult)),
-            lambda: [v(V.tensor_tensor(T.trade[:, k:40:2], T.odd[:], T.dif[:, k:40:2], A.mult)) for k in range(2)][1],
-            lambda: v(V.tensor_tensor(T.new[:], T.trade[:], T.old[:], A.add)),
+            lambda: v(V.tensor_tensor(T.trade[:], T.odd[:], T.dif[:], A.mult)),
+            lambda: v(V.tensor_tensor(T.new[:], T.trade[:], T.qa[:, 168:208:2], A.add)),
             new_list))
+        place = chain(
+            lambda: (after("v", at["lrow"]), turn(T.tin2, T.irow2))[1],
+            lambda: at.update(l=v(V.tensor_scalar(T.l_o[:], T.tin2[:, 0:672].indirect(T.one_o[:]), float(MID), None, A.add))))
         after("s", at["xh"])
-        zb = [far_side(h) for h in range(3)]
-        after("v", ni)
+        zb = [far_side(h) for h in range(2)]
         if r == 0:
             need("p", "ldw", 32)
-        for k in range(4):
-            step()
-            mean(0, k)
-        step()
-        mean(1, 0)
-        tz0 = products(0, ps[0:4])
-        for k in range(1, 4):
-            step()
-            mean(1, k)
-        todo[:] = [(r + 1, name) for name in CHAIN] if r < 2 else [(3, "out")]
-        after("s", at["f"])
-        more(M[0])
-        ha = layer(0, tz0, ps[0:4], "s", range(4))
-        more(M[1])
-        mean(2, 0)
-        tz1 = products(1, ps[4:8])
-        mean(2, 1)
-        after("v", ha)
-        codes(0)
-        mean(2, 2)
-        hb = layer(1, tz1, ps[4:8], "s", [0, 1])
-        vb = layer(1, tz1, ps[4:8], "v", [2, 3])
-        mean(2, 3)
-        after("v", hb, vb)
-        codes(1)
-        more(M[2])
-        after("p", ha)
-        tz2 = products(2, ps[0:4])
-        if r < 2:
-            v(V.tensor_copy(T.old[:, 0:40:2], T.new[:, 0:40:2]))
-            n = v(V.tensor_scalar(T.sign[:], T.odd[:], -2.0, 1.0, A.mult, A.add))
-            aside.extend(third_power(r + 1))
-            step()
-            after("v", n)
-            v(V.tensor_tensor(T.dif[:, 0:40:2], T.dif[:, 0:40:2], T.sign[:], A.mult))
-            step()
-            inverse(r + 1)
+        planes = [list(range(4)) for h in range(3)]
+        for call in ORDER[r]:
+            if call == "e":
+                step()
+                if not aside:
+                    todo[:] = [(r + 1, name) for name in ["l"] + (CHAIN if r < 2 else ["out"])]
+            elif call in "abc":
+                mean("abc".index(call), planes["abc".index(call)].pop(0))
+            elif call == "A":
+                tz0 = products(0, ps[0:4])
+                ha = layer(0, tz0, ps[0:4], "s", range(4))
+            elif call == "B":
+                tz1 = products(1, ps[4:8])
+            elif call == "s":
+                hb = layer(1, tz1, ps[4:8], "s", [0, 1])
+            elif call == "v":
+                vb = layer(1, tz1, ps[4:8], "v", [2, 3])
+            elif call == "0":
+                after("v", ha)
+                codes(0)
+            elif call == "1":
+                after("v", hb, vb)
+                codes(1)
+            elif call == "C":
+                after("p", ha)
+                tz2 = products(2, ps[0:4])
+            elif call == "z":
+                zb.append(far_side(2))
+            else:
+                more(1)
         if r == 0:
             after("v", g4)
             after("p", v(V.quantize_mx(T.qe[:], T.pe[:], T.eb[:])))
-        if r == 2:
+        place[0]()
+        if r < 2:
+            inverse(r + 1)
+        else:
             need("v", "ldv", 16)
             v(V.quantize_mx(T.qv[:], T.pv[:], T.vt[:]))
-        step()
+        place[1]()
+        for call in third_power(r + 1) if r < 2 else []:
+            call()
         for b in range(4):
             after("s", tz2[b])
             near = s(S.activation(T.j[:, C * b + FAR:C * b + C], ps[b][:, 128 - (C - FAR):128], F.Copy, scale=0.03125))
-        more(M[3])
         after("p", hb, vb)
         for h, banks in (0, ps[4:8]), (1, ps[0:4]):
             lo, hi = SENT[h]
@@ -586,20 +601,27 @@ def rank_program(g, core, T, topo):
             if h == 0:
                 first = ja[3]
                 after("p", near)
-                more(M[4])
+                more(1)
         after("v", at["l"], first)
         after("p", ja[1], ja[3])
-        more(M[5])
+        lo, hi = HALVES[1]
+        picked = {}
+        for b in HELP:
+            after("s", ja[b], ja[3], at["l"])
+            picked[b] = s(S.activation(T.jp[:, 128 * b:128 * b + 128], T.j[:, C * b:C * b + C].indirect(T.l_o[:, lo // 16:hi // 16]), F.Copy))
+        more(2)
 
         def add(h, b):
             lo, hi = HALVES[h]
             after("v", ja[b])
+            if h and b in picked:
+                after("v", picked[b])
+                return v(V.tensor_tensor(xn[:, 4 * lo + b:4 * hi:4], T.jp[:, 128 * b:128 * b + 128], x[:, 4 * lo + b:4 * hi:4], A.add))
             return v(V.tensor_tensor(xn[:, 4 * lo + b:4 * hi:4], T.j[:, C * b:C * b + C].indirect(T.l_o[:, lo // 16:hi // 16]), x[:, 4 * lo + b:4 * hi:4], A.add))
         n = [add(0, b) for b in range(4)][3]
         add(1, 0)
         after("v", n)
         quantise(xn, *HALVES[0], r + 1)
-        more(M[6])
         after("v", [add(1, b) for b in range(1, 4)][2])
         quantise(xn, *HALVES[1], r + 1)
 

import numpy as np
from concourse.mybir import dt, AluOpType as A, ActivationFunctionType as F

C, FAR, MID = 320, 240, 160
MASKS = [4, 1, 2]
HUGE = 2.0 ** 80
PARTS = [(0, 128), (128, 256), (256, 320)]
SENT = [(0, 128), (128, FAR)]
HALVES = [(0, 192), (192, C)]
SPLIT = [(0, MID), (MID, C)]
OWN_SLOT, FAR_SLOT = [4, 8, 12, 1, 5, 9, 13], [2, 6, 10, 14, 3, 7, 11]
CHAIN = ["a1", "a2", "a3", "e1", "e2", "e3", "a4", "e4"]
ORDER0 = "cocc-" + "p" * 7
W1 = [3, 5, 5]
ORDER1 = ["aabb-ababaabbmm"] + ["aa-bababaambmbb"] * 2
ORDER = ["zaeaeaeaebAebebeb.cBc0csvc1....C"] * 2 + ["aaaabAzbbbeBe0esevee1ecccc..C"]
HELP = [1, 2, 3]

f32, b16, i32, u16, q8, u8 = "float32", "bfloat16", "int32", "uint16", "float8_e4m3fn_x4", "uint8"
SCRATCH = {
    "xa": ("sbuf", [128, 4 * C], b16), "xb": ("sbuf", [128, 4 * C], b16),
    "xh": ("sbuf", [128, 4 * C], b16), "zb": ("sbuf", [128, 4 * C], b16), "z": ("sbuf", [128, 4 * C], b16),
    "h": ("sbuf", [128, 4 * FAR], b16), "j": ("sbuf", [128, 4 * C], b16),
    "ut": ("sbuf", [128, 512], b16), "vt": ("sbuf", [128, 512], b16),
    "ones": ("sbuf", [128, 512], b16), "eb": ("sbuf", [128, 2048], b16),
    "qu": ("sbuf", [128, 128], q8), "pu": ("sbuf", [128, 128], u8),
    "qr": ("sbuf", [128, 128], q8), "pr": ("sbuf", [128, 128], u8),
    "qv": ("sbuf", [128, 128], q8), "pv": ("sbuf", [128, 128], u8),
    "qe": ("sbuf", [128, 512], q8), "pe": ("sbuf", [128, 512], u8),
    "qw": ("sbuf", [128, 512], q8), "pw": ("sbuf", [128, 512], u8),
    "qx": ("sbuf", [128, C], q8), "px": ("sbuf", [128, C], u8),
    "qz": ("sbuf", [128, 384], q8), "pz": ("sbuf", [128, 384], u8),
    "dli": ("sbuf", [128, 20], i32), "nli": ("sbuf", [128, 20], i32),
    "n_o": ("sbuf", [128, 20], u16), "f_o0": ("sbuf", [128, 20], u16),
    "a_o": ("sbuf", [128, 20], u16), "b_o": ("sbuf", [128, 20], u16), "l_o": ("sbuf", [128, 32], u16),
    "flag_o": ("sbuf", [128, 10], u16), "own_o": ("sbuf", [128, 16], u16), "far_o": ("sbuf", [128, 10], u16), "one_o": ("sbuf", [128, 2], u16),
    "odd": ("sbuf", [128, 20], f32), "dif": ("sbuf", [128, 20], f32), "trade": ("sbuf", [128, 20], f32), "new": ("sbuf", [128, 20], f32),
    "rowi": ("sbuf", [128, 8], i32), "row_o": ("sbuf", [128, 8], u16),
    "cst": ("sbuf", [128, 12], f32), "tv": ("sbuf", [128, 48], f32),
    "krow": ("sbuf", [128, 352], f32), "kcol": ("sbuf", [128, 352], f32),
    "iot": ("sbuf", [128, C], b16), "wt": ("sbuf", [128, 240], f32), "wtb": ("sbuf", [128, 160], f32), "alt": ("sbuf", [128, 160], b16),
    "w0": ("sbuf", [128, C], f32), "w1": ("sbuf", [128, C], f32), "w2": ("sbuf", [128, C], f32),
    "y1": ("sbuf", [128, C], f32), "y2": ("sbuf", [128, C], f32), "yo": ("sbuf", [128, C], f32), "oa": ("sbuf", [128, C], f32),
    "ts": ("sbuf", [128, C], f32), "pt": ("sbuf", [128, 352], f32),
    "wp": ("sbuf", [128, C], f32), "yp": ("sbuf", [128, C], f32), "mb": ("sbuf", [128, C], f32),
    "tat": ("sbuf", [128, C], b16), "tbt": ("sbuf", [128, C], b16), "a456": ("sbuf", [128, C], b16), "e456": ("sbuf", [128, C], b16),
    "r1": ("sbuf", [128, 2 * C], b16), "r2": ("sbuf", [128, 2 * C], b16), "e3": ("sbuf", [128, C], b16), "a3": ("sbuf", [128, 352], b16),
    "einv": ("sbuf", [128, C], b16), "jp": ("sbuf", [128, 512], b16),
    "irow": ("sbuf", [128, 352], b16), "irow2": ("sbuf", [128, 352], b16), "prow": ("sbuf", [128, 352], b16),
    "tin": ("sbuf", [128, 704], b16), "tin2": ("sbuf", [128, 704], b16), "tp": ("sbuf", [128, 672], b16), "t3": ("sbuf", [128, 672], b16),
    "qa": ("sbuf", [128, 248], f32), "qb": ("sbuf", [128, 168], f32), "da": ("sbuf", [128, 160], f32), "db": ("sbuf", [128, 160], f32),
    "fc": ("sbuf", [128, 160], b16), "sa": ("sbuf", [128, 160], f32), "sb": ("sbuf", [128, 160], f32),
    "yc": ("sbuf", [128, 160], b16), "sy": ("sbuf", [128, 160], b16),
}
for _r in range(3):
    SCRATCH["ss%d" % _r] = ("sbuf", [128, 80], f32)
    SCRATCH["sl%d" % _r] = ("sbuf", [128, 80], f32)
    SCRATCH["el%d" % _r] = ("sbuf", [128, 20], u16)
    SCRATCH["e3l%d" % _r] = ("sbuf", [128, 20], u16)
    SCRATCH["d3_o%d" % _r] = ("sbuf", [128, 32], u16)
    SCRATCH["f_o%d" % (_r + 1)] = ("sbuf", [128, 20], u16)
    SCRATCH["qh%d" % _r] = ("sbuf", [128, 256], q8)
    SCRATCH["ph%d" % _r] = ("sbuf", [128, 256], u8)
    SCRATCH["ql%d" % _r] = ("sbuf", [128, FAR], q8)
    SCRATCH["pl%d" % _r] = ("sbuf", [128, FAR], u8)
for _i in range(8):
    SCRATCH["ps%d" % _i] = ("psum", [128, 512], f32)

COUNTED = ["sv", "sa", "st", "sg", "sent", "ta", "tb", "shift", "out"]
SEMAPHORES = COUNTED + ["ldx", "ldu", "ldw", "ldv", "ldd", "ldn"]
for _r in range(3):
    SEMAPHORES += ["s%d" % _r, "e%d" % _r, "t%d" % _r, "c0%d" % _r, "c1%d" % _r, "p0%d" % _r, "p1%d" % _r]


def rank_program(g, core, T, topo):
    rank = T.rank_of(core)
    if rank is None:
        return
    V, S, P, Y = g.vector, g.scalar, g.tensor, g.sync
    queue = {"v": V, "s": S, "p": P, "y": Y, "g": g}
    cnt = {k: 0 for k in COUNTED}
    known = {}

    def need(q, sem, n=None):
        n = cnt[sem] if n is None else n
        if known.get((q, sem), 0) < n:
            queue[q].wait_ge(T.sem[sem], n)
            known[(q, sem)] = n

    def after(q, *calls):
        for call in calls:
            if call:
                need(q, *call)

    def done(sem, ins, k=1):
        ins.then_inc(T.sem[sem], k)
        cnt[sem] += k
        return sem, cnt[sem]

    def v(ins):
        return done("sv", ins)

    def s(ins):
        return done("sa", ins)

    def p(ins):
        return done("st", ins)

    def gc(ins):
        return done("sg", ins)

    aside = []

    def step(n=1):
        for _ in range(min(n, len(aside))):
            aside.pop(0)()

    def chain(*calls):
        last = [None]

        def link(call):
            def run():
                after("v", last[0])
                last[0] = call() or last[0]
            return run
        return [link(call) for call in calls]

    def peer(r):
        return T.cores[rank ^ MASKS[r]]

    def send(dst, out, in_, sem):
        rid, pid = topo.addr(dst, core)
        g.remote_dma(out, in_, T.sem[sem], T.sem.sent, pid, rid, topo.mask(core, dst))
        cnt["sent"] += len(topo.engines(core, dst))

    def landed(q, r, sem):
        need(q, "%s%d" % (sem, r), len(topo.engines(peer(r), core)))

    def slot(sem, tile, i, row, k=None, step=16):
        done(sem, Y.dma_start(tile[i:128:step, :], row[(i if k is None else k):128:step, :]), 16)

    def turn(out, row):
        v(V.transpose(out[:, 0:320], row[:, 16:336]))
        return v(V.transpose(out[:, 320:672], row[:, 0:352]))

    def turn_part(out, row, h, k):
        lo, hi, at = ((0, 128, 0), (128, C, 288))[h]
        if k == 0:
            return v(V.transpose(out[:, at:at + hi - lo], row[:, 16 + lo:16 + hi]))
        return v(V.transpose(out[:, at + hi - lo:at + 2 * (hi - lo) + 32], row[:, lo:hi + 32]))

    Y.dma_start(T.dli[:], T.dl[:]).then_inc(T.sem.ldd, 16)
    Y.dma_start(T.ut[:], T.u[:]).then_inc(T.sem.ldu, 16)
    Y.dma_start(T.xa[:], T.x[:]).then_inc(T.sem.ldx, 16)
    Y.dma_start(T.nli[:], T.nl[:]).then_inc(T.sem.ldn, 16)
    Y.dma_start(T.qw[:].bitcast(dt.uint8), T.wc[:]).then_inc(T.sem.ldw, 16)
    Y.dma_start(T.pw[:], T.ws[:]).then_inc(T.sem.ldw, 16)

    def count(out, pattern, base):
        return gc(g.iota(out, pattern, base, 0, allow_small_or_imprecise_dtypes=True))

    def table(k, first=0, step=1, last=32):
        return T.krow[:, 32 * k + first:32 * k + last:step]

    def turned(k):
        return T.kcol[:, 32 * k:32 * k + 1]

    def halves(k, inner, even, odd, base=0):
        count(table(k, 0, 1, 16), [inner[0], [even + odd, 2]] + inner[1:], base)
        return count(table(k, 16), [inner[0], [even - odd, 2]] + inner[1:], base + odd)
    DEPTH, AT1, AT2, AT8, ATA, ATB, FLAG, OWN, OTHER, SLOT = range(10)
    gc(g.iota(T.rowi[:], [[16, 8]], 0, 0))
    count(table(DEPTH, 1, 4), [[0, 2], [-1, 2], [-2, 2]], 2)
    count(table(DEPTH, 3, 4), [[0, 2], [1, 2], [2, 2]], 0)
    halves(AT1, [[32, 8]], 16, 336)
    count(T.tv[:, 0:3], [[1, 3]], 0)
    g1 = count(T.tv[:, 4:6], [[256, 2]], 0)

    act, bias, floor = T.cst[:, 0:3], T.cst[:, 4:7], T.cst[:, 8:9]
    ones = v(V.memset(T.ones[:], 1.0))
    v(V.memset(table(DEPTH, 0, 4), 2.0))
    v(V.memset(table(DEPTH, 2, 4), -1.0))
    v(V.memset(T.tat[:], 0.0))
    after("v", ones)
    g2 = v(V.tensor_tensor_scan(T.iot[:], T.ones[:, 0:C], T.ones[:, 0:C], -1.0 - MID, A.mult, A.add))
    n0 = v(V.memset(T.tbt[:], 0.0))
    v(V.memset(T.a3[:], 0.0))
    after("s", g2)
    for pad in T.prow, T.irow, T.irow2:
        for lo in 0, 336:
            s(S.activation(pad[:, lo:lo + 16], T.iot[:, 0:16], F.Copy, scale=0.0))
    yo = s(S.activation(T.yo[:], T.iot[:], F.Copy))

    def fills():
        for out, lo, hi, fill in (T.alt, 0, 160, -1.0), (T.wt, 0, 160, 0.0), (T.wt, 160, 240, MID), (T.wtb, 0, 160, 0.0), (T.qa, 0, 8, 0.0), (T.qb, 0, 8, 0.0):
            n = s(S.activation(out[:, lo:hi], T.iot[:, lo:hi], F.Identity, scale=0.0, bias=float(fill)))
        after("s", n)
        return s(S.activation(T.alt[:, 0:160:8], T.iot[:, 0:20], F.Copy, scale=0.0))
    need("v", "ldd", 16)
    vd = v(V.tensor_copy(T.f_o0[:], T.dli[:]))
    after("g", vd)
    send(peer(0), T.el0[:], T.f_o0[:], "e0")
    after("v", g1, n0)
    v(V.tensor_copy(T.row_o[:], T.rowi[:]))
    after("v", v(V.transpose(T.kcol[:, 0:64], T.krow[:, 0:64])))
    n1 = v(V.tensor_scalar(act, T.tv[:, 0:3], turned(DEPTH), None, A.is_le))
    v(V.tensor_scalar(T.one_o[:], T.tv[:, 4:6], turned(AT1), 671.0, A.add, A.min))
    need("v", "ldu", 16)
    n2 = v(V.quantize_mx(T.qu[:], T.pu[:], T.ut[:]))
    after("v", n1)
    v(V.tensor_scalar(bias, act, -HUGE, HUGE, A.mult, A.add))
    masks = v(V.tensor_scalar(floor, act[:, 2:3], -2 * HUGE, HUGE, A.mult, A.add))
    after("v", n2)
    v(V.tensor_copy(T.qr[:].bitcast(dt.uint32), T.qu[:].bitcast(dt.uint32).indirect(T.row_o[:])))
    after("y", n0, yo)
    slot("ta", T.tat, OWN_SLOT[0], T.iot)
    need("v", "ldx", 16)
    count(table(OWN), [[0, 4], [-1, 2], [-4, 4]], 13)
    places = count(table(OTHER), [[0, 4], [1, 2], [4, 4]], 2)
    halves(ATA, [[0, 1], [0, 8]], 16, 144)
    halves(ATB, [[0, 1], [0, 8]], 16, 208, 160)
    halves(AT8, [[0, 1], [0, 8]], 16, 336)
    halves(AT2, [[32, 4], [FAR_SLOT[0] - OWN_SLOT[1], 2]], 16, 336, OWN_SLOT[1])

    def late_tables():
        for first, stride, base in (0, 2, 0), (1, 9, 1), (2, -3, 9), (3, 9, 5):
            count(table(FLAG, first, 4), [[0, 4], [stride, 2]], base)

    def last_tables():
        count(T.tv[:, 20:24], [[128, 4]], 0)
        count(table(SLOT), [[0, 2], [-1, 16]], 0)
        count(T.tv[:, 8:18], [[32, 10]], 0)
        return count(T.tv[:, 24:44], [[-16, 20]], 0)

    def late_constants(g3):
        def itself():
            after("v", places)
            return [v(V.memset(table(k, t, 8), float(OWN_SLOT[0]))) for k, t in ((OWN, 7), (OTHER, 0), (OTHER, 7))][2]

        def first():
            after("v", g3)
            return v(V.transpose(T.kcol[:, 64:320], T.krow[:, 64:320]))

        def lists():
            after("v", at["fills"])
            n = [v(V.tensor_scalar(wt[:, 7:160:8], T.tv[:, 24:44], turned(SLOT), None, A.add)) for wt in (T.wt, T.wtb)][0]
            for base, k, out, lo, hi in (ATA, FLAG, T.flag_o, 0, 4), (ATB, FLAG, T.flag_o, 4, 10), (AT8, OWN, T.own_o, 0, 10), (AT8, OTHER, T.far_o, 0, 10):
                v(V.tensor_scalar(out[:, lo:hi], T.tv[:, 8 + lo:8 + hi], turned(base), turned(k), A.add, A.add))
            v(V.tensor_scalar(T.own_o[:, 10:14], T.tv[:, 20:24], turned(AT2), 671.0, A.add, A.min))
            after("v", n)
            at["lists"] = v(V.tensor_tensor(T.wtb[:, 0:160:8], T.nli[:], T.wt[:, 7:160:8], A.add))
        return chain(itself, first, lists)

    X = [T.xa, T.xb, T.xa, T.xb]
    ps = [T["ps%d" % i] for i in range(8)]
    at = {}
    todo = [(0, name) for name in CHAIN]
    own_rows = [T.iot[:], T.r1[:, 0:C], T.r2[:, 0:C], T.a3[:, 16:336]]
    far_rows = [T.iot[:], T.r1[:, C:2 * C], T.r2[:, C:2 * C], T.e3[:]]

    def more(n):
        for r, name in todo[:n]:
            d_o, e_o = T["f_o%d" % r], T["el%d" % min(r, 2)]
            k = int(name[1]) if name[1:].isdigit() else 0
            if name[0] == "e":
                landed("s", r, "e" if k < 4 else "t")
            if name in ("a1", "l", "out"):
                after("s", at.get("f"))
            if 1 < k < 4:
                after("s", at[name[0] + str(k - 1)])
            if name in ("a1", "a2", "a3"):
                at[name] = s(S.activation(own_rows[k], own_rows[k - 1].indirect(d_o[:]), F.Copy))
                need("y", "sa")
                slot("ta", T.tat, OWN_SLOT[k], own_rows[k])
                if k == 1:
                    slot("tb", T.tbt, FAR_SLOT[0], own_rows[k])
            elif name in ("e1", "e2", "e3"):
                at[name] = s(S.activation(far_rows[k], far_rows[k - 1].indirect(e_o[:]), F.Copy))
                need("y", "sa")
                slot("tb", T.tbt, FAR_SLOT[k], far_rows[k])
            elif name == "a4":
                need("s", "ta")
                after("s", at["d3"])
                s(S.activation(T.a456[:], T.tat[:].indirect(T["d3_o%d" % r][:, 0:20]), F.Copy))
                need("y", "sa")
                for k in 1, 2, 3:
                    slot("ta", T.tat, OWN_SLOT[k + 3], T.a456, OWN_SLOT[k])
            elif name == "e4":
                need("s", "tb")
                s(S.activation(T.e456[:], T.tbt[:].indirect(T["e3l%d" % r][:]), F.Copy))
                need("y", "sa")
                for k in 1, 2, 3:
                    slot("tb", T.tbt, FAR_SLOT[k + 3], T.e456, FAR_SLOT[k])
            elif name == "l":
                after("s", at["inv"])
                at["lrow"] = s(S.activation(T.irow2[:, 16:336], T.einv[:].indirect(d_o[:]), F.Copy))
            else:
                s(S.activation(T.y1[:], T.iot[:].indirect(d_o[:]), F.Identity, bias=float(MID)))
                need("y", "sa")
                done("out", Y.dma_start(T.dn[:], T.y1[0:128:16, :]), 16)
        del todo[:n]

    def halve(x):
        for k in range(4):
            at["xh"] = s(S.activation(T.xh[:, C * k:C * k + C], x[:, k:4 * C:4], F.Copy, scale=0.5))

    def third_power(r):
        def first():
            after("v", at["a3"])
            return turn(T.t3, T.a3)

        def second():
            at["d3"] = v(V.tensor_scalar(T["d3_o%d" % r][:], T.t3[:].indirect(T.one_o[:]), float(MID), None, A.add))
            after("g", at["d3"])
            send(peer(r), T["e3l%d" % r][:], T["d3_o%d" % r][:, 0:20], "t%d" % r)
        return chain(first, second)

    def inverse(r):
        landed("v", r, "e")
        at["inv"] = v(V.tensor_copy(T.einv[:].indirect(T["el%d" % r][:]), T.iot[:]))

    def turn_places():
        def join():
            need("v", "ta")
            need("v", "tb")
            return v(V.tensor_tensor(T.prow[:, 16:336], T.tbt[:].indirect(T.n_o[:]), T.tat[:], A.add))

        def far():
            after("v", at["lists"])
            at["qb"] = v(V.tensor_tensor(T.qb[:, 8:168], T.tp[:].indirect(T.far_o[:]), T.wtb[:], A.add))

        def own():
            at["qa"] = v(V.tensor_tensor(T.qa[:, 8:216], T.tp[:].indirect(T.own_o[:, 0:13]), T.wt[:, 0:208], A.add))

        def far_steps():
            after("v", at["qb"])
            at["db"] = v(V.tensor_tensor(T.db[:], T.qb[:, 7:167], T.qb[:, 8:168], A.subtract))

        def own_steps():
            after("v", at["qa"])
            at["da"] = v(V.tensor_tensor(T.da[:], T.qa[:, 7:167], T.qa[:, 8:168], A.subtract))

        def mates():
            v(V.tensor_tensor(T.dif[:], T.qa[:, 169:208:2], T.qa[:, 168:208:2], A.subtract))
        return chain(join, lambda: turn(T.tp, T.prow), far, own, far_steps, own_steps, mates)

    def quantise(x, lo, hi, r):
        n = v(V.quantize_mx(T.qx[:, lo:hi], T.px[:, lo:hi], x[:, 4 * lo:4 * hi]))
        after("p", n)
        last = hi == C
        if r < 3:
            bank = ps[1 if last else 4][:, 0:hi - lo]
            t = p(P.matmul_mx(bank, T.qr[:], T.pr[:], T.qx[:, lo:hi], T.px[:, lo:hi], True, True))
            if last:
                at["t1"] = p(P.matmul_mx(ps[0][:, 0:hi - lo], T.qr[:], T.pr[:], T.qx[:, lo:hi], T.px[:, lo:hi], True, True))
            after("s", t, masks)
            if not last:
                s(S.activation(T.w0[:, lo:hi], bank, F.Identity, bias=bias[:, 2:3], scale=act[:, 2:3]))
            at["y1"] = s(S.activation(T.y1[:, lo:hi], bank, F.Identity, bias=bias[:, 1:2], scale=act[:, 1:2]))
            at["y2"] = s(S.activation(T.y2[:, lo:hi], bank, F.Identity, bias=bias[:, 0:1], scale=act[:, 0:1]))
            return
        bank = ps[0 if last else 4][:, 0:hi - lo]
        t = p(P.matmul_mx(bank, T.qv[:], T.pv[:], T.qx[:, lo:hi], T.px[:, lo:hi], True, True))
        after("y", n)
        done("out", Y.dma_start(T.oc[:, 4 * lo:4 * hi], T.qx[:, lo:hi].bitcast(dt.uint8)), 16)
        if last:
            after("s", n)
            for k in range(4):
                done("out", (S if k % 2 else Y).dma_start(T.osc[4 * k:4 * k + 4, :], T.px[32 * k:32 * k + 4, :]), 16)
            after("v", t)
            after("y", v(V.tensor_copy(T.w0[:, lo:hi], bank)))
            done("out", Y.dma_start(T.y[:, lo:hi], T.w0[:, lo:hi]), 16)
        else:
            after("s", t)
            after("s", s(S.activation(T.w0[:, lo:hi], bank, F.Copy)))
            done("out", S.dma_start(T.y[:, lo:hi], T.w0[:, lo:hi]), 16)

    after("s", vd)
    more(1)
    after("s", n2)
    after("p", s(S.activation(T.pr[:], T.pu[:].indirect(T.row_o[:]), F.Copy)))
    more(2)

    for r in range(3):
        x, xn = X[r], X[r + 1]
        d_o, f_o = T["f_o%d" % r], T["f_o%d" % (r + 1)]
        if r == 0:
            for lo, hi in HALVES:
                quantise(x, lo, hi, 0)
            need("v", "ldn", 16)
            v(V.tensor_copy(T.n_o[:], T.nli[:]))
            at["pt"] = v(V.memset(T.pt[:], HUGE))
            aside.extend(third_power(0))
        else:
            more(len(todo))
            halve(x)
            aside.extend(turn_places())
        lo, hi = HALVES[-1]
        after("v", at["t1"], masks)
        n = v(V.tensor_scalar(T.w0[:, lo:hi], ps[0][:, 0:hi - lo], floor, None, A.max))
        step(1 if r == 0 else 0)
        after("v", n, at["y1"])
        n = v(V.tensor_tensor(T.w1[:], T.w0[:].indirect(d_o[:]), T.y1[:], A.min))
        if r == 0:
            step()
            late_tables()
        after("v", n, at["y2"])
        n = [v(V.tensor_tensor(T.w2[:, lo:hi], T.w1[:].indirect(d_o[:, lo // 16:hi // 16]), T.y2[:, lo:hi], A.min)) for lo, hi in SPLIT]
        after("y", n[-1])
        for k in range(2):
            slot("shift", T.yo, k + 1, T.w2, k, 4)
        for h, (lo, hi) in enumerate(SPLIT):
            after("v", n[h])
            n[h] = v(V.transpose(T.ts[:, lo:hi], T.w2[:, lo:hi]))
        for h, (lo, hi) in enumerate(SPLIT):
            after("v", n[h])
            n[h] = v(V.tensor_copy(T["ss%d" % r][:, lo // 4:hi // 4], T.ts[:, lo + 3:hi:4]))
        after("g", n[-1])
        send(peer(r), T["sl%d" % r][:], T["ss%d" % r][:], "s%d" % r)

        def own_minima():
            need("v", "shift")
            at["oa"] = v(V.tensor_tensor(T.oa[:], T.w2[:].indirect(T["d3_o%d" % r][:, 0:20]), T.yo[:], A.min))

        if r == 0:
            g3 = last_tables()
            after("g", ones)
            g4 = [gc(g.affine_select(T.eb[:, 512 * b:512 * b + 512], T.ones[:], [[-1, 512]], A.is_equal, 0.0, b, 4)) for b in range(4)][-1]
            inverse(0)
            more(4)
            at["fills"] = fills()
            more(len(todo))
            calls = {"-": [lambda: None], "o": [own_minima], "c": late_constants(g3), "p": turn_places()}
            aside.extend([calls[k].pop(0) for k in ORDER0])
        else:
            aside.insert(2, own_minima)
        if r == 1:
            Y.dma_start(T.vt[:], T.v[:]).then_inc(T.sem.ldv, 16)
        step(W1[r])
        sl = T["sl%d" % r]
        landed("s", r, "s")
        landed("v", r, "s")
        after("s", at["pt"])
        n1 = v(V.tensor_copy(T.pt[:, 2:320:4], sl[:]))
        s(S.activation(T.pt[:, 3:320:8], sl[:, 1:80:2], F.Copy))
        n2 = s(S.activation(T.pt[:, 7:320:16], sl[:, 1:80:4], F.Copy))
        step()
        after("v", n1, n2)
        v(V.transpose(T.wp[:], T.pt[:, 0:320]))
        at["pt"] = v(V.transpose(T.yp[:], T.pt[:, 1:321]))
        if r == 0:
            halve(x)
        step()
        after("v", at["pt"])
        landed("v", r, "t")
        n = v(V.tensor_tensor(T.mb[:], T.wp[:].indirect(T["e3l%d" % r][:]), T.yp[:], A.min))
        step()
        after("v", n, at["oa"])
        flags = [v(V.tensor_tensor(T.irow[:, 16 + lo:16 + hi], T.mb[:].indirect(T.n_o[:, lo // 16:hi // 16]), T.oa[:, lo:hi], A.is_lt)) for lo, hi in SPLIT]
        after("s", flags[1])
        ni = s(S.activation(T.irow2[:, 16:336], T.irow[:, 16:336].indirect(T.n_o[:]), F.Copy))
        ends = [[None, None], [None, None]]

        def cursors(h):
            lo, hi = ((0, 64), (64, 160))[h]
            scans = []

            def turn_half(k):
                after("v", flags[h])
                return turn_part(T.tin, T.irow, h, k)

            def pick():
                after("v", at["lists"])
                return v(V.tensor_copy(T.fc[:, lo:hi], T.tin[:, 0:(288, 704)[h]].indirect(T.flag_o[:, lo // 16:hi // 16])))

            def scan():
                after("v", at["da"], at["db"])
                scans.extend([v(V.tensor_tensor_scan(out[:, lo:hi], d[:, lo:hi], T.fc[:, lo:hi], 0.0, A.add, A.mult)) for out, d in ((T.sb, T.db), (T.sa, T.da))])

            def end(k):
                after("v", scans[k])
                ends[h][k] = v(V.tensor_copy((T.b_o, T.a_o)[k][:, lo // 8:hi // 8], (T.sb, T.sa)[k][:, lo + 7:hi:8]))
            return [lambda: turn_half(0)] + chain(lambda: turn_half(1), pick, scan, lambda: end(0), lambda: end(1))

        def mate_flags(h):
            after("v", ni)
            at["mates"] = [turn_part(T.tin2, T.irow2, h, k) for k in range(2)][1]
        calls = {"a": cursors(0), "b": cursors(1), "-": [lambda: step(len(aside))], "m": [lambda: mate_flags(0), lambda: mate_flags(1)]}
        for call in ORDER1[r]:
            calls[call].pop(0)()

        def far_side(h):
            lo, hi = PARTS[h]
            after("s", ends[min(h, 1)][0])
            return [s(S.activation(T.zb[:, C * k + lo:C * k + hi], T.xh[:, C * k:C * k + C].indirect(T.b_o[:, lo // 16:hi // 16]), F.Copy)) for k in range(4)]

        def mean(h, k):
            lo, hi = PARTS[h]
            after("v", zb[h][k], ends[min(h, 1)][1])
            at["z%d" % h] = v(V.tensor_tensor(T.z[:, 4 * lo + k:4 * hi:4], T.xh[:, C * k:C * k + C].indirect(T.a_o[:, lo // 16:hi // 16]), T.zb[:, C * k + lo:C * k + hi], A.add))

        def products(h, banks):
            lo, hi = PARTS[h]
            qz, pz = T.qz[:, 128 * h:128 * h + 128], T.pz[:, 128 * h:128 * h + 128]
            after("v", at["z%d" % h])
            after("p", v(V.quantize_mx(qz, pz, T.z[:, 4 * hi - 512:4 * hi])))
            return [p(P.matmul_mx(banks[b][:, 0:128], T.qw[:, 128 * b:128 * b + 128], T.pw[:, 128 * b:128 * b + 128], qz, pz, True, True)) for b in range(4)]

        def layer(h, tz, banks, q, bs):
            lo, hi = SENT[h]
            for b in bs:
                after(q, tz[b])
                out, in_ = T.h[:, 4 * lo + b:4 * hi:4], banks[b][:, 0:hi - lo]
                n = s(S.activation(out, in_, F.Copy, scale=0.03125)) if q == "s" else v(V.tensor_scalar(out, in_, 0.03125, None, A.mult))
            return n

        def codes(h):
            lo, hi = SENT[h]
            qh, ph, end = T["qh%d" % r], T["ph%d" % r], 128 * h + 128
            after("g", v(V.quantize_mx(qh[:, end - 128:end], ph[:, end - 128:end], T.h[:, 4 * hi - 512:4 * hi])))
            send(peer(r), T["ql%d" % r][:, lo:hi].bitcast(dt.uint8), qh[:, end - (hi - lo):end].bitcast(dt.uint8), "c%d%d" % (h, r))
            send(peer(r), T["pl%d" % r][:, lo:hi], ph[:, end - (hi - lo):end], "p%d%d" % (h, r))

        def new_list():
            at["f"] = v(V.tensor_copy(f_o[:], T.new[:]))
            if r < 2:
                after("g", at["f"])
                send(peer(r + 1), T["el%d" % (r + 1)][:], f_o[:], "e%d" % (r + 1))

        aside.extend(chain(
            lambda: (after("v", at["mates"]), v(V.tensor_tensor(T.yc[:], T.tin2[:].indirect(T.flag_o[:]), T.fc[:], A.subtract)))[1],
            lambda: v(V.tensor_tensor_scan(T.sy[:], T.alt[:], T.yc[:], 0.0, A.mult, A.add)),
            lambda: v(V.tensor_tensor(T.odd[:], T.sy[:, 7:160:8], T.sy[:, 7:160:8], A.mult)),
            lambda: v(V.tensor_tensor(T.trade[:], T.odd[:], T.dif[:], A.mult)),
            lambda: v(V.tensor_tensor(T.new[:], T.trade[:], T.qa[:, 168:208:2], A.add)),
            new_list))
        place = chain(
            lambda: (after("v", at["lrow"]), turn(T.tin2, T.irow2))[1],
            lambda: at.update(l=v(V.tensor_scalar(T.l_o[:], T.tin2[:, 0:672].indirect(T.one_o[:]), float(MID), None, A.add))))
        after("s", at["xh"])
        zb = [far_side(h) for h in range(2)]
        if r == 0:
            need("p", "ldw", 32)
        planes = [list(range(4)) for h in range(3)]
        for call in ORDER[r]:
            if call == "e":
                step()
                if not aside:
                    todo[:] = [(r + 1, name) for name in ["l"] + (CHAIN if r < 2 else ["out"])]
            elif call in "abc":
                mean("abc".index(call), planes["abc".index(call)].pop(0))
            elif call == "A":
                tz0 = products(0, ps[0:4])
                ha = layer(0, tz0, ps[0:4], "s", range(4))
            elif call == "B":
                tz1 = products(1, ps[4:8])
            elif call == "s":
                hb = layer(1, tz1, ps[4:8], "s", [0, 1])
            elif call == "v":
                vb = layer(1, tz1, ps[4:8], "v", [2, 3])
            elif call == "0":
                after("v", ha)
                codes(0)
            elif call == "1":
                after("v", hb, vb)
                codes(1)
            elif call == "C":
                after("p", ha)
                tz2 = products(2, ps[0:4])
            elif call == "z":
                zb.append(far_side(2))
            else:
                more(1)
        if r == 0:
            after("v", g4)
            after("p", v(V.quantize_mx(T.qe[:], T.pe[:], T.eb[:])))
        place[0]()
        if r < 2:
            inverse(r + 1)
        else:
            need("v", "ldv", 16)
            v(V.quantize_mx(T.qv[:], T.pv[:], T.vt[:]))
        place[1]()
        for call in third_power(r + 1) if r < 2 else []:
            call()
        for b in range(4):
            after("s", tz2[b])
            near = s(S.activation(T.j[:, C * b + FAR:C * b + C], ps[b][:, 128 - (C - FAR):128], F.Copy, scale=0.03125))
        after("p", hb, vb)
        for h, banks in (0, ps[4:8]), (1, ps[0:4]):
            lo, hi = SENT[h]
            landed("p", r, "c%d" % h)
            landed("p", r, "p%d" % h)
            td = [p(P.matmul_mx(banks[b][:, 0:128], T.qe[:, 128 * b:128 * b + 128], T.pe[:, 128 * b:128 * b + 128], T["ql%d" % r][:, hi - 128:hi], T["pl%d" % r][:, hi - 128:hi], True, True)) for b in range(4)]
            ja = []
            for b in range(4):
                q = "v" if h == 1 and b < 2 else "s"
                out, in_ = T.j[:, C * b + lo:C * b + hi], banks[b][:, 128 - (hi - lo):128]
                after(q, td[b])
                ja.append(v(V.tensor_copy(out, in_)) if q == "v" else s(S.activation(out, in_, F.Copy)))
            if h == 0:
                first = ja[3]
                after("p", near)
                more(1)
        after("v", at["l"], first)
        after("p", ja[1], ja[3])
        lo, hi = HALVES[1]
        picked = {}
        for b in HELP:
            after("s", ja[b], ja[3], at["l"])
            picked[b] = s(S.activation(T.jp[:, 128 * b:128 * b + 128], T.j[:, C * b:C * b + C].indirect(T.l_o[:, lo // 16:hi // 16]), F.Copy))
        more(2)

        def add(h, b):
            lo, hi = HALVES[h]
            after("v", ja[b])
            if h and b in picked:
                after("v", picked[b])
                return v(V.tensor_tensor(xn[:, 4 * lo + b:4 * hi:4], T.jp[:, 128 * b:128 * b + 128], x[:, 4 * lo + b:4 * hi:4], A.add))
            return v(V.tensor_tensor(xn[:, 4 * lo + b:4 * hi:4], T.j[:, C * b:C * b + C].indirect(T.l_o[:, lo // 16:hi // 16]), x[:, 4 * lo + b:4 * hi:4], A.add))
        n = [add(0, b) for b in range(4)][3]
        add(1, 0)
        after("v", n)
        quantise(xn, *HALVES[0], r + 1)
        after("v", [add(1, b) for b in range(1, 4)][2])
        quantise(xn, *HALVES[1], r + 1)

    for k in COUNTED:
        need("g", k)
